import numpy as np
import ml_dtypes


def mxq(x, axis, fmt="e4m3"):
    dtype, down = {"e4m3": (ml_dtypes.float8_e4m3fn, 7), "e5m2": (ml_dtypes.float8_e5m2, 14)}[fmt]
    v = np.moveaxis(np.asarray(x, np.float32).astype(ml_dtypes.bfloat16).astype(np.float64), axis, -1)
    blocks = v.reshape(v.shape[:-1] + (-1, 32))
    amax = np.abs(blocks).max(-1, keepdims=True)
    byte = np.maximum(np.where(amax > 0, np.frexp(amax)[1] - 1 + 127, 0) - down, 1)
    scale = np.exp2(byte - 127.0)
    codes = (blocks / scale).astype(np.float32).astype(dtype).astype(np.float64)
    return np.moveaxis((codes * scale).reshape(v.shape), -1, axis)


WIDE = False


def mx_kscale(k):
    if not WIDE:
        return np.ones(k)
    levels = np.array([24, -24, 12, -12, 0])
    if k % 512:
        return np.exp2(np.random.permutation(np.resize(levels, k // 32))).repeat(32)
    a = np.empty((k // 512, 16))
    for p in range(k // 512):
        a[p, :8] = np.random.permutation(np.resize(levels, 8))
        for g in range(8):
            far = levels[np.abs(levels - a[p, g]) >= 10]
            a[p, g + 8] = far[np.random.randint(len(far))]
    return np.exp2(a.ravel()).repeat(32)


def f64(x):
    return np.asarray(x).astype(np.float64)


def striped8(idx):
    return np.concatenate([v.reshape(-1, 16).T for v in idx]).astype(np.uint16)


def unstriped8(offs):
    return np.stack([offs[16 * g:16 * g + 16].T.reshape(-1) for g in range(8)]).astype(np.int64)


E2M1 = np.array([0.0, 0.5, 1.0, 1.5, 2.0, 3.0, 4.0, 6.0, -0.0, -0.5, -1.0, -1.5, -2.0, -3.0, -4.0, -6.0])


def pack_weight(w, fmt):
    k, n = w.shape
    w = f64(np.asarray(w, np.float32).astype(ml_dtypes.bfloat16)).reshape(k // 32, 32, n)
    amax = np.abs(w).max(1)
    if fmt == "e4m3":
        byte = np.frexp(amax)[1] - 1 + 127 - 7
    else:
        mant, ex = np.frexp(amax / 6.0)
        byte = np.where(mant > 0.5, ex, ex - 1) + 127
    byte = np.clip(np.where(amax > 0, byte, 1), 1, 254)
    scaled = (w * np.exp2(127.0 - byte)[:, None, :]).reshape(k, n).astype(np.float32)
    by_word = np.ascontiguousarray(scaled.reshape(k // 512, 128, 4, n).transpose(0, 1, 3, 2))
    if fmt == "e4m3":
        words = by_word.astype(ml_dtypes.float8_e4m3fn).view(np.uint8)
    else:
        c = by_word.astype(ml_dtypes.float4_e2m1fn).view(np.uint8) & 0xF
        words = (c[..., 0::2] | (c[..., 1::2] << 4)).reshape(k // 512, 128, 2 * n)
    return np.ascontiguousarray(words), np.ascontiguousarray(byte.astype(np.uint8).reshape(k // 512, 16, n))


def unpack_weight(words, scales, fmt):
    g, _, n = scales.shape
    words = np.ascontiguousarray(words).reshape(g, 128, n, -1)
    if fmt == "e4m3":
        vals = words.view(ml_dtypes.float8_e4m3fn).astype(np.float64)
    else:
        nib = np.empty((g, 128, n, 4), np.uint8)
        nib[..., 0::2] = words & 0xF
        nib[..., 1::2] = words >> 4
        vals = E2M1[nib]
    vals = vals * np.repeat(np.exp2(scales.astype(np.float64) - 127.0), 8, axis=1)[..., None]
    return vals.transpose(0, 1, 3, 2).reshape(g * 512, n)


K, R, N, T, J = 1024, 512, 512, 2048, 1024


def setup_inputs():
    n = np.random.standard_normal
    s = mx_kscale(K)[:, None]
    u = mx_kscale(R)[:, None]
    p_wu = pack_weight(n((K, R)) / np.sqrt(K) / s * u.T, "e2m1")
    p_wd = pack_weight(n((R, N)) / np.sqrt(R) / u, "e4m3")
    return {
        "xT": (n((K, T)) * s).astype(np.float32),
        "wgt": np.repeat(np.random.uniform(0.5, 2.0, (8, J)), 16, axis=0).astype(np.float32),
        "wg": (n((K, R)) / np.sqrt(K) / s).astype(np.float32),
        "wu_words": p_wu[0],
        "wu_scales": p_wu[1],
        "wd_words": p_wd[0],
        "wd_scales": p_wd[1],
        "offs": striped8(np.stack([np.random.permutation(T)[:J] for _ in range(8)])),
    }


def reference(xT, wgt, wg, wu_words, wu_scales, wd_words, wd_scales, offs):
    idx = unstriped8(offs)
    rows = np.arange(K)
    xg = f64(wgt)[rows // 4 % 128] * f64(xT)[rows[:, None], idx[rows % 512 // 64]]
    xT_ = mxq(xg, 0, "e4m3")
    wg_ = mxq(f64(wg), 0, "e4m3")
    wu_ = unpack_weight(wu_words, wu_scales, "e2m1")
    ga = wg_.T @ xT_
    ub = wu_.T @ xT_
    h = np.tanh(ga) * ub
    h_ = mxq(h, 0, "e4m3")
    wd_ = unpack_weight(wd_words, wd_scales, "e4m3")
    y = wd_.T @ h_
    return y

@@ -1,0 +1,376 @@
+from contextlib import ExitStack
+
+import concourse.mybir as mybir
+
+K, R, N, T, J = 1024, 512, 512, 2048, 1024
+FLOPS = 2 * K * R * J * 2 + 2 * R * N * J
+
+F32 = mybir.dt.float32
+BF16 = mybir.dt.bfloat16
+I32 = mybir.dt.int32
+U32 = mybir.dt.uint32
+U16 = mybir.dt.uint16
+U8 = mybir.dt.uint8
+FP8X4 = mybir.dt.float8_e4m3fn_x4
+FP4X4 = mybir.dt.float4_e2m1fn_x4
+MULT = mybir.AluOpType.mult
+TANH = mybir.ActivationFunctionType.Tanh
+
+P = 128
+PACK = 4
+PASSES = K // (P * PACK)
+CH = 128
+CHUNKS = J // CH
+
+
+def tile_list_tanh_none_kernel(
+    tc, xT, wgt, wg, wu_words, wu_scales, wd_words, wd_scales, offs, out
+):
+    nc = tc.nc
+    with ExitStack() as ctx:
+        keep = ctx.enter_context(tc.tile_pool(name="keep", bufs=1))
+        ring = ctx.enter_context(tc.tile_pool(name="ring", bufs=3))
+        psum = ctx.enter_context(tc.psum_pool(name="psum", bufs=1))
+
+        offsets = keep.tile([P, J // 16], U16, name="offsets")
+        wgt_sb = keep.tile([P, J], F32, name="wgt_sb")
+        planes = [[keep.tile([P, T], F32, name="plane_%d_%d" % (a, i)) for i in range(PACK)] for a in range(PASSES)]
+        picked = [keep.tile([P, PACK, J], F32, name="picked_%d" % a) for a in range(PASSES)]
+        x_bf = [keep.tile([P, J, PACK], BF16, name="x_bf_%d" % a, align_bytes=64) for a in range(PASSES)]
+        x_codes = [keep.tile([P, J], U32, name="x_codes_%d" % a, align_bytes=64) for a in range(PASSES)]
+        x_scales = [keep.tile([P, J], U8, name="x_scales_%d" % a, align_bytes=64) for a in range(PASSES)]
+        wg_raw = [keep.tile([P, PACK, R], F32, name="wg_raw_%d" % a) for a in range(PASSES)]
+        wg_bf = [keep.tile([P, R, PACK], BF16, name="wg_bf_%d" % a, align_bytes=64) for a in range(PASSES)]
+        wg_codes = [keep.tile([P, R], U32, name="wg_codes_%d" % a, align_bytes=64) for a in range(PASSES)]
+        wg_scales = [keep.tile([P, R], U8, name="wg_scales_%d" % a, align_bytes=64) for a in range(PASSES)]
+        wu_raw = keep.tile([P, PASSES, 2 * R], U8, name="wu_raw", align_bytes=64)
+        wu_codes = keep.tile([P, PASSES, 2 * R], U8, name="wu_codes", align_bytes=64)
+        wu_sc_raw = keep.tile([P, PASSES, R], U8, name="wu_sc_raw", align_bytes=64)
+        wu_sc = keep.tile([P, PASSES, R], U8, name="wu_sc", align_bytes=64)
+        wd_codes = keep.tile([P, N], I32, name="wd_codes", align_bytes=64)
+        wd_sc = keep.tile([P, N], U8, name="wd_sc", align_bytes=64)
+        h_codes = keep.tile([P, J], U32, name="h_codes", align_bytes=64)
+        h_scales = keep.tile([P, J], U8, name="h_scales", align_bytes=64)
+        y_sb = keep.tile([P, N // P, J], F32, name="y_sb")
+        warm = keep.tile([P, 1], F32, name="warm")
+
+        x_rows = xT.rearrange("(a p i) t -> a p i t", p=P, i=PACK)
+        wg_rows = wg.rearrange("(a p i) r -> a p i r", p=P, i=PACK)
+        out_rows = out.rearrange("(q p) j -> p q j", p=P)
+
+        def load_plane(a, i):
+            nc.sync.dma_start(out=planes[a][i][:], in_=x_rows[a, :, i, :])
+
+        def load_wg(a, r0, r1):
+            nc.sync.dma_start(out=wg_raw[a][:, :, r0:r1], in_=wg_rows[a, :, :, r0:r1])
+
+        def load_wgt(j0, j1):
+            nc.sync.dma_start(out=wgt_sb[:, j0:j1], in_=wgt[:, j0:j1])
+
+        def load_wu():
+            nc.sync.dma_start(out=wu_raw[:].bitcast(I32), in_=wu_words.rearrange("a p b -> p a b").bitcast(I32))
+
+        def load_wd():
+            nc.sync.dma_start(out=wd_codes[:], in_=wd_words[0].rearrange("p n i -> p (n i)").bitcast(I32))
+
+        def copy_on(engine, dst, src):
+            if engine == "S":
+                nc.scalar.copy(out=dst, in_=src)
+            else:
+                nc.vector.tensor_copy(out=dst, in_=src)
+
+        def gather(a, i, j0, j1):
+            nc.vector.tensor_tensor(
+                out=picked[a][:, i, j0:j1],
+                in0=planes[a][i][:].indirect(offsets[:, j0 // 16 : j1 // 16]),
+                in1=wgt_sb[:, j0:j1],
+                op=MULT,
+            )
+
+        def interleave_x(engine, a, j0, j1):
+            copy_on(
+                engine,
+                x_bf[a][:, j0:j1, :].rearrange("p (c e) i -> p c i e", e=4),
+                picked[a][:, :, j0:j1].rearrange("p i (c e) -> p c i e", e=4),
+            )
+
+        def quantize_x(a, j0, j1):
+            nc.vector.quantize_mx(
+                out=x_codes[a][:, j0:j1].bitcast(FP8X4),
+                scales=x_scales[a][:, j0:j1],
+                in_=x_bf[a][:, j0:j1, :].rearrange("p j i -> p (j i)"),
+            )
+
+        def interleave_wg(engine, a, r0, r1):
+            copy_on(
+                engine,
+                wg_bf[a][:].rearrange("p (t m) i -> p m i t", t=PACK)[:, r0 // PACK : r1 // PACK, :, :],
+                wg_raw[a][:, :, r0:r1].rearrange("p i (m t) -> p m i t", t=PACK),
+            )
+
+        def quantize_wg(a, c0, c1):
+            nc.vector.quantize_mx(
+                out=wg_codes[a][:, c0:c1].bitcast(FP8X4),
+                scales=wg_scales[a][:, c0:c1],
+                in_=wg_bf[a][:, c0:c1, :].rearrange("p c i -> p (c i)"),
+            )
+
+        def first_product(c, tag, bufs, weights):
+            acc = psum.tile([P, PACK, CH], F32, name=tag, tag=tag, bufs=bufs)
+            js = slice(c * CH, (c + 1) * CH)
+            for t in range(PACK):
+                for a in range(PASSES):
+                    codes, scales = weights(a, t)
+                    nc.tensor.matmul_mx(
+                        out=acc[:, t, :],
+                        lhsT=codes,
+                        lhsT_scale=scales,
+                        rhs=x_codes[a][:, js].bitcast(FP8X4),
+                        rhs_scale=x_scales[a][:, js],
+                        start=(a == 0),
+                        stop=(a == PASSES - 1),
+                    )
+            return acc
+
+        def wu_tile(a, t):
+            return wu_codes[:, a, 2 * P * t : 2 * P * (t + 1)].bitcast(FP4X4), wu_sc[:, a, P * t : P * (t + 1)]
+
+        def wg_tile(a, t):
+            return wg_codes[a][:, P * t : P * (t + 1)].bitcast(FP8X4), wg_scales[a][:, P * t : P * (t + 1)]
+
+        def gate(ga):
+            th = ring.tile([P, CH, PACK], F32, name="th", tag="th")
+            nc.scalar.activation(out=th[:], in_=ga[:].rearrange("p t j -> p j t"), func=TANH)
+            return th
+
+        def hidden(ub, th):
+            h_bf = ring.tile([P, CH, PACK], BF16, name="h_bf", tag="h_bf", align_bytes=64)
+            nc.vector.tensor_tensor(out=h_bf[:], in0=ub[:].rearrange("p t j -> p j t"), in1=th[:], op=MULT)
+            return h_bf
+
+        def quantize_h(c, h_bf):
+            js = slice(c * CH, (c + 1) * CH)
+            nc.vector.quantize_mx(
+                out=h_codes[:, js].bitcast(FP8X4), scales=h_scales[:, js], in_=h_bf[:].rearrange("p j t -> p (j t)")
+            )
+
+        def second_product(c, engine):
+            js = slice(c * CH, (c + 1) * CH)
+            y = psum.tile([P, N // P, CH], F32, name="y", tag="y", bufs=2)
+            for q in range(N // P):
+                nc.tensor.matmul_mx(
+                    out=y[:, q, :],
+                    lhsT=wd_codes[:, P * q : P * (q + 1)].bitcast(FP8X4),
+                    lhsT_scale=wd_sc[:, P * q : P * (q + 1)],
+                    rhs=h_codes[:, js].bitcast(FP8X4),
+                    rhs_scale=h_scales[:, js],
+                    start=True,
+                    stop=True,
+                )
+            copy_on(engine, y_sb[:, :, js], y[:])
+
+        def store(j0, j1):
+            nc.sync.dma_start(out=out_rows[:, :, j0:j1], in_=y_sb[:, :, j0:j1])
+
+        th_all = keep.tile([P, PACK, J], F32, name="th_all")
+        ga_banks = {}
+
+        def clear_scales():
+            nc.gpsimd.memset(wu_sc_raw[:].rearrange("p a r -> p (a r)").bitcast(I32), 0)
+            nc.gpsimd.memset(wd_sc[:].bitcast(I32), 0)
+
+        def load_offsets():
+            nc.sync.dma_start(offsets[:], offs)
+
+        def warm_up():
+            nc.scalar.activation(out=warm[:], in_=wgt_sb[:, 0:1], func=TANH)
+
+        def load_wu_scales(queue):
+            for q in range(4):
+                nc.sync.dma_start(
+                    out=wu_sc_raw[32 * q : 32 * q + 4, :, :].bitcast(I32),
+                    in_=wu_scales[:, 4 * q : 4 * q + 4, :].rearrange("a s r -> s a r").bitcast(I32),
+                )
+
+        def load_wd_scales(queue):
+            for q in range(4):
+                nc.sync.dma_start(
+                    out=wd_sc[32 * q : 32 * q + 4, :].bitcast(I32),
+                    in_=wd_scales[0, 4 * q : 4 * q + 4, :].bitcast(I32),
+                )
+
+        def permute_wu(a):
+            nc.vector.tensor_copy(
+                out=wu_codes[:, a, :].bitcast(U16).rearrange("p (t m) -> p m t", t=PACK),
+                in_=wu_raw[:, a, :].bitcast(U16).rearrange("p (m t) -> p m t", t=PACK),
+            )
+
+        def permute_wu_scales():
+            nc.vector.tensor_copy(
+                out=wu_sc[:].rearrange("p a (t m) -> p a m t", t=PACK),
+                in_=wu_sc_raw[:].rearrange("p a (m t) -> p a m t", t=PACK),
+            )
+
+        def ga_pass(h, a, t):
+            if a == 0:
+                ga_banks[t] = psum.tile([P, 512], F32, name="ga%d" % t, tag="ga%d" % t, bufs=1)
+            js = slice(512 * h, 512 * (h + 1))
+            codes, scales = wg_tile(a, t)
+            nc.tensor.matmul_mx(
+                out=ga_banks[t][:],
+                lhsT=codes,
+                lhsT_scale=scales,
+                rhs=x_codes[a][:, js].bitcast(FP8X4),
+                rhs_scale=x_scales[a][:, js],
+                start=(a == 0),
+                stop=(a == PASSES - 1),
+            )
+
+        def tanh(t, j0, j1):
+            nc.scalar.activation(out=th_all[:, t, j0:j1], in_=ga_banks[t][:, j0 % 512 : j0 % 512 + j1 - j0], func=TANH)
+
+        def hidden2(c, acc):
+            h_tile = ring.tile([P, CH, PACK], BF16, name="h_tile", tag="h_tile", align_bytes=64)
+            nc.vector.tensor_tensor(
+                out=h_tile[:].rearrange("p (g e) t -> p g t e", e=4),
+                in0=acc[:].rearrange("p t (g e) -> p g t e", e=4),
+                in1=th_all[:, :, c * CH : (c + 1) * CH].rearrange("p t (g e) -> p g t e", e=4),
+                op=MULT,
+            )
+            return h_tile
+
+        def second2(c, engine, tag, bufs):
+            js = slice(c * CH, (c + 1) * CH)
+            y = psum.tile([P, N // P, CH], F32, name="y", tag=tag, bufs=bufs)
+            for q in range(N // P):
+                nc.tensor.matmul_mx(
+                    out=y[:, q, :],
+                    lhsT=wd_codes[:, P * q : P * (q + 1)].bitcast(FP8X4),
+                    lhsT_scale=wd_sc[:, P * q : P * (q + 1)],
+                    rhs=h_codes[:, js].bitcast(FP8X4),
+                    rhs_scale=h_scales[:, js],
+                    start=True,
+                    stop=True,
+                )
+            copy_on(engine, y_sb[:, :, js], y[:])
+
+        ub = {}
+        h_bf = {}
+        ga = {}
+        th = {}
+        clear_scales()
+        load_offsets()
+        load_wu()
+        load_wgt(0, 512)
+        load_wu_scales("s")
+        load_plane(0, 0)
+        load_wgt(512, 1024)
+        load_plane(0, 1)
+        load_plane(0, 2)
+        load_plane(0, 3)
+        load_plane(1, 0)
+        load_wg(0, 0, R)
+        load_plane(1, 1)
+        load_plane(1, 2)
+        load_plane(1, 3)
+        load_wg(1, 0, 256)
+        load_wg(1, 256, 512)
+        load_wd()
+        load_wd_scales("s")
+        warm_up()
+        permute_wu(0)
+        permute_wu(1)
+        permute_wu_scales()
+        gather(0, 0, 0, 512)
+        gather(0, 0, 512, 1024)
+        gather(0, 1, 0, 512)
+        gather(0, 1, 512, 1024)
+        gather(0, 2, 0, 512)
+        gather(0, 2, 512, 1024)
+        gather(0, 3, 0, 256)
+        interleave_x("S", 0, 0, 256)
+        gather(0, 3, 256, 512)
+        interleave_x("S", 0, 256, 512)
+        gather(0, 3, 512, 768)
+        interleave_x("S", 0, 512, 768)
+        gather(0, 3, 768, 1024)
+        interleave_x("S", 0, 768, 1024)
+        quantize_x(0, 0, 512)
+        gather(1, 1, 0, 512)
+        interleave_wg("S", 0, 0, R)
+        gather(1, 0, 512, 1024)
+        gather(1, 3, 0, 256)
+        gather(1, 3, 256, 512)
+        gather(1, 2, 0, 512)
+        gather(1, 0, 0, 512)
+        interleave_x("S", 1, 0, 256)
+        quantize_x(1, 0, 256)
+        quantize_wg(0, 0, R)
+        interleave_wg("S", 1, 0, 256)
+        interleave_wg("V", 1, 256, 512)
+        quantize_wg(1, 256, 512)
+        interleave_x("S", 1, 256, 512)
+        gather(1, 2, 512, 1024)
+        quantize_wg(1, 0, 256)
+        ga[0] = first_product(0, "ga", 2, wg_tile)
+        quantize_x(1, 256, 512)
+        ub[0] = first_product(0, "ub", 4, wu_tile)
+        ub[1] = first_product(1, "ub", 4, wu_tile)
+        ub[2] = first_product(2, "ub", 4, wu_tile)
+        ub[3] = first_product(3, "ub", 4, wu_tile)
+        gather(1, 1, 512, 1024)
+        ga[1] = first_product(1, "ga", 2, wg_tile)
+        th[0] = gate(ga[0])
+        th[1] = gate(ga[1])
+        ga[2] = first_product(2, "ga", 2, wg_tile)
+        ga[3] = first_product(3, "ga", 2, wg_tile)
+        h_bf[0] = hidden(ub[0], th[0])
+        h_bf[1] = hidden(ub[1], th[1])
+        th[2] = gate(ga[2])
+        th[3] = gate(ga[3])
+        gather(1, 3, 512, 768)
+        interleave_x("S", 1, 512, 768)
+        quantize_h(0, h_bf[0])
+        second2(0, "S", "y", 2)
+        quantize_h(1, h_bf[1])
+        h_bf[2] = hidden(ub[2], th[2])
+        gather(1, 3, 768, 1024)
+        interleave_x("S", 1, 768, 1024)
+        second2(1, "S", "y", 2)
+        quantize_x(1, 512, 768)
+        store(0, 256)
+        h_bf[3] = hidden(ub[3], th[3])
+        quantize_x(0, 512, 1024)
+        ga[4] = first_product(4, "ga", 2, wg_tile)
+        th[4] = gate(ga[4])
+        ub[4] = first_product(4, "ub", 4, wu_tile)
+        quantize_h(2, h_bf[2])
+        ga[5] = first_product(5, "ga", 2, wg_tile)
+        th[5] = gate(ga[5])
+        quantize_x(1, 768, 1024)
+        ub[5] = first_product(5, "ub", 4, wu_tile)
+        ga[6] = first_product(6, "ga", 2, wg_tile)
+        second2(2, "S", "y", 2)
+        th[6] = gate(ga[6])
+        h_bf[4] = hidden(ub[4], th[4])
+        quantize_h(3, h_bf[3])
+        second2(3, "S", "y", 2)
+        ga[7] = first_product(7, "ga", 2, wg_tile)
+        h_bf[5] = hidden(ub[5], th[5])
+        th[7] = gate(ga[7])
+        quantize_h(4, h_bf[4])
+        second2(4, "S", "y", 2)
+        store(256, 512)
+        ub[6] = first_product(6, "ub", 4, wu_tile)
+        h_bf[6] = hidden(ub[6], th[6])
+        quantize_h(5, h_bf[5])
+        ub[7] = first_product(7, "ub", 4, wu_tile)
+        h_bf[7] = hidden(ub[7], th[7])
+        quantize_h(6, h_bf[6])
+        quantize_h(7, h_bf[7])
+        second2(5, "S", "y", 2)
+        second2(6, "S", "y", 2)
+        store(512, 768)
+        store(768, 896)
+        second2(7, "S", "y", 2)
+        store(896, 1024)

@@ -29,7 +29,7 @@ def tile_list_tanh_none_kernel(
     nc = tc.nc
     with ExitStack() as ctx:
         keep = ctx.enter_context(tc.tile_pool(name="keep", bufs=1))
-        ring = ctx.enter_context(tc.tile_pool(name="ring", bufs=3))
+        ring = ctx.enter_context(tc.tile_pool(name="ring", bufs=8))
         psum = ctx.enter_context(tc.psum_pool(name="psum", bufs=1))
 
         offsets = keep.tile([P, J // 16], U16, name="offsets")
@@ -254,6 +254,66 @@ def tile_list_tanh_none_kernel(
                 )
             copy_on(engine, y_sb[:, :, js], y[:])
 
+        wgt_late = keep.tile([P, J], F32, name="wgt_late")
+
+        def load_wgt2(j0, j1):
+            nc.sync.dma_start(out=wgt_late[:, j0:j1], in_=wgt[:, j0:j1])
+
+        def gather2(a, i, j0, j1):
+            nc.vector.tensor_tensor(
+                out=picked[a][:, i, j0:j1],
+                in0=planes[a][i][:].indirect(offsets[:, j0 // 16 : j1 // 16]),
+                in1=wgt_late[:, j0:j1],
+                op=MULT,
+            )
+
+        def ga256(g, u, bufs):
+            acc = psum.tile([P, 2, 256], F32, name="g2", tag="g2", bufs=bufs)
+            js = slice(256 * g, 256 * (g + 1))
+            for v in range(2):
+                for a in range(PASSES):
+                    codes, scales = wg_tile(a, 2 * u + v)
+                    nc.tensor.matmul_mx(
+                        out=acc[:, v, :],
+                        lhsT=codes,
+                        lhsT_scale=scales,
+                        rhs=x_codes[a][:, js].bitcast(FP8X4),
+                        rhs_scale=x_scales[a][:, js],
+                        start=(a == 0),
+                        stop=(a == PASSES - 1),
+                    )
+            return acc
+
+        def tanh256(g, u, acc):
+            nc.scalar.activation(out=th_all[:, 2 * u : 2 * u + 2, 256 * g : 256 * (g + 1)], in_=acc[:], func=TANH)
+
+        def second_half(c, u, engine, tag, bufs):
+            js = slice(c * CH, (c + 1) * CH)
+            y = psum.tile([P, 2, CH], F32, name="y", tag=tag, bufs=bufs)
+            for v in range(2):
+                q = 2 * u + v
+                nc.tensor.matmul_mx(
+                    out=y[:, v, :],
+                    lhsT=wd_codes[:, P * q : P * (q + 1)].bitcast(FP8X4),
+                    lhsT_scale=wd_sc[:, P * q : P * (q + 1)],
+                    rhs=h_codes[:, js].bitcast(FP8X4),
+                    rhs_scale=h_scales[:, js],
+                    start=True,
+                    stop=True,
+                )
+            copy_on(engine, y_sb[:, 2 * u : 2 * u + 2, js], y[:])
+
+        def store_half(c, u):
+            js = slice(c * CH, (c + 1) * CH)
+            nc.sync.dma_start(out=out_rows[:, 2 * u : 2 * u + 2, js], in_=y_sb[:, 2 * u : 2 * u + 2, js])
+
+        def interleave_pair(engine, a, u, j0, j1):
+            copy_on(
+                engine,
+                x_bf[a][:, j0:j1, 2 * u : 2 * u + 2],
+                picked[a][:, 2 * u : 2 * u + 2, j0:j1].rearrange("p i j -> p j i"),
+            )
+
         ub = {}
         h_bf = {}
         ga = {}
@@ -275,6 +335,7 @@ def tile_list_tanh_none_kernel(
         load_plane(1, 3)
         load_wg(1, 0, 256)
         load_wg(1, 256, 512)
+        load_wgt2(512, 1024)
         load_wd()
         load_wd_scales("s")
         warm_up()
@@ -288,89 +349,93 @@ def tile_list_tanh_none_kernel(
         gather(0, 2, 0, 512)
         gather(0, 2, 512, 1024)
         gather(0, 3, 0, 256)
-        interleave_x("S", 0, 0, 256)
         gather(0, 3, 256, 512)
-        interleave_x("S", 0, 256, 512)
-        gather(0, 3, 512, 768)
-        interleave_x("S", 0, 512, 768)
         gather(0, 3, 768, 1024)
-        interleave_x("S", 0, 768, 1024)
-        quantize_x(0, 0, 512)
+        gather(0, 3, 512, 768)
+        gather(1, 1, 512, 1024)
+        gather(1, 0, 512, 1024)
+        gather(1, 2, 0, 256)
+        interleave_x("S", 0, 0, 256)
+        interleave_x("S", 0, 256, 512)
         gather(1, 1, 0, 512)
         interleave_wg("S", 0, 0, R)
-        gather(1, 0, 512, 1024)
-        gather(1, 3, 0, 256)
-        gather(1, 3, 256, 512)
-        gather(1, 2, 0, 512)
-        gather(1, 0, 0, 512)
-        interleave_x("S", 1, 0, 256)
-        quantize_x(1, 0, 256)
         quantize_wg(0, 0, R)
-        interleave_wg("S", 1, 0, 256)
-        interleave_wg("V", 1, 256, 512)
-        quantize_wg(1, 256, 512)
-        interleave_x("S", 1, 256, 512)
-        gather(1, 2, 512, 1024)
-        quantize_wg(1, 0, 256)
-        ga[0] = first_product(0, "ga", 2, wg_tile)
-        quantize_x(1, 256, 512)
-        ub[0] = first_product(0, "ub", 4, wu_tile)
-        ub[1] = first_product(1, "ub", 4, wu_tile)
-        ub[2] = first_product(2, "ub", 4, wu_tile)
-        ub[3] = first_product(3, "ub", 4, wu_tile)
-        gather(1, 1, 512, 1024)
-        ga[1] = first_product(1, "ga", 2, wg_tile)
-        th[0] = gate(ga[0])
-        th[1] = gate(ga[1])
-        ga[2] = first_product(2, "ga", 2, wg_tile)
-        ga[3] = first_product(3, "ga", 2, wg_tile)
-        h_bf[0] = hidden(ub[0], th[0])
-        h_bf[1] = hidden(ub[1], th[1])
-        th[2] = gate(ga[2])
-        th[3] = gate(ga[3])
-        gather(1, 3, 512, 768)
-        interleave_x("S", 1, 512, 768)
-        quantize_h(0, h_bf[0])
-        second2(0, "S", "y", 2)
-        quantize_h(1, h_bf[1])
-        h_bf[2] = hidden(ub[2], th[2])
-        gather(1, 3, 768, 1024)
-        interleave_x("S", 1, 768, 1024)
-        second2(1, "S", "y", 2)
-        quantize_x(1, 512, 768)
-        store(0, 256)
-        h_bf[3] = hidden(ub[3], th[3])
+        gather(1, 3, 0, 256)
+        interleave_x("S", 0, 512, 768)
+        interleave_x("V", 0, 768, 1024)
+        gather(1, 0, 0, 512)
         quantize_x(0, 512, 1024)
-        ga[4] = first_product(4, "ga", 2, wg_tile)
-        th[4] = gate(ga[4])
-        ub[4] = first_product(4, "ub", 4, wu_tile)
-        quantize_h(2, h_bf[2])
-        ga[5] = first_product(5, "ga", 2, wg_tile)
-        th[5] = gate(ga[5])
+        interleave_x("V", 1, 0, 256)
+        interleave_wg("S", 1, 256, 512)
+        quantize_x(0, 0, 512)
+        quantize_x(1, 0, 256)
+        gather(1, 3, 256, 512)
+        interleave_wg("S", 1, 0, 256)
+        ub[0] = first_product(0, "ub", 3, wu_tile)
+        ub[1] = first_product(1, "ub", 3, wu_tile)
+        gather(1, 2, 256, 512)
+        interleave_x("V", 1, 256, 512)
+        quantize_x(1, 256, 512)
+        gather2(1, 2, 512, 768)
+        gather2(1, 3, 512, 768)
+        interleave_x("S", 1, 512, 768)
+        quantize_x(1, 512, 768)
+        ub[2] = first_product(2, "ub", 3, wu_tile)
+        quantize_wg(1, 0, 256)
+        quantize_wg(1, 256, 512)
+        ga[0] = ga256(0, 0, 3)
+        tanh256(0, 0, ga[0])
+        ga[1] = ga256(0, 1, 3)
+        ga[2] = ga256(1, 0, 3)
+        gather2(1, 2, 768, 1024)
+        tanh256(0, 1, ga[1])
+        h_bf[0] = hidden2(0, ub[0])
+        h_bf[1] = hidden2(1, ub[1])
+        gather2(1, 3, 768, 1024)
+        interleave_x("V", 1, 768, 1024)
+        ga[3] = ga256(1, 1, 3)
+        ga[4] = ga256(2, 0, 3)
+        quantize_h(0, h_bf[0])
+        quantize_h(1, h_bf[1])
+        ub[3] = first_product(3, "ub", 3, wu_tile)
+        tanh256(1, 0, ga[2])
+        tanh256(1, 1, ga[3])
+        h_bf[2] = hidden2(2, ub[2])
+        tanh256(2, 0, ga[4])
+        ga[5] = ga256(2, 1, 3)
         quantize_x(1, 768, 1024)
-        ub[5] = first_product(5, "ub", 4, wu_tile)
-        ga[6] = first_product(6, "ga", 2, wg_tile)
-        second2(2, "S", "y", 2)
-        th[6] = gate(ga[6])
-        h_bf[4] = hidden(ub[4], th[4])
+        h_bf[3] = hidden2(3, ub[3])
+        ga[6] = ga256(3, 0, 3)
+        quantize_h(2, h_bf[2])
+        second2(0, "V", "y", 2)
+        second2(1, "S", "y", 2)
+        store(0, 256)
         quantize_h(3, h_bf[3])
+        tanh256(2, 1, ga[5])
+        second2(2, "S", "y", 2)
         second2(3, "S", "y", 2)
-        ga[7] = first_product(7, "ga", 2, wg_tile)
-        h_bf[5] = hidden(ub[5], th[5])
-        th[7] = gate(ga[7])
+        ub[4] = first_product(4, "ub", 3, wu_tile)
+        ub[5] = first_product(5, "ub", 3, wu_tile)
+        tanh256(3, 0, ga[6])
+        h_bf[4] = hidden2(4, ub[4])
         quantize_h(4, h_bf[4])
-        second2(4, "S", "y", 2)
+        ga[7] = ga256(3, 1, 3)
         store(256, 512)
-        ub[6] = first_product(6, "ub", 4, wu_tile)
-        h_bf[6] = hidden(ub[6], th[6])
+        ub[6] = first_product(6, "ub", 3, wu_tile)
+        h_bf[5] = hidden2(5, ub[5])
         quantize_h(5, h_bf[5])
-        ub[7] = first_product(7, "ub", 4, wu_tile)
-        h_bf[7] = hidden(ub[7], th[7])
-        quantize_h(6, h_bf[6])
-        quantize_h(7, h_bf[7])
+        second2(4, "S", "y", 2)
         second2(5, "S", "y", 2)
-        second2(6, "S", "y", 2)
         store(512, 768)
+        tanh256(3, 1, ga[7])
+        h_bf[6] = hidden2(6, ub[6])
+        quantize_h(6, h_bf[6])
+        second2(6, "S", "y", 2)
+        ub[7] = first_product(7, "ub", 3, wu_tile)
+        h_bf[7] = hidden2(7, ub[7])
+        quantize_h(7, h_bf[7])
+        second_half(7, 0, "V", "y", 2)
         store(768, 896)
-        second2(7, "S", "y", 2)
-        store(896, 1024)
+        store_half(7, 0)
+        second_half(7, 1, "V", "y", 2)
+        store_half(7, 1)

@@ -35,11 +35,11 @@ def tile_list_tanh_none_kernel(
         offsets = keep.tile([P, J // 16], U16, name="offsets")
         wgt_sb = keep.tile([P, J], F32, name="wgt_sb")
         planes = [[keep.tile([P, T], F32, name="plane_%d_%d" % (a, i)) for i in range(PACK)] for a in range(PASSES)]
-        picked = [keep.tile([P, PACK, J], F32, name="picked_%d" % a) for a in range(PASSES)]
+        picked = [[keep.tile([P, PACK, 512], F32, name="picked_%d_%d" % (a, h)) for h in range(2)] for a in range(PASSES)]
         x_bf = [keep.tile([P, J, PACK], BF16, name="x_bf_%d" % a, align_bytes=64) for a in range(PASSES)]
         x_codes = [keep.tile([P, J], U32, name="x_codes_%d" % a, align_bytes=64) for a in range(PASSES)]
         x_scales = [keep.tile([P, J], U8, name="x_scales_%d" % a, align_bytes=64) for a in range(PASSES)]
-        wg_raw = [keep.tile([P, PACK, R], F32, name="wg_raw_%d" % a) for a in range(PASSES)]
+        wg_raw = [[keep.tile([P, PACK, 256], F32, name="wg_raw_%d_%d" % (a, h)) for h in range(2)] for a in range(PASSES)]
         wg_bf = [keep.tile([P, R, PACK], BF16, name="wg_bf_%d" % a, align_bytes=64) for a in range(PASSES)]
         wg_codes = [keep.tile([P, R], U32, name="wg_codes_%d" % a, align_bytes=64) for a in range(PASSES)]
         wg_scales = [keep.tile([P, R], U8, name="wg_scales_%d" % a, align_bytes=64) for a in range(PASSES)]
@@ -51,7 +51,13 @@ def tile_list_tanh_none_kernel(
         wd_sc = keep.tile([P, N], U8, name="wd_sc", align_bytes=64)
         h_codes = keep.tile([P, J], U32, name="h_codes", align_bytes=64)
         h_scales = keep.tile([P, J], U8, name="h_scales", align_bytes=64)
-        y_sb = keep.tile([P, N // P, J], F32, name="y_sb")
+        y_groups = [[0,1],[1,3],[3,5],[5,7]]
+        y_tiles = {}
+        for c0, c1 in y_groups:
+            y_tile = keep.tile([P, N // P, (c1 - c0) * CH], F32, name="y_sb_%d" % c0)
+            for c in range(c0, c1):
+                y_tiles[c] = (y_tile, c - c0)
+        y_last = [keep.tile([P, 2, CH], F32, name="y_last_%d" % u) for u in range(2)]
         warm = keep.tile([P, 1], F32, name="warm")
 
         x_rows = xT.rearrange("(a p i) t -> a p i t", p=P, i=PACK)
@@ -62,7 +68,7 @@ def tile_list_tanh_none_kernel(
             nc.sync.dma_start(out=planes[a][i][:], in_=x_rows[a, :, i, :])
 
         def load_wg(a, r0, r1):
-            nc.sync.dma_start(out=wg_raw[a][:, :, r0:r1], in_=wg_rows[a, :, :, r0:r1])
+            nc.sync.dma_start(out=wg_raw[a][r0 // 256][:], in_=wg_rows[a, :, :, r0:r1])
 
         def load_wgt(j0, j1):
             nc.sync.dma_start(out=wgt_sb[:, j0:j1], in_=wgt[:, j0:j1])
@@ -81,7 +87,7 @@ def tile_list_tanh_none_kernel(
 
         def gather(a, i, j0, j1):
             nc.vector.tensor_tensor(
-                out=picked[a][:, i, j0:j1],
+                out=picked[a][j0 // 512][:, i, j0 % 512 : j0 % 512 + j1 - j0],
                 in0=planes[a][i][:].indirect(offsets[:, j0 // 16 : j1 // 16]),
                 in1=wgt_sb[:, j0:j1],
                 op=MULT,
@@ -91,7 +97,7 @@ def tile_list_tanh_none_kernel(
             copy_on(
                 engine,
                 x_bf[a][:, j0:j1, :].rearrange("p (c e) i -> p c i e", e=4),
-                picked[a][:, :, j0:j1].rearrange("p i (c e) -> p c i e", e=4),
+                picked[a][j0 // 512][:, :, j0 % 512 : j0 % 512 + j1 - j0].rearrange("p i (c e) -> p c i e", e=4),
             )
 
         def quantize_x(a, j0, j1):
@@ -105,7 +111,7 @@ def tile_list_tanh_none_kernel(
             copy_on(
                 engine,
                 wg_bf[a][:].rearrange("p (t m) i -> p m i t", t=PACK)[:, r0 // PACK : r1 // PACK, :, :],
-                wg_raw[a][:, :, r0:r1].rearrange("p i (m t) -> p m i t", t=PACK),
+                wg_raw[a][r0 // 256][:].rearrange("p i (m t) -> p m i t", t=PACK),
             )
 
         def quantize_wg(a, c0, c1):
@@ -167,17 +173,17 @@ def tile_list_tanh_none_kernel(
                     start=True,
                     stop=True,
                 )
-            copy_on(engine, y_sb[:, :, js], y[:])
+            copy_on(engine, y_tiles[c][0][:, :, y_tiles[c][1] * CH : (y_tiles[c][1] + 1) * CH], y[:])
 
         def store(j0, j1):
-            nc.sync.dma_start(out=out_rows[:, :, j0:j1], in_=y_sb[:, :, j0:j1])
+            nc.sync.dma_start(out=out_rows[:, :, j0:j1], in_=y_tiles[j0 // CH][0][:])
 
-        th_all = keep.tile([P, PACK, J], F32, name="th_all")
+        th_all = [keep.tile([P, PACK, 256], F32, name="th_%d" % g) for g in range(4)]
         ga_banks = {}
 
-        def clear_scales():
-            nc.gpsimd.memset(wu_sc_raw[:].rearrange("p a r -> p (a r)").bitcast(I32), 0)
-            nc.gpsimd.memset(wd_sc[:].bitcast(I32), 0)
+        def clear_scales_v():
+            nc.vector.memset(wu_sc_raw[:].rearrange("p a r -> p (a r)").bitcast(I32), 0)
+            nc.vector.memset(wd_sc[:].bitcast(I32), 0)
 
         def load_offsets():
             nc.sync.dma_start(offsets[:], offs)
@@ -213,7 +219,7 @@ def tile_list_tanh_none_kernel(
 
         def ga_pass(h, a, t):
             if a == 0:
-                ga_banks[t] = psum.tile([P, 512], F32, name="ga%d" % t, tag="ga%d" % t, bufs=1)
+                ga_banks[t] = psum.tile([P, 512], F32, name="ga%d" % t, tag="b%d" % t, bufs=1)
             js = slice(512 * h, 512 * (h + 1))
             codes, scales = wg_tile(a, t)
             nc.tensor.matmul_mx(
@@ -227,14 +233,14 @@ def tile_list_tanh_none_kernel(
             )
 
         def tanh(t, j0, j1):
-            nc.scalar.activation(out=th_all[:, t, j0:j1], in_=ga_banks[t][:, j0 % 512 : j0 % 512 + j1 - j0], func=TANH)
+            nc.scalar.activation(out=th_all[j0 // 256][:, t, :], in_=ga_banks[t][:, j0 % 512 : j0 % 512 + j1 - j0], func=TANH)
 
         def hidden2(c, acc):
             h_tile = ring.tile([P, CH, PACK], BF16, name="h_tile", tag="h_tile", align_bytes=64)
             nc.vector.tensor_tensor(
                 out=h_tile[:].rearrange("p (g e) t -> p g t e", e=4),
                 in0=acc[:].rearrange("p t (g e) -> p g t e", e=4),
-                in1=th_all[:, :, c * CH : (c + 1) * CH].rearrange("p t (g e) -> p g t e", e=4),
+                in1=th_all[c // 2][:, :, c % 2 * CH : (c % 2 + 1) * CH].rearrange("p t (g e) -> p g t e", e=4),
                 op=MULT,
             )
             return h_tile
@@ -252,7 +258,7 @@ def tile_list_tanh_none_kernel(
                     start=True,
                     stop=True,
                 )
-            copy_on(engine, y_sb[:, :, js], y[:])
+            copy_on(engine, y_tiles[c][0][:, :, y_tiles[c][1] * CH : (y_tiles[c][1] + 1) * CH], y[:])
 
         wgt_late = keep.tile([P, J], F32, name="wgt_late")
 
@@ -261,14 +267,14 @@ def tile_list_tanh_none_kernel(
 
         def gather2(a, i, j0, j1):
             nc.vector.tensor_tensor(
-                out=picked[a][:, i, j0:j1],
+                out=picked[a][j0 // 512][:, i, j0 % 512 : j0 % 512 + j1 - j0],
                 in0=planes[a][i][:].indirect(offsets[:, j0 // 16 : j1 // 16]),
                 in1=wgt_late[:, j0:j1],
                 op=MULT,
             )
 
-        def ga256(g, u, bufs):
-            acc = psum.tile([P, 2, 256], F32, name="g2", tag="g2", bufs=bufs)
+        def ga256(g, u, bufs, tag):
+            acc = psum.tile([P, 2, 256], F32, name="g2", tag=tag, bufs=bufs)
             js = slice(256 * g, 256 * (g + 1))
             for v in range(2):
                 for a in range(PASSES):
@@ -285,7 +291,7 @@ def tile_list_tanh_none_kernel(
             return acc
 
         def tanh256(g, u, acc):
-            nc.scalar.activation(out=th_all[:, 2 * u : 2 * u + 2, 256 * g : 256 * (g + 1)], in_=acc[:], func=TANH)
+            nc.scalar.activation(out=th_all[g][:, 2 * u : 2 * u + 2, :], in_=acc[:], func=TANH)
 
         def second_half(c, u, engine, tag, bufs):
             js = slice(c * CH, (c + 1) * CH)
@@ -301,24 +307,41 @@ def tile_list_tanh_none_kernel(
                     start=True,
                     stop=True,
                 )
-            copy_on(engine, y_sb[:, 2 * u : 2 * u + 2, js], y[:])
+            copy_on(engine, y_last[u][:], y[:])
 
         def store_half(c, u):
             js = slice(c * CH, (c + 1) * CH)
-            nc.sync.dma_start(out=out_rows[:, 2 * u : 2 * u + 2, js], in_=y_sb[:, 2 * u : 2 * u + 2, js])
+            nc.sync.dma_start(out=out_rows[:, 2 * u : 2 * u + 2, js], in_=y_last[u][:])
 
         def interleave_pair(engine, a, u, j0, j1):
             copy_on(
                 engine,
                 x_bf[a][:, j0:j1, 2 * u : 2 * u + 2],
-                picked[a][:, 2 * u : 2 * u + 2, j0:j1].rearrange("p i j -> p j i"),
+                picked[a][j0 // 512][:, 2 * u : 2 * u + 2, j0 % 512 : j0 % 512 + j1 - j0].rearrange("p i j -> p j i"),
+            )
+
+        wg_half = [keep.tile([P, PACK, 64, PACK], BF16, name="wg_half_%d" % h, align_bytes=64) for h in range(2)]
+
+        def interleave_wgh(engine, a, h):
+            copy_on(
+                engine,
+                wg_half[h][:].rearrange("p t m i -> p m i t"),
+                wg_raw[a][h][:].rearrange("p i (m t) -> p m i t", t=PACK),
+            )
+
+        def quantize_wgh(a, h, t):
+            cols = slice(P * t + 64 * h, P * t + 64 * (h + 1))
+            nc.vector.quantize_mx(
+                out=wg_codes[a][:, cols].bitcast(FP8X4),
+                scales=wg_scales[a][:, cols],
+                in_=wg_half[h][:, t, :, :].rearrange("p m i -> p (m i)"),
             )
 
         ub = {}
         h_bf = {}
         ga = {}
         th = {}
-        clear_scales()
+        clear_scales_v()
         load_offsets()
         load_wu()
         load_wgt(0, 512)
@@ -329,9 +352,10 @@ def tile_list_tanh_none_kernel(
         load_plane(0, 2)
         load_plane(0, 3)
         load_plane(1, 0)
-        load_wg(0, 0, R)
         load_plane(1, 1)
         load_plane(1, 2)
+        load_wg(0, 0, 256)
+        load_wg(0, 256, 512)
         load_plane(1, 3)
         load_wg(1, 0, 256)
         load_wg(1, 256, 512)
@@ -349,93 +373,101 @@ def tile_list_tanh_none_kernel(
         gather(0, 2, 0, 512)
         gather(0, 2, 512, 1024)
         gather(0, 3, 0, 256)
-        gather(0, 3, 256, 512)
-        gather(0, 3, 768, 1024)
-        gather(0, 3, 512, 768)
-        gather(1, 1, 512, 1024)
-        gather(1, 0, 512, 1024)
-        gather(1, 2, 0, 256)
         interleave_x("S", 0, 0, 256)
-        interleave_x("S", 0, 256, 512)
-        gather(1, 1, 0, 512)
-        interleave_wg("S", 0, 0, R)
-        quantize_wg(0, 0, R)
-        gather(1, 3, 0, 256)
-        interleave_x("S", 0, 512, 768)
-        interleave_x("V", 0, 768, 1024)
+        gather(0, 3, 256, 512)
+        gather(0, 3, 512, 768)
         gather(1, 0, 0, 512)
-        quantize_x(0, 512, 1024)
-        interleave_x("V", 1, 0, 256)
-        interleave_wg("S", 1, 256, 512)
-        quantize_x(0, 0, 512)
-        quantize_x(1, 0, 256)
-        gather(1, 3, 256, 512)
-        interleave_wg("S", 1, 0, 256)
-        ub[0] = first_product(0, "ub", 3, wu_tile)
-        ub[1] = first_product(1, "ub", 3, wu_tile)
-        gather(1, 2, 256, 512)
-        interleave_x("V", 1, 256, 512)
-        quantize_x(1, 256, 512)
-        gather2(1, 2, 512, 768)
+        gather(1, 3, 0, 128)
+        interleave_x("S", 0, 256, 512)
+        gather(0, 3, 768, 1024)
+        gather(1, 3, 128, 256)
+        gather(1, 2, 0, 512)
         gather2(1, 3, 512, 768)
+        interleave_wgh("V", 1, 1)
+        interleave_x("S", 0, 512, 768)
+        interleave_x("S", 0, 768, 1024)
+        interleave_wgh("S", 1, 0)
+        quantize_wgh(1, 0, 1)
+        quantize_wgh(1, 0, 2)
+        interleave_wg("S", 0, 0, 256)
+        gather(1, 3, 256, 512)
+        quantize_x(0, 0, 512)
+        gather(1, 1, 0, 512)
+        interleave_x("S", 1, 0, 128)
+        quantize_x(1, 0, 128)
+        ub[0] = first_product(0, "b4", 1, wu_tile)
+        interleave_x("S", 1, 128, 256)
+        interleave_wg("S", 0, 256, 512)
+        quantize_x(1, 128, 256)
+        quantize_wgh(1, 1, 2)
+        interleave_x("V", 1, 256, 512)
+        quantize_wgh(1, 1, 3)
+        ub[1] = first_product(1, "b5", 1, wu_tile)
+        quantize_wgh(1, 0, 3)
+        quantize_wg(0, 0, R)
+        quantize_x(0, 512, 1024)
+        quantize_x(1, 256, 512)
+        ub[2] = first_product(2, "b6", 1, wu_tile)
+        quantize_wgh(1, 0, 0)
+        quantize_wgh(1, 1, 0)
+        quantize_wgh(1, 1, 1)
+        gather2(1, 3, 768, 1024)
+        gather(1, 0, 512, 1024)
+        ga[0] = ga256(0, 0, 1, "b0")
+        tanh256(0, 0, ga[0])
+        ga[1] = ga256(0, 1, 1, "b1")
+        ga[2] = ga256(1, 0, 1, "b2")
+        gather(1, 2, 512, 1024)
+        ga[3] = ga256(1, 1, 1, "b3")
+        gather(1, 1, 512, 1024)
         interleave_x("S", 1, 512, 768)
         quantize_x(1, 512, 768)
-        ub[2] = first_product(2, "ub", 3, wu_tile)
-        quantize_wg(1, 0, 256)
-        quantize_wg(1, 256, 512)
-        ga[0] = ga256(0, 0, 3)
-        tanh256(0, 0, ga[0])
-        ga[1] = ga256(0, 1, 3)
-        ga[2] = ga256(1, 0, 3)
-        gather2(1, 2, 768, 1024)
+        ub[3] = first_product(3, "b7", 1, wu_tile)
+        ga[4] = ga256(2, 0, 1, "b0")
         tanh256(0, 1, ga[1])
         h_bf[0] = hidden2(0, ub[0])
-        h_bf[1] = hidden2(1, ub[1])
-        gather2(1, 3, 768, 1024)
         interleave_x("V", 1, 768, 1024)
-        ga[3] = ga256(1, 1, 3)
-        ga[4] = ga256(2, 0, 3)
+        h_bf[1] = hidden2(1, ub[1])
         quantize_h(0, h_bf[0])
-        quantize_h(1, h_bf[1])
-        ub[3] = first_product(3, "ub", 3, wu_tile)
         tanh256(1, 0, ga[2])
         tanh256(1, 1, ga[3])
-        h_bf[2] = hidden2(2, ub[2])
-        tanh256(2, 0, ga[4])
-        ga[5] = ga256(2, 1, 3)
+        quantize_h(1, h_bf[1])
+        ga[5] = ga256(2, 1, 1, "b1")
         quantize_x(1, 768, 1024)
+        ga[6] = ga256(3, 0, 1, "b2")
+        tanh256(2, 0, ga[4])
+        h_bf[2] = hidden2(2, ub[2])
         h_bf[3] = hidden2(3, ub[3])
-        ga[6] = ga256(3, 0, 3)
+        ga[7] = ga256(3, 1, 1, "b3")
         quantize_h(2, h_bf[2])
-        second2(0, "V", "y", 2)
-        second2(1, "S", "y", 2)
-        store(0, 256)
-        quantize_h(3, h_bf[3])
+        second2(0, "S", "b5", 1)
+        second2(1, "S", "b4", 1)
+        ub[4] = first_product(4, "b0", 1, wu_tile)
         tanh256(2, 1, ga[5])
-        second2(2, "S", "y", 2)
-        second2(3, "S", "y", 2)
-        ub[4] = first_product(4, "ub", 3, wu_tile)
-        ub[5] = first_product(5, "ub", 3, wu_tile)
+        store(0, 128)
+        quantize_h(3, h_bf[3])
         tanh256(3, 0, ga[6])
+        ub[5] = first_product(5, "b1", 1, wu_tile)
         h_bf[4] = hidden2(4, ub[4])
+        second2(2, "S", "b2", 1)
         quantize_h(4, h_bf[4])
-        ga[7] = ga256(3, 1, 3)
-        store(256, 512)
-        ub[6] = first_product(6, "ub", 3, wu_tile)
+        ub[6] = first_product(6, "b5", 1, wu_tile)
+        second2(3, "S", "b4", 1)
         h_bf[5] = hidden2(5, ub[5])
         quantize_h(5, h_bf[5])
-        second2(4, "S", "y", 2)
-        second2(5, "S", "y", 2)
-        store(512, 768)
+        store(128, 384)
+        second2(4, "S", "b1", 1)
+        ub[7] = first_product(7, "b0", 1, wu_tile)
+        store(384, 640)
+        second2(5, "V", "b2", 1)
         tanh256(3, 1, ga[7])
         h_bf[6] = hidden2(6, ub[6])
         quantize_h(6, h_bf[6])
-        second2(6, "S", "y", 2)
-        ub[7] = first_product(7, "ub", 3, wu_tile)
         h_bf[7] = hidden2(7, ub[7])
         quantize_h(7, h_bf[7])
-        second_half(7, 0, "V", "y", 2)
-        store(768, 896)
+        second2(6, "S", "b7", 1)
+        second_half(7, 0, "S", "b7", 1)
+        store(640, 896)
         store_half(7, 0)
-        second_half(7, 1, "V", "y", 2)
+        second_half(7, 1, "S", "b6", 1)
         store_half(7, 1)

@@ -20,7 +20,7 @@ P = 128
 PACK = 4
 PASSES = K // (P * PACK)
 CH = 128
-CHUNKS = J // CH
+QUARTER = 256
 
 
 def tile_list_tanh_none_kernel(
@@ -29,18 +29,23 @@ def tile_list_tanh_none_kernel(
     nc = tc.nc
     with ExitStack() as ctx:
         keep = ctx.enter_context(tc.tile_pool(name="keep", bufs=1))
-        ring = ctx.enter_context(tc.tile_pool(name="ring", bufs=8))
         psum = ctx.enter_context(tc.psum_pool(name="psum", bufs=1))
 
         offsets = keep.tile([P, J // 16], U16, name="offsets")
         wgt_sb = keep.tile([P, J], F32, name="wgt_sb")
-        planes = [[keep.tile([P, T], F32, name="plane_%d_%d" % (a, i)) for i in range(PACK)] for a in range(PASSES)]
-        picked = [[keep.tile([P, PACK, 512], F32, name="picked_%d_%d" % (a, h)) for h in range(2)] for a in range(PASSES)]
-        x_bf = [keep.tile([P, J, PACK], BF16, name="x_bf_%d" % a, align_bytes=64) for a in range(PASSES)]
-        x_codes = [keep.tile([P, J], U32, name="x_codes_%d" % a, align_bytes=64) for a in range(PASSES)]
-        x_scales = [keep.tile([P, J], U8, name="x_scales_%d" % a, align_bytes=64) for a in range(PASSES)]
-        wg_raw = [[keep.tile([P, PACK, 256], F32, name="wg_raw_%d_%d" % (a, h)) for h in range(2)] for a in range(PASSES)]
-        wg_bf = [keep.tile([P, R, PACK], BF16, name="wg_bf_%d" % a, align_bytes=64) for a in range(PASSES)]
+        planes = [[keep.tile([P, T], F32, name="plane_%d_%d" % (a, i), align_bytes=64) for i in range(PACK)] for a in range(PASSES)]
+        picked_0 = keep.tile([P, PACK, J], F32, name="picked_0")
+        picked_first = keep.tile([P, 2, J], F32, name="picked_first")
+        picked_low = keep.tile([P, 2, J // 2], F32, name="picked_low")
+        shared = keep.tile([P, 3, J // 2], F32, name="shared", align_bytes=64)
+        x_bf = {}
+        x_mx = {}
+        wg_raw = [[keep.tile([P, PACK, R // 2], F32, name="wg_raw_%d_%d" % (a, h), align_bytes=64) for h in range(2)] for a in range(PASSES)]
+        wg_bf_0 = keep.tile([P, R, PACK], BF16, name="wg_bf_0", align_bytes=64)
+        wg_bf = [
+            wg_bf_0[:],
+            shared[:, 1:3, :].rearrange("p s j -> p (s j)").bitcast(BF16).rearrange("p (r i) -> p r i", i=PACK),
+        ]
         wg_codes = [keep.tile([P, R], U32, name="wg_codes_%d" % a, align_bytes=64) for a in range(PASSES)]
         wg_scales = [keep.tile([P, R], U8, name="wg_scales_%d" % a, align_bytes=64) for a in range(PASSES)]
         wu_raw = keep.tile([P, PASSES, 2 * R], U8, name="wu_raw", align_bytes=64)
@@ -49,15 +54,10 @@ def tile_list_tanh_none_kernel(
         wu_sc = keep.tile([P, PASSES, R], U8, name="wu_sc", align_bytes=64)
         wd_codes = keep.tile([P, N], I32, name="wd_codes", align_bytes=64)
         wd_sc = keep.tile([P, N], U8, name="wd_sc", align_bytes=64)
+        th = [keep.tile([P, PACK, QUARTER], F32, name="th_%d" % g) for g in range(J // QUARTER)]
+        h_bf = keep.tile([P, J, PACK], BF16, name="h_bf", align_bytes=64)
         h_codes = keep.tile([P, J], U32, name="h_codes", align_bytes=64)
         h_scales = keep.tile([P, J], U8, name="h_scales", align_bytes=64)
-        y_groups = [[0,1],[1,3],[3,5],[5,7]]
-        y_tiles = {}
-        for c0, c1 in y_groups:
-            y_tile = keep.tile([P, N // P, (c1 - c0) * CH], F32, name="y_sb_%d" % c0)
-            for c in range(c0, c1):
-                y_tiles[c] = (y_tile, c - c0)
-        y_last = [keep.tile([P, 2, CH], F32, name="y_last_%d" % u) for u in range(2)]
         warm = keep.tile([P, 1], F32, name="warm")
 
         x_rows = xT.rearrange("(a p i) t -> a p i t", p=P, i=PACK)
@@ -67,17 +67,25 @@ def tile_list_tanh_none_kernel(
         def load_plane(a, i):
             nc.sync.dma_start(out=planes[a][i][:], in_=x_rows[a, :, i, :])
 
-        def load_wg(a, r0, r1):
-            nc.sync.dma_start(out=wg_raw[a][r0 // 256][:], in_=wg_rows[a, :, :, r0:r1])
+        def load_wg(a, h):
+            nc.sync.dma_start(out=wg_raw[a][h][:], in_=wg_rows[a, :, :, h * R // 2 : (h + 1) * R // 2])
 
         def load_wgt(j0, j1):
             nc.sync.dma_start(out=wgt_sb[:, j0:j1], in_=wgt[:, j0:j1])
 
-        def load_wu():
-            nc.sync.dma_start(out=wu_raw[:].bitcast(I32), in_=wu_words.rearrange("a p b -> p a b").bitcast(I32))
+        def load_wu_scales():
+            for q in range(4):
+                nc.sync.dma_start(
+                    out=wu_sc_raw[32 * q : 32 * q + 4, :, :].bitcast(I32),
+                    in_=wu_scales[:, 4 * q : 4 * q + 4, :].rearrange("a s r -> s a r").bitcast(I32),
+                )
 
-        def load_wd():
-            nc.sync.dma_start(out=wd_codes[:], in_=wd_words[0].rearrange("p n i -> p (n i)").bitcast(I32))
+        def load_wd_scales():
+            for q in range(4):
+                nc.sync.dma_start(
+                    out=wd_sc[32 * q : 32 * q + 4, :].bitcast(I32),
+                    in_=wd_scales[0, 4 * q : 4 * q + 4, :].bitcast(I32),
+                )
 
         def copy_on(engine, dst, src):
             if engine == "S":
@@ -85,33 +93,69 @@ def tile_list_tanh_none_kernel(
             else:
                 nc.vector.tensor_copy(out=dst, in_=src)
 
+        def picks(a, i0, i1, j0, j1):
+            if a == 0:
+                return picked_0[:, i0:i1, j0:j1]
+            if i1 <= 2:
+                return picked_first[:, i0:i1, j0:j1]
+            if j1 <= J // 2:
+                return picked_low[:, i0 - 2 : i1 - 2, j0:j1]
+            return shared[:, i0 - 2 : i1 - 2, j0 - J // 2 : j1 - J // 2]
+
         def gather(a, i, j0, j1):
             nc.vector.tensor_tensor(
-                out=picked[a][j0 // 512][:, i, j0 % 512 : j0 % 512 + j1 - j0],
+                out=picks(a, i, i + 1, j0, j1).rearrange("p i j -> p (i j)"),
                 in0=planes[a][i][:].indirect(offsets[:, j0 // 16 : j1 // 16]),
                 in1=wgt_sb[:, j0:j1],
                 op=MULT,
             )
 
+        def x_tile(a, j0, j1, tag):
+            tile = keep.tile([P, j1 - j0, PACK], BF16, name=tag, tag=tag, align_bytes=64)
+            for j in range(j0, j1, CH):
+                x_bf[a, j] = (tile, j0)
+
+        def x_cols(a, j0, j1):
+            tile, first = x_bf[a, j0]
+            return tile[:, j0 - first : j1 - first, :]
+
         def interleave_x(engine, a, j0, j1):
             copy_on(
                 engine,
-                x_bf[a][:, j0:j1, :].rearrange("p (c e) i -> p c i e", e=4),
-                picked[a][j0 // 512][:, :, j0 % 512 : j0 % 512 + j1 - j0].rearrange("p i (c e) -> p c i e", e=4),
+                x_cols(a, j0, j1).rearrange("p (c e) i -> p c i e", e=4),
+                picks(a, 0, PACK, j0, j1).rearrange("p i (c e) -> p c i e", e=4),
             )
 
-        def quantize_x(a, j0, j1):
-            nc.vector.quantize_mx(
-                out=x_codes[a][:, j0:j1].bitcast(FP8X4),
-                scales=x_scales[a][:, j0:j1],
-                in_=x_bf[a][:, j0:j1, :].rearrange("p j i -> p (j i)"),
-            )
-
-        def interleave_wg(engine, a, r0, r1):
+        def interleave_pair(engine, a, u, j0, j1):
             copy_on(
                 engine,
-                wg_bf[a][:].rearrange("p (t m) i -> p m i t", t=PACK)[:, r0 // PACK : r1 // PACK, :, :],
-                wg_raw[a][r0 // 256][:].rearrange("p i (m t) -> p m i t", t=PACK),
+                x_cols(a, j0, j1)[:, :, 2 * u : 2 * u + 2].rearrange("p (c e) i -> p c i e", e=4),
+                picks(a, 2 * u, 2 * u + 2, j0, j1).rearrange("p i (c e) -> p c i e", e=4),
+            )
+
+        def mx_tiles(a, j0, j1, scale_tag):
+            codes = keep.tile([P, j1 - j0], U32, name="x_codes_%d_%d" % (a, j0), align_bytes=64)
+            scales = keep.tile([P, j1 - j0], U8, name=scale_tag, tag=scale_tag, align_bytes=64)
+            for j in range(j0, j1, CH):
+                x_mx[a, j] = (codes, scales, j0)
+
+        def x_operand(a, j0, j1):
+            codes, scales, first = x_mx[a, j0]
+            return codes[:, j0 - first : j1 - first].bitcast(FP8X4), scales[:, j0 - first : j1 - first]
+
+        def quantize_x(a, j0, j1):
+            codes, scales = x_operand(a, j0, j1)
+            nc.vector.quantize_mx(
+                out=codes,
+                scales=scales,
+                in_=x_cols(a, j0, j1).rearrange("p j i -> p (j i)"),
+            )
+
+        def interleave_wg(engine, a, h):
+            copy_on(
+                engine,
+                wg_bf[a].rearrange("p (t m) i -> p m i t", t=PACK)[:, h * 64 : (h + 1) * 64, :, :],
+                wg_raw[a][h][:].rearrange("p i (m t) -> p m i t", t=PACK),
             )
 
         def quantize_wg(a, c0, c1):
@@ -121,353 +165,211 @@ def tile_list_tanh_none_kernel(
                 in_=wg_bf[a][:, c0:c1, :].rearrange("p c i -> p (c i)"),
             )
 
-        def first_product(c, tag, bufs, weights):
-            acc = psum.tile([P, PACK, CH], F32, name=tag, tag=tag, bufs=bufs)
-            js = slice(c * CH, (c + 1) * CH)
+        def bank(b, slices):
+            return psum.tile([P, slices, 512 // slices], F32, name="bank_%d" % b, tag="bank_%d" % b)
+
+        def up_pass(acc, c, a):
+            codes, scales = x_operand(a, c * CH, (c + 1) * CH)
             for t in range(PACK):
-                for a in range(PASSES):
-                    codes, scales = weights(a, t)
-                    nc.tensor.matmul_mx(
-                        out=acc[:, t, :],
-                        lhsT=codes,
-                        lhsT_scale=scales,
-                        rhs=x_codes[a][:, js].bitcast(FP8X4),
-                        rhs_scale=x_scales[a][:, js],
-                        start=(a == 0),
-                        stop=(a == PASSES - 1),
-                    )
-            return acc
+                nc.tensor.matmul_mx(
+                    out=acc[:, t, :],
+                    lhsT=wu_codes[:, a, 2 * P * t : 2 * P * (t + 1)].bitcast(FP4X4),
+                    lhsT_scale=wu_sc[:, a, P * t : P * (t + 1)],
+                    rhs=codes,
+                    rhs_scale=scales,
+                    start=(a == 0 and t == 0),
+                    stop=(a == PASSES - 1 and t == PACK - 1),
+                )
 
-        def wu_tile(a, t):
-            return wu_codes[:, a, 2 * P * t : 2 * P * (t + 1)].bitcast(FP4X4), wu_sc[:, a, P * t : P * (t + 1)]
+        def gate_pass(acc, g, u, a):
+            codes, scales = x_operand(a, g * QUARTER, (g + 1) * QUARTER)
+            for v in range(2):
+                t = 2 * u + v
+                nc.tensor.matmul_mx(
+                    out=acc[:, v, :],
+                    lhsT=wg_codes[a][:, P * t : P * (t + 1)].bitcast(FP8X4),
+                    lhsT_scale=wg_scales[a][:, P * t : P * (t + 1)],
+                    rhs=codes,
+                    rhs_scale=scales,
+                    start=(a == 0 and v == 0),
+                    stop=(a == PASSES - 1 and v == 1),
+                )
 
-        def wg_tile(a, t):
-            return wg_codes[a][:, P * t : P * (t + 1)].bitcast(FP8X4), wg_scales[a][:, P * t : P * (t + 1)]
+        def tanh(acc, g, u):
+            nc.scalar.activation(out=th[g][:, 2 * u : 2 * u + 2, :], in_=acc[:], func=TANH)
 
-        def gate(ga):
-            th = ring.tile([P, CH, PACK], F32, name="th", tag="th")
-            nc.scalar.activation(out=th[:], in_=ga[:].rearrange("p t j -> p j t"), func=TANH)
-            return th
-
-        def hidden(ub, th):
-            h_bf = ring.tile([P, CH, PACK], BF16, name="h_bf", tag="h_bf", align_bytes=64)
-            nc.vector.tensor_tensor(out=h_bf[:], in0=ub[:].rearrange("p t j -> p j t"), in1=th[:], op=MULT)
-            return h_bf
-
-        def quantize_h(c, h_bf):
-            js = slice(c * CH, (c + 1) * CH)
-            nc.vector.quantize_mx(
-                out=h_codes[:, js].bitcast(FP8X4), scales=h_scales[:, js], in_=h_bf[:].rearrange("p j t -> p (j t)")
+        def hidden(acc, c):
+            nc.vector.tensor_tensor(
+                out=h_bf[:, c * CH : (c + 1) * CH, :].rearrange("p (g e) t -> p g t e", e=4),
+                in0=acc[:].rearrange("p t (g e) -> p g t e", e=4),
+                in1=th[c // 2][:, :, c % 2 * CH : (c % 2 + 1) * CH].rearrange("p t (g e) -> p g t e", e=4),
+                op=MULT,
             )
 
-        def second_product(c, engine):
-            js = slice(c * CH, (c + 1) * CH)
-            y = psum.tile([P, N // P, CH], F32, name="y", tag="y", bufs=2)
-            for q in range(N // P):
+        def quantize_h(j0, j1):
+            nc.vector.quantize_mx(
+                out=h_codes[:, j0:j1].bitcast(FP8X4),
+                scales=h_scales[:, j0:j1],
+                in_=h_bf[:, j0:j1, :].rearrange("p j t -> p (j t)"),
+            )
+
+        def down(b, engine, q0, q1, j0, j1):
+            acc = psum.tile([P, q1 - q0, j1 - j0], F32, name="bank_%d" % b, tag="bank_%d" % b)
+            for q in range(q0, q1):
                 nc.tensor.matmul_mx(
-                    out=y[:, q, :],
+                    out=acc[:, q - q0, :],
                     lhsT=wd_codes[:, P * q : P * (q + 1)].bitcast(FP8X4),
                     lhsT_scale=wd_sc[:, P * q : P * (q + 1)],
-                    rhs=h_codes[:, js].bitcast(FP8X4),
-                    rhs_scale=h_scales[:, js],
+                    rhs=h_codes[:, j0:j1].bitcast(FP8X4),
+                    rhs_scale=h_scales[:, j0:j1],
                     start=True,
                     stop=True,
                 )
-            copy_on(engine, y_tiles[c][0][:, :, y_tiles[c][1] * CH : (y_tiles[c][1] + 1) * CH], y[:])
+            y = keep.tile([P, q1 - q0, j1 - j0], F32, name="y_%d_%d" % (q0, j0))
+            copy_on(engine, y[:], acc[:])
+            nc.sync.dma_start(out=out_rows[:, q0:q1, j0:j1], in_=y[:])
 
-        def store(j0, j1):
-            nc.sync.dma_start(out=out_rows[:, :, j0:j1], in_=y_tiles[j0 // CH][0][:])
-
-        th_all = [keep.tile([P, PACK, 256], F32, name="th_%d" % g) for g in range(4)]
-        ga_banks = {}
-
-        def clear_scales_v():
-            nc.vector.memset(wu_sc_raw[:].rearrange("p a r -> p (a r)").bitcast(I32), 0)
-            nc.vector.memset(wd_sc[:].bitcast(I32), 0)
-
-        def load_offsets():
-            nc.sync.dma_start(offsets[:], offs)
-
-        def warm_up():
-            nc.scalar.activation(out=warm[:], in_=wgt_sb[:, 0:1], func=TANH)
-
-        def load_wu_scales(queue):
-            for q in range(4):
-                nc.sync.dma_start(
-                    out=wu_sc_raw[32 * q : 32 * q + 4, :, :].bitcast(I32),
-                    in_=wu_scales[:, 4 * q : 4 * q + 4, :].rearrange("a s r -> s a r").bitcast(I32),
+        def permute_wu():
+            for a in range(PASSES):
+                nc.vector.tensor_copy(
+                    out=wu_codes[:, a, :].bitcast(U16).rearrange("p (t m) -> p m t", t=PACK),
+                    in_=wu_raw[:, a, :].bitcast(U16).rearrange("p (m t) -> p m t", t=PACK),
                 )
-
-        def load_wd_scales(queue):
-            for q in range(4):
-                nc.sync.dma_start(
-                    out=wd_sc[32 * q : 32 * q + 4, :].bitcast(I32),
-                    in_=wd_scales[0, 4 * q : 4 * q + 4, :].bitcast(I32),
-                )
-
-        def permute_wu(a):
-            nc.vector.tensor_copy(
-                out=wu_codes[:, a, :].bitcast(U16).rearrange("p (t m) -> p m t", t=PACK),
-                in_=wu_raw[:, a, :].bitcast(U16).rearrange("p (m t) -> p m t", t=PACK),
-            )
-
-        def permute_wu_scales():
             nc.vector.tensor_copy(
                 out=wu_sc[:].rearrange("p a (t m) -> p a m t", t=PACK),
                 in_=wu_sc_raw[:].rearrange("p a (m t) -> p a m t", t=PACK),
             )
 
-        def ga_pass(h, a, t):
-            if a == 0:
-                ga_banks[t] = psum.tile([P, 512], F32, name="ga%d" % t, tag="b%d" % t, bufs=1)
-            js = slice(512 * h, 512 * (h + 1))
-            codes, scales = wg_tile(a, t)
-            nc.tensor.matmul_mx(
-                out=ga_banks[t][:],
-                lhsT=codes,
-                lhsT_scale=scales,
-                rhs=x_codes[a][:, js].bitcast(FP8X4),
-                rhs_scale=x_scales[a][:, js],
-                start=(a == 0),
-                stop=(a == PASSES - 1),
-            )
+        def load_wu():
+            nc.sync.dma_start(out=wu_raw[:].bitcast(I32), in_=wu_words.rearrange("a p b -> p a b").bitcast(I32))
 
-        def tanh(t, j0, j1):
-            nc.scalar.activation(out=th_all[j0 // 256][:, t, :], in_=ga_banks[t][:, j0 % 512 : j0 % 512 + j1 - j0], func=TANH)
+        def load_wd():
+            nc.sync.dma_start(out=wd_codes[:], in_=wd_words[0].rearrange("p n i -> p (n i)").bitcast(I32))
 
-        def hidden2(c, acc):
-            h_tile = ring.tile([P, CH, PACK], BF16, name="h_tile", tag="h_tile", align_bytes=64)
-            nc.vector.tensor_tensor(
-                out=h_tile[:].rearrange("p (g e) t -> p g t e", e=4),
-                in0=acc[:].rearrange("p t (g e) -> p g t e", e=4),
-                in1=th_all[c // 2][:, :, c % 2 * CH : (c % 2 + 1) * CH].rearrange("p t (g e) -> p g t e", e=4),
-                op=MULT,
-            )
-            return h_tile
-
-        def second2(c, engine, tag, bufs):
-            js = slice(c * CH, (c + 1) * CH)
-            y = psum.tile([P, N // P, CH], F32, name="y", tag=tag, bufs=bufs)
-            for q in range(N // P):
-                nc.tensor.matmul_mx(
-                    out=y[:, q, :],
-                    lhsT=wd_codes[:, P * q : P * (q + 1)].bitcast(FP8X4),
-                    lhsT_scale=wd_sc[:, P * q : P * (q + 1)],
-                    rhs=h_codes[:, js].bitcast(FP8X4),
-                    rhs_scale=h_scales[:, js],
-                    start=True,
-                    stop=True,
-                )
-            copy_on(engine, y_tiles[c][0][:, :, y_tiles[c][1] * CH : (y_tiles[c][1] + 1) * CH], y[:])
-
-        wgt_late = keep.tile([P, J], F32, name="wgt_late")
-
-        def load_wgt2(j0, j1):
-            nc.sync.dma_start(out=wgt_late[:, j0:j1], in_=wgt[:, j0:j1])
-
-        def gather2(a, i, j0, j1):
-            nc.vector.tensor_tensor(
-                out=picked[a][j0 // 512][:, i, j0 % 512 : j0 % 512 + j1 - j0],
-                in0=planes[a][i][:].indirect(offsets[:, j0 // 16 : j1 // 16]),
-                in1=wgt_late[:, j0:j1],
-                op=MULT,
-            )
-
-        def ga256(g, u, bufs, tag):
-            acc = psum.tile([P, 2, 256], F32, name="g2", tag=tag, bufs=bufs)
-            js = slice(256 * g, 256 * (g + 1))
-            for v in range(2):
-                for a in range(PASSES):
-                    codes, scales = wg_tile(a, 2 * u + v)
-                    nc.tensor.matmul_mx(
-                        out=acc[:, v, :],
-                        lhsT=codes,
-                        lhsT_scale=scales,
-                        rhs=x_codes[a][:, js].bitcast(FP8X4),
-                        rhs_scale=x_scales[a][:, js],
-                        start=(a == 0),
-                        stop=(a == PASSES - 1),
-                    )
-            return acc
-
-        def tanh256(g, u, acc):
-            nc.scalar.activation(out=th_all[g][:, 2 * u : 2 * u + 2, :], in_=acc[:], func=TANH)
-
-        def second_half(c, u, engine, tag, bufs):
-            js = slice(c * CH, (c + 1) * CH)
-            y = psum.tile([P, 2, CH], F32, name="y", tag=tag, bufs=bufs)
-            for v in range(2):
-                q = 2 * u + v
-                nc.tensor.matmul_mx(
-                    out=y[:, v, :],
-                    lhsT=wd_codes[:, P * q : P * (q + 1)].bitcast(FP8X4),
-                    lhsT_scale=wd_sc[:, P * q : P * (q + 1)],
-                    rhs=h_codes[:, js].bitcast(FP8X4),
-                    rhs_scale=h_scales[:, js],
-                    start=True,
-                    stop=True,
-                )
-            copy_on(engine, y_last[u][:], y[:])
-
-        def store_half(c, u):
-            js = slice(c * CH, (c + 1) * CH)
-            nc.sync.dma_start(out=out_rows[:, 2 * u : 2 * u + 2, js], in_=y_last[u][:])
-
-        def interleave_pair(engine, a, u, j0, j1):
-            copy_on(
-                engine,
-                x_bf[a][:, j0:j1, 2 * u : 2 * u + 2],
-                picked[a][j0 // 512][:, 2 * u : 2 * u + 2, j0 % 512 : j0 % 512 + j1 - j0].rearrange("p i j -> p j i"),
-            )
-
-        wg_half = [keep.tile([P, PACK, 64, PACK], BF16, name="wg_half_%d" % h, align_bytes=64) for h in range(2)]
-
-        def interleave_wgh(engine, a, h):
-            copy_on(
-                engine,
-                wg_half[h][:].rearrange("p t m i -> p m i t"),
-                wg_raw[a][h][:].rearrange("p i (m t) -> p m i t", t=PACK),
-            )
-
-        def quantize_wgh(a, h, t):
-            cols = slice(P * t + 64 * h, P * t + 64 * (h + 1))
-            nc.vector.quantize_mx(
-                out=wg_codes[a][:, cols].bitcast(FP8X4),
-                scales=wg_scales[a][:, cols],
-                in_=wg_half[h][:, t, :, :].rearrange("p m i -> p (m i)"),
-            )
-
-        ub = {}
-        h_bf = {}
-        ga = {}
-        th = {}
-        clear_scales_v()
-        load_offsets()
+        nc.vector.memset(wu_sc_raw[:].rearrange("p a r -> p (a r)").bitcast(I32), 0)
+        nc.vector.memset(wd_sc[:].bitcast(I32), 0)
+        nc.sync.dma_start(offsets[:], offs)
         load_wu()
-        load_wgt(0, 512)
-        load_wu_scales("s")
+        load_wgt(0, 256)
+        load_wu_scales()
         load_plane(0, 0)
-        load_wgt(512, 1024)
-        load_plane(0, 1)
-        load_plane(0, 2)
-        load_plane(0, 3)
-        load_plane(1, 0)
-        load_plane(1, 1)
-        load_plane(1, 2)
-        load_wg(0, 0, 256)
-        load_wg(0, 256, 512)
+        load_wgt(256, J)
+        for i in range(1, PACK):
+            load_plane(0, i)
+        for i in range(PACK - 1):
+            load_plane(1, i)
+        load_wg(0, 0)
+        load_wg(0, 1)
         load_plane(1, 3)
-        load_wg(1, 0, 256)
-        load_wg(1, 256, 512)
-        load_wgt2(512, 1024)
+        load_wg(1, 0)
+        load_wg(1, 1)
         load_wd()
-        load_wd_scales("s")
-        warm_up()
-        permute_wu(0)
-        permute_wu(1)
-        permute_wu_scales()
-        gather(0, 0, 0, 512)
-        gather(0, 0, 512, 1024)
-        gather(0, 1, 0, 512)
-        gather(0, 1, 512, 1024)
-        gather(0, 2, 0, 512)
-        gather(0, 2, 512, 1024)
-        gather(0, 3, 0, 256)
-        interleave_x("S", 0, 0, 256)
-        gather(0, 3, 256, 512)
-        gather(0, 3, 512, 768)
-        gather(1, 0, 0, 512)
-        gather(1, 3, 0, 128)
-        interleave_x("S", 0, 256, 512)
-        gather(0, 3, 768, 1024)
-        gather(1, 3, 128, 256)
-        gather(1, 2, 0, 512)
-        gather2(1, 3, 512, 768)
-        interleave_wgh("V", 1, 1)
-        interleave_x("S", 0, 512, 768)
-        interleave_x("S", 0, 768, 1024)
-        interleave_wgh("S", 1, 0)
-        quantize_wgh(1, 0, 1)
-        quantize_wgh(1, 0, 2)
-        interleave_wg("S", 0, 0, 256)
-        gather(1, 3, 256, 512)
-        quantize_x(0, 0, 512)
+        load_wd_scales()
+        nc.scalar.activation(out=warm[:], in_=wgt_sb[:, 0:1], func=TANH)
+        permute_wu()
+
+        gather(0, 0, 0, 256)
+        gather(0, 0, 256, 512)
+        gather(0, 0, 512, J)
+        gather(0, 1, 0, J)
+        gather(0, 2, 0, J)
+        x_tile(0, 0, J, "x_bf_0")
+        for j0 in range(0, J, 512):
+            gather(0, 3, j0, j0 + 512)
+            interleave_x("S", 0, j0, j0 + 512)
+        gather(1, 0, 0, J)
+        x_tile(1, 0, 512, "x_bf_1")
         gather(1, 1, 0, 512)
-        interleave_x("S", 1, 0, 128)
-        quantize_x(1, 0, 128)
-        ub[0] = first_product(0, "b4", 1, wu_tile)
-        interleave_x("S", 1, 128, 256)
-        interleave_wg("S", 0, 256, 512)
-        quantize_x(1, 128, 256)
-        quantize_wgh(1, 1, 2)
-        interleave_x("V", 1, 256, 512)
-        quantize_wgh(1, 1, 3)
-        ub[1] = first_product(1, "b5", 1, wu_tile)
-        quantize_wgh(1, 0, 3)
+        interleave_pair("S", 1, 0, 0, 512)
+        gather(1, 1, 512, J)
+        mx_tiles(0, 0, J, "x_scales_0")
+        quantize_x(0, 0, J)
+        gather(1, 2, 0, 512)
+        gather(1, 2, 512, J)
+        interleave_wg("S", 0, 0)
+        interleave_wg("S", 0, 1)
         quantize_wg(0, 0, R)
-        quantize_x(0, 512, 1024)
+        x_tile(1, 512, J, "wg_raw_0_1")
+        interleave_pair("S", 1, 0, 512, J)
+        up = {}
+        gate = {}
+        for c in range(4):
+            up[c] = bank(4 + c, PACK)
+            up_pass(up[c], c, 0)
+        for g in range(2):
+            for u in range(2):
+                gate[g, u] = bank(2 * g + u, 2)
+                gate_pass(gate[g, u], g, u, 0)
+        mx_tiles(1, 0, J, "x_scales_1")
+        gather(1, 3, 0, 256)
+        gather(1, 3, 256, 512)
+        interleave_wg("S", 1, 0)
+        interleave_wg("S", 1, 1)
+        interleave_pair("V", 1, 1, 0, 256)
+        interleave_pair("V", 1, 1, 256, 512)
+        quantize_x(1, 0, 256)
         quantize_x(1, 256, 512)
-        ub[2] = first_product(2, "b6", 1, wu_tile)
-        quantize_wgh(1, 0, 0)
-        quantize_wgh(1, 1, 0)
-        quantize_wgh(1, 1, 1)
-        gather2(1, 3, 768, 1024)
-        gather(1, 0, 512, 1024)
-        ga[0] = ga256(0, 0, 1, "b0")
-        tanh256(0, 0, ga[0])
-        ga[1] = ga256(0, 1, 1, "b1")
-        ga[2] = ga256(1, 0, 1, "b2")
-        gather(1, 2, 512, 1024)
-        ga[3] = ga256(1, 1, 1, "b3")
-        gather(1, 1, 512, 1024)
-        interleave_x("S", 1, 512, 768)
-        quantize_x(1, 512, 768)
-        ub[3] = first_product(3, "b7", 1, wu_tile)
-        ga[4] = ga256(2, 0, 1, "b0")
-        tanh256(0, 1, ga[1])
-        h_bf[0] = hidden2(0, ub[0])
-        interleave_x("V", 1, 768, 1024)
-        h_bf[1] = hidden2(1, ub[1])
-        quantize_h(0, h_bf[0])
-        tanh256(1, 0, ga[2])
-        tanh256(1, 1, ga[3])
-        quantize_h(1, h_bf[1])
-        ga[5] = ga256(2, 1, 1, "b1")
-        quantize_x(1, 768, 1024)
-        ga[6] = ga256(3, 0, 1, "b2")
-        tanh256(2, 0, ga[4])
-        h_bf[2] = hidden2(2, ub[2])
-        h_bf[3] = hidden2(3, ub[3])
-        ga[7] = ga256(3, 1, 1, "b3")
-        quantize_h(2, h_bf[2])
-        second2(0, "S", "b5", 1)
-        second2(1, "S", "b4", 1)
-        ub[4] = first_product(4, "b0", 1, wu_tile)
-        tanh256(2, 1, ga[5])
-        store(0, 128)
-        quantize_h(3, h_bf[3])
-        tanh256(3, 0, ga[6])
-        ub[5] = first_product(5, "b1", 1, wu_tile)
-        h_bf[4] = hidden2(4, ub[4])
-        second2(2, "S", "b2", 1)
-        quantize_h(4, h_bf[4])
-        ub[6] = first_product(6, "b5", 1, wu_tile)
-        second2(3, "S", "b4", 1)
-        h_bf[5] = hidden2(5, ub[5])
-        quantize_h(5, h_bf[5])
-        store(128, 384)
-        second2(4, "S", "b1", 1)
-        ub[7] = first_product(7, "b0", 1, wu_tile)
-        store(384, 640)
-        second2(5, "V", "b2", 1)
-        tanh256(3, 1, ga[7])
-        h_bf[6] = hidden2(6, ub[6])
-        quantize_h(6, h_bf[6])
-        h_bf[7] = hidden2(7, ub[7])
-        quantize_h(7, h_bf[7])
-        second2(6, "S", "b7", 1)
-        second_half(7, 0, "S", "b7", 1)
-        store(640, 896)
-        store_half(7, 0)
-        second_half(7, 1, "S", "b6", 1)
-        store_half(7, 1)
+        for c in range(4):
+            up_pass(up[c], c, 1)
+        quantize_wg(1, 0, 256)
+        quantize_wg(1, 256, 512)
+        for g in range(2):
+            for u in range(2):
+                gate_pass(gate[g, u], g, u, 1)
+                tanh(gate[g, u], g, u)
+        for g in range(2, 4):
+            gather(1, 3, g * QUARTER, (g + 1) * QUARTER)
+        for g in range(2, 4):
+            interleave_pair("V", 1, 1, g * QUARTER, (g + 1) * QUARTER)
+        for g in range(2, 4):
+            quantize_x(1, g * QUARTER, (g + 1) * QUARTER)
+
+
+        def gate_full(g, b0):
+            for u in range(2):
+                gate[g, u] = bank(b0 + u, 2)
+                for a in range(PASSES):
+                    gate_pass(gate[g, u], g, u, a)
+
+
+        def up_full(c0, b0):
+            for c in range(c0, c0 + 2):
+                up[c] = bank(b0 + c - c0, PACK)
+                for a in range(PASSES):
+                    up_pass(up[c], c, a)
+
+
+        def hidden_pair(g):
+            hidden(up[2 * g], 2 * g)
+            hidden(up[2 * g + 1], 2 * g + 1)
+            quantize_h(g * QUARTER, (g + 1) * QUARTER)
+
+
+        def down_pair(g, b0, engines):
+            for u in range(2):
+                down(b0 + u, engines[u], 2 * u, 2 * u + 2, g * QUARTER, (g + 1) * QUARTER)
+
+
+        hidden(up[0], 0)
+        hidden(up[1], 1)
+        quantize_h(0, 256)
+        gate_full(2, 0)
+        tanh(gate[2, 0], 2, 0)
+        tanh(gate[2, 1], 2, 1)
+        gate_full(3, 2)
+        down_pair(0, 0, "SS")
+        up_full(4, 4)
+        tanh(gate[3, 0], 3, 0)
+        tanh(gate[3, 1], 3, 1)
+        hidden_pair(1)
+        down_pair(1, 2, "SS")
+        up_full(6, 6)
+        hidden_pair(2)
+        down_pair(2, 4, "SS")
+        hidden(up[6], 6)
+        quantize_h(768, 896)
+        hidden(up[7], 7)
+        quantize_h(896, J)
+        down(0, "V", 0, 4, 768, 896)
+        down(1, "S", 0, 2, 896, J)
+        down(6, "V", 2, 4, 896, J)

@@ -37,15 +37,15 @@ def tile_list_tanh_none_kernel(
         picked_0 = keep.tile([P, PACK, J], F32, name="picked_0")
         picked_first = keep.tile([P, 2, J], F32, name="picked_first")
         picked_low = keep.tile([P, 2, J // 2], F32, name="picked_low")
-        shared = keep.tile([P, 3, J // 2], F32, name="shared", align_bytes=64)
+        shared = keep.tile([P, 2, J // 2], F32, name="shared", align_bytes=64)
         x_bf = {}
         x_mx = {}
-        wg_raw = [[keep.tile([P, PACK, R // 2], F32, name="wg_raw_%d_%d" % (a, h), align_bytes=64) for h in range(2)] for a in range(PASSES)]
-        wg_bf_0 = keep.tile([P, R, PACK], BF16, name="wg_bf_0", align_bytes=64)
-        wg_bf = [
-            wg_bf_0[:],
-            shared[:, 1:3, :].rearrange("p s j -> p (s j)").bitcast(BF16).rearrange("p (r i) -> p r i", i=PACK),
-        ]
+        wg_raw = [keep.tile([P, PACK, R], F32, name="wg_raw_%d" % a, align_bytes=64) for a in range(PASSES)]
+        wg_bf = {
+            (a, u): keep.tile([P, 2 * P * PACK], BF16, name="wg_bf_%d_%d" % (a, u), align_bytes=64)[:]
+            for a, u in ((0, 0), (0, 1), (1, 0))
+        }
+        wg_bf[1, 1] = shared[:, 1, :].bitcast(BF16)
         wg_codes = [keep.tile([P, R], U32, name="wg_codes_%d" % a, align_bytes=64) for a in range(PASSES)]
         wg_scales = [keep.tile([P, R], U8, name="wg_scales_%d" % a, align_bytes=64) for a in range(PASSES)]
         wu_raw = keep.tile([P, PASSES, 2 * R], U8, name="wu_raw", align_bytes=64)
@@ -67,8 +67,8 @@ def tile_list_tanh_none_kernel(
         def load_plane(a, i):
             nc.sync.dma_start(out=planes[a][i][:], in_=x_rows[a, :, i, :])
 
-        def load_wg(a, h):
-            nc.sync.dma_start(out=wg_raw[a][h][:], in_=wg_rows[a, :, :, h * R // 2 : (h + 1) * R // 2])
+        def load_wg(a):
+            nc.sync.dma_start(out=wg_raw[a][:], in_=wg_rows[a])
 
         def load_wgt(j0, j1):
             nc.sync.dma_start(out=wgt_sb[:, j0:j1], in_=wgt[:, j0:j1])
@@ -151,18 +151,19 @@ def tile_list_tanh_none_kernel(
                 in_=x_cols(a, j0, j1).rearrange("p j i -> p (j i)"),
             )
 
-        def interleave_wg(engine, a, h):
+        def interleave_wg(engine, a, u):
             copy_on(
                 engine,
-                wg_bf[a].rearrange("p (t m) i -> p m i t", t=PACK)[:, h * 64 : (h + 1) * 64, :, :],
-                wg_raw[a][h][:].rearrange("p i (m t) -> p m i t", t=PACK),
+                wg_bf[a, u].rearrange("p (t m i) -> p m i t", t=2, i=PACK),
+                wg_raw[a][:].rearrange("p i (m t) -> p m i t", t=PACK)[:, :, :, 2 * u : 2 * u + 2],
             )
 
-        def quantize_wg(a, c0, c1):
+        def quantize_wg(a, u):
+            c0, c1 = 2 * P * u, 2 * P * (u + 1)
             nc.vector.quantize_mx(
                 out=wg_codes[a][:, c0:c1].bitcast(FP8X4),
                 scales=wg_scales[a][:, c0:c1],
-                in_=wg_bf[a][:, c0:c1, :].rearrange("p c i -> p (c i)"),
+                in_=wg_bf[a, u],
             )
 
         def bank(b, slices):
@@ -258,11 +259,9 @@ def tile_list_tanh_none_kernel(
             load_plane(0, i)
         for i in range(PACK - 1):
             load_plane(1, i)
-        load_wg(0, 0)
-        load_wg(0, 1)
+        load_wg(0)
         load_plane(1, 3)
-        load_wg(1, 0)
-        load_wg(1, 1)
+        load_wg(1)
         load_wd()
         load_wd_scales()
         nc.scalar.activation(out=warm[:], in_=wgt_sb[:, 0:1], func=TANH)
@@ -288,8 +287,9 @@ def tile_list_tanh_none_kernel(
         gather(1, 2, 512, J)
         interleave_wg("S", 0, 0)
         interleave_wg("S", 0, 1)
-        quantize_wg(0, 0, R)
-        x_tile(1, 512, J, "wg_raw_0_1")
+        quantize_wg(0, 0)
+        quantize_wg(0, 1)
+        x_tile(1, 512, J, "wg_raw_0")
         interleave_pair("S", 1, 0, 512, J)
         up = {}
         gate = {}
@@ -303,7 +303,7 @@ def tile_list_tanh_none_kernel(
         mx_tiles(1, 0, J, "x_scales_1")
         gather(1, 3, 0, 256)
         gather(1, 3, 256, 512)
-        interleave_wg("S", 1, 0)
+        interleave_wg("V", 1, 0)
         interleave_wg("S", 1, 1)
         interleave_pair("V", 1, 1, 0, 256)
         interleave_pair("V", 1, 1, 256, 512)
@@ -311,8 +311,8 @@ def tile_list_tanh_none_kernel(
         quantize_x(1, 256, 512)
         for c in range(4):
             up_pass(up[c], c, 1)
-        quantize_wg(1, 0, 256)
-        quantize_wg(1, 256, 512)
+        quantize_wg(1, 0)
+        quantize_wg(1, 1)
         for g in range(2):
             for u in range(2):
                 gate_pass(gate[g, u], g, u, 1)
@@ -320,7 +320,7 @@ def tile_list_tanh_none_kernel(
         for g in range(2, 4):
             gather(1, 3, g * QUARTER, (g + 1) * QUARTER)
         for g in range(2, 4):
-            interleave_pair("V", 1, 1, g * QUARTER, (g + 1) * QUARTER)
+            interleave_pair("VVVV"[g], 1, 1, g * QUARTER, (g + 1) * QUARTER)
         for g in range(2, 4):
             quantize_x(1, g * QUARTER, (g + 1) * QUARTER)
 

@@ -35,19 +35,21 @@ def tile_list_tanh_none_kernel(
         wgt_sb = keep.tile([P, J], F32, name="wgt_sb")
         planes = [[keep.tile([P, T], F32, name="plane_%d_%d" % (a, i), align_bytes=64) for i in range(PACK)] for a in range(PASSES)]
         picked_0 = keep.tile([P, PACK, J], F32, name="picked_0")
-        picked_first = keep.tile([P, 2, J], F32, name="picked_first")
-        picked_low = keep.tile([P, 2, J // 2], F32, name="picked_low")
-        shared = keep.tile([P, 2, J // 2], F32, name="shared", align_bytes=64)
+        picked_1 = keep.tile([P, PACK, J], F32, name="picked_1", align_bytes=64)
+        picked = [picked_0, picked_1]
         x_bf = {}
         x_mx = {}
         wg_raw = [keep.tile([P, PACK, R], F32, name="wg_raw_%d" % a, align_bytes=64) for a in range(PASSES)]
         wg_bf = {
             (a, u): keep.tile([P, 2 * P * PACK], BF16, name="wg_bf_%d_%d" % (a, u), align_bytes=64)[:]
-            for a, u in ((0, 0), (0, 1), (1, 0))
+            for a, u in ((0, 0), (0, 1), (1, 1))
         }
-        wg_bf[1, 1] = shared[:, 1, :].bitcast(BF16)
+        wg_bf[1, 0] = picked_1[:, PACK - 1, J // 2 :].bitcast(BF16)
         wg_codes = [keep.tile([P, R], U32, name="wg_codes_%d" % a, align_bytes=64) for a in range(PASSES)]
-        wg_scales = [keep.tile([P, R], U8, name="wg_scales_%d" % a, align_bytes=64) for a in range(PASSES)]
+        wg_scales = {
+            (a, u): keep.tile([P, 2 * P], U8, name="wg_scales_%d_%d" % (a, u), align_bytes=64)
+            for a, u in ((0, 0), (1, 0), (1, 1))
+        }
         wu_raw = keep.tile([P, PASSES, 2 * R], U8, name="wu_raw", align_bytes=64)
         wu_codes = keep.tile([P, PASSES, 2 * R], U8, name="wu_codes", align_bytes=64)
         wu_sc_raw = keep.tile([P, PASSES, R], U8, name="wu_sc_raw", align_bytes=64)
@@ -93,18 +95,9 @@ def tile_list_tanh_none_kernel(
             else:
                 nc.vector.tensor_copy(out=dst, in_=src)
 
-        def picks(a, i0, i1, j0, j1):
-            if a == 0:
-                return picked_0[:, i0:i1, j0:j1]
-            if i1 <= 2:
-                return picked_first[:, i0:i1, j0:j1]
-            if j1 <= J // 2:
-                return picked_low[:, i0 - 2 : i1 - 2, j0:j1]
-            return shared[:, i0 - 2 : i1 - 2, j0 - J // 2 : j1 - J // 2]
-
         def gather(a, i, j0, j1):
             nc.vector.tensor_tensor(
-                out=picks(a, i, i + 1, j0, j1).rearrange("p i j -> p (i j)"),
+                out=picked[a][:, i, j0:j1],
                 in0=planes[a][i][:].indirect(offsets[:, j0 // 16 : j1 // 16]),
                 in1=wgt_sb[:, j0:j1],
                 op=MULT,
@@ -123,14 +116,14 @@ def tile_list_tanh_none_kernel(
             copy_on(
                 engine,
                 x_cols(a, j0, j1).rearrange("p (c e) i -> p c i e", e=4),
-                picks(a, 0, PACK, j0, j1).rearrange("p i (c e) -> p c i e", e=4),
+                picked[a][:, :, j0:j1].rearrange("p i (c e) -> p c i e", e=4),
             )
 
         def interleave_pair(engine, a, u, j0, j1):
             copy_on(
                 engine,
                 x_cols(a, j0, j1)[:, :, 2 * u : 2 * u + 2].rearrange("p (c e) i -> p c i e", e=4),
-                picks(a, 2 * u, 2 * u + 2, j0, j1).rearrange("p i (c e) -> p c i e", e=4),
+                picked[a][:, 2 * u : 2 * u + 2, j0:j1].rearrange("p i (c e) -> p c i e", e=4),
             )
 
         def mx_tiles(a, j0, j1, scale_tag):
@@ -162,7 +155,7 @@ def tile_list_tanh_none_kernel(
             c0, c1 = 2 * P * u, 2 * P * (u + 1)
             nc.vector.quantize_mx(
                 out=wg_codes[a][:, c0:c1].bitcast(FP8X4),
-                scales=wg_scales[a][:, c0:c1],
+                scales=wg_scales[a, u][:],
                 in_=wg_bf[a, u],
             )
 
@@ -189,7 +182,7 @@ def tile_list_tanh_none_kernel(
                 nc.tensor.matmul_mx(
                     out=acc[:, v, :],
                     lhsT=wg_codes[a][:, P * t : P * (t + 1)].bitcast(FP8X4),
-                    lhsT_scale=wg_scales[a][:, P * t : P * (t + 1)],
+                    lhsT_scale=wg_scales[a, u][:, P * v : P * (v + 1)],
                     rhs=codes,
                     rhs_scale=scales,
                     start=(a == 0 and v == 0),
@@ -257,8 +250,9 @@ def tile_list_tanh_none_kernel(
         load_wgt(256, J)
         for i in range(1, PACK):
             load_plane(0, i)
-        for i in range(PACK - 1):
-            load_plane(1, i)
+        load_plane(1, 0)
+        load_plane(1, 1)
+        load_plane(1, 2)
         load_wg(0)
         load_plane(1, 3)
         load_wg(1)
@@ -277,50 +271,51 @@ def tile_list_tanh_none_kernel(
             gather(0, 3, j0, j0 + 512)
             interleave_x("S", 0, j0, j0 + 512)
         gather(1, 0, 0, J)
-        x_tile(1, 0, 512, "x_bf_1")
-        gather(1, 1, 0, 512)
-        interleave_pair("S", 1, 0, 0, 512)
-        gather(1, 1, 512, J)
+        for j0 in range(0, J, 512):
+            gather(1, 1, j0, j0 + 512)
         mx_tiles(0, 0, J, "x_scales_0")
         quantize_x(0, 0, J)
-        gather(1, 2, 0, 512)
-        gather(1, 2, 512, J)
+        gather(1, 2, 0, J)
         interleave_wg("S", 0, 0)
         interleave_wg("S", 0, 1)
         quantize_wg(0, 0)
-        quantize_wg(0, 1)
-        x_tile(1, 512, J, "wg_raw_0")
-        interleave_pair("S", 1, 0, 512, J)
         up = {}
         gate = {}
         for c in range(4):
             up[c] = bank(4 + c, PACK)
             up_pass(up[c], c, 0)
         for g in range(2):
-            for u in range(2):
-                gate[g, u] = bank(2 * g + u, 2)
-                gate_pass(gate[g, u], g, u, 0)
+            gate[g, 0] = bank(2 * g, 2)
+            gate_pass(gate[g, 0], g, 0, 0)
         mx_tiles(1, 0, J, "x_scales_1")
         gather(1, 3, 0, 256)
         gather(1, 3, 256, 512)
+        x_tile(1, 0, 256, "x_bf_1_0")
+        x_tile(1, 256, 512, "x_bf_1_1")
+        interleave_x("S", 1, 0, 256)
+        interleave_x("S", 1, 256, 512)
         interleave_wg("V", 1, 0)
         interleave_wg("S", 1, 1)
-        interleave_pair("V", 1, 1, 0, 256)
-        interleave_pair("V", 1, 1, 256, 512)
         quantize_x(1, 0, 256)
         quantize_x(1, 256, 512)
+        wg_scales[0, 1] = keep.tile([P, 2 * P], U8, name="x_bf_1_0", tag="x_bf_1_0", align_bytes=64)
+        quantize_wg(0, 1)
+        for g in range(2):
+            gate[g, 1] = bank(2 * g + 1, 2)
+            gate_pass(gate[g, 1], g, 1, 0)
         for c in range(4):
             up_pass(up[c], c, 1)
         quantize_wg(1, 0)
         quantize_wg(1, 1)
+        x_tile(1, 512, J, "x_bf_1_2")
+        for g in range(2, 4):
+            gather(1, 3, g * QUARTER, (g + 1) * QUARTER)
         for g in range(2):
             for u in range(2):
                 gate_pass(gate[g, u], g, u, 1)
                 tanh(gate[g, u], g, u)
-        for g in range(2, 4):
-            gather(1, 3, g * QUARTER, (g + 1) * QUARTER)
-        for g in range(2, 4):
-            interleave_pair("VVVV"[g], 1, 1, g * QUARTER, (g + 1) * QUARTER)
+        interleave_x("V", 1, 512, 768)
+        interleave_x("V", 1, 768, J)
         for g in range(2, 4):
             quantize_x(1, g * QUARTER, (g + 1) * QUARTER)
 

@@ -35,8 +35,8 @@ def tile_list_tanh_none_kernel(
         wgt_sb = keep.tile([P, J], F32, name="wgt_sb")
         planes = [[keep.tile([P, T], F32, name="plane_%d_%d" % (a, i), align_bytes=64) for i in range(PACK)] for a in range(PASSES)]
         picked_0 = keep.tile([P, PACK, J], F32, name="picked_0")
-        picked_1 = keep.tile([P, PACK, J], F32, name="picked_1", align_bytes=64)
-        picked = [picked_0, picked_1]
+        picked_1 = keep.tile([P, PACK * J + QUARTER], F32, name="picked_1", align_bytes=64)
+        picked = [picked_0, picked_1[:, : PACK * J].rearrange("p (i j) -> p i j", i=PACK)]
         x_bf = {}
         x_mx = {}
         wg_raw = [keep.tile([P, PACK, R], F32, name="wg_raw_%d" % a, align_bytes=64) for a in range(PASSES)]
@@ -44,7 +44,7 @@ def tile_list_tanh_none_kernel(
             (a, u): keep.tile([P, 2 * P * PACK], BF16, name="wg_bf_%d_%d" % (a, u), align_bytes=64)[:]
             for a, u in ((0, 0), (0, 1), (1, 1))
         }
-        wg_bf[1, 0] = picked_1[:, PACK - 1, J // 2 :].bitcast(BF16)
+        wg_bf[1, 0] = picked_1[:, PACK * J - QUARTER :].bitcast(BF16)
         wg_codes = [keep.tile([P, R], U32, name="wg_codes_%d" % a, align_bytes=64) for a in range(PASSES)]
         wg_scales = {
             (a, u): keep.tile([P, 2 * P], U8, name="wg_scales_%d_%d" % (a, u), align_bytes=64)
@@ -288,15 +288,20 @@ def tile_list_tanh_none_kernel(
             gate[g, 0] = bank(2 * g, 2)
             gate_pass(gate[g, 0], g, 0, 0)
         mx_tiles(1, 0, J, "x_scales_1")
-        gather(1, 3, 0, 256)
+        gather(1, 3, 0, 128)
+        gather(1, 3, 128, 256)
         gather(1, 3, 256, 512)
-        x_tile(1, 0, 256, "x_bf_1_0")
+        gather(1, 3, 512, 768)
+        x_tile(1, 0, 128, "x_bf_1_0")
+        x_tile(1, 128, 256, "x_bf_1_4")
         x_tile(1, 256, 512, "x_bf_1_1")
-        interleave_x("S", 1, 0, 256)
+        interleave_x("S", 1, 0, 128)
+        interleave_x("S", 1, 128, 256)
         interleave_x("S", 1, 256, 512)
         interleave_wg("V", 1, 0)
         interleave_wg("S", 1, 1)
-        quantize_x(1, 0, 256)
+        quantize_x(1, 0, 128)
+        quantize_x(1, 128, 256)
         quantize_x(1, 256, 512)
         wg_scales[0, 1] = keep.tile([P, 2 * P], U8, name="x_bf_1_0", tag="x_bf_1_0", align_bytes=64)
         quantize_wg(0, 1)
@@ -307,14 +312,14 @@ def tile_list_tanh_none_kernel(
             up_pass(up[c], c, 1)
         quantize_wg(1, 0)
         quantize_wg(1, 1)
-        x_tile(1, 512, J, "x_bf_1_2")
-        for g in range(2, 4):
-            gather(1, 3, g * QUARTER, (g + 1) * QUARTER)
+        x_tile(1, 512, 768, "wg_raw_1")
+        interleave_x("S", 1, 512, 768)
+        gather(1, 3, 768, J)
+        x_tile(1, 768, J, "x_bf_1_3")
         for g in range(2):
             for u in range(2):
                 gate_pass(gate[g, u], g, u, 1)
                 tanh(gate[g, u], g, u)
-        interleave_x("V", 1, 512, 768)
         interleave_x("V", 1, 768, J)
         for g in range(2, 4):
             quantize_x(1, g * QUARTER, (g + 1) * QUARTER)
@@ -361,10 +366,5 @@ def tile_list_tanh_none_kernel(
         up_full(6, 6)
         hidden_pair(2)
         down_pair(2, 4, "SS")
-        hidden(up[6], 6)
-        quantize_h(768, 896)
-        hidden(up[7], 7)
-        quantize_h(896, J)
-        down(0, "V", 0, 4, 768, 896)
-        down(1, "S", 0, 2, 896, J)
-        down(6, "V", 2, 4, 896, J)
+        hidden_pair(3)
+        down_pair(3, 0, "SV")

@@ -1,6 +1,7 @@
 from contextlib import ExitStack
 
 import concourse.mybir as mybir
+from concourse.masks import make_identity
 
 K, R, N, T, J = 1024, 512, 512, 2048, 1024
 FLOPS = 2 * K * R * J * 2 + 2 * R * N * J
@@ -60,6 +61,9 @@ def tile_list_tanh_none_kernel(
         h_bf = keep.tile([P, J, PACK], BF16, name="h_bf", align_bytes=64)
         h_codes = keep.tile([P, J], U32, name="h_codes", align_bytes=64)
         h_scales = keep.tile([P, J], U8, name="h_scales", align_bytes=64)
+        wgt_rows = keep.tile([P, J // 2], F32, name="wgt_rows")
+        wgt_t = keep.tile([P, J], F32, name="wgt_t")
+        identity = keep.tile([P, P], F32, name="identity")
         warm = keep.tile([P, 1], F32, name="warm")
 
         x_rows = xT.rearrange("(a p i) t -> a p i t", p=P, i=PACK)
@@ -75,9 +79,29 @@ def tile_list_tanh_none_kernel(
         def load_wgt(j0, j1):
             nc.sync.dma_start(out=wgt_sb[:, j0:j1], in_=wgt[:, j0:j1])
 
+        def spread_wgt():
+            blocks = QUARTER // P
+            for k in range(2):
+                heads = psum.tile([P, blocks, P], F32, name="bank_%d" % k, tag="bank_%d" % k)
+                for b in range(blocks):
+                    j0 = k * QUARTER + b * P
+                    nc.tensor.transpose(out=heads[:, b, :], in_=wgt_rows[:, j0 : j0 + P], identity=identity[:])
+                for half in range(2):
+                    j0 = half * J // 2 + k * QUARTER
+                    nc.scalar.copy(
+                        out=wgt_t[:, j0 : j0 + QUARTER].rearrange("p (b h r) -> p b h r", h=8, r=16),
+                        in_=heads[:, :, 8 * half :: 16].unsqueeze(3).to_broadcast([P, blocks, 8, 16]),
+                    )
+            for g in range(J // QUARTER):
+                rows = psum.tile([P, blocks, P], F32, name="bank_%d" % (4 + g), tag="bank_%d" % (4 + g))
+                for b in range(blocks):
+                    j0 = g * QUARTER + b * P
+                    nc.tensor.transpose(out=rows[:, b, :], in_=wgt_t[:, j0 : j0 + P], identity=identity[:])
+                nc.scalar.copy(out=wgt_sb[:, g * QUARTER : (g + 1) * QUARTER], in_=rows[:].rearrange("p k j -> p (k j)"))
+
         def load_wu_scales():
             for q in range(4):
-                nc.sync.dma_start(
+                nc.scalar.dma_start(
                     out=wu_sc_raw[32 * q : 32 * q + 4, :, :].bitcast(I32),
                     in_=wu_scales[:, 4 * q : 4 * q + 4, :].rearrange("a s r -> s a r").bitcast(I32),
                 )
@@ -240,14 +264,16 @@ def tile_list_tanh_none_kernel(
         def load_wd():
             nc.sync.dma_start(out=wd_codes[:], in_=wd_words[0].rearrange("p n i -> p (n i)").bitcast(I32))
 
+        nc.vector.memset(wgt_rows[:], 0.0)
+        make_identity(nc, identity[:])
         nc.vector.memset(wu_sc_raw[:].rearrange("p a r -> p (a r)").bitcast(I32), 0)
         nc.vector.memset(wd_sc[:].bitcast(I32), 0)
         nc.sync.dma_start(offsets[:], offs)
         load_wu()
-        load_wgt(0, 256)
-        load_wu_scales()
+        for half in range(2):
+            nc.sync.dma_start(out=wgt_rows[8 * half :: 16, :], in_=wgt[::16, half * J // 2 : (half + 1) * J // 2])
         load_plane(0, 0)
-        load_wgt(256, J)
+        load_wu_scales()
         for i in range(1, PACK):
             load_plane(0, i)
         load_plane(1, 0)
@@ -258,12 +284,14 @@ def tile_list_tanh_none_kernel(
         load_wg(1)
         load_wd()
         load_wd_scales()
-        nc.scalar.activation(out=warm[:], in_=wgt_sb[:, 0:1], func=TANH)
+        nc.scalar.activation(out=warm[:], in_=identity[:, 0:1], func=TANH)
         permute_wu()
+        spread_wgt()
 
         gather(0, 0, 0, 256)
         gather(0, 0, 256, 512)
-        gather(0, 0, 512, J)
+        gather(0, 0, 512, 768)
+        gather(0, 0, 768, J)
         gather(0, 1, 0, J)
         gather(0, 2, 0, J)
         x_tile(0, 0, J, "x_bf_0")
@@ -366,5 +394,10 @@ def tile_list_tanh_none_kernel(
         up_full(6, 6)
         hidden_pair(2)
         down_pair(2, 4, "SS")
-        hidden_pair(3)
-        down_pair(3, 0, "SV")
+        hidden(up[6], 6)
+        quantize_h(768, 896)
+        hidden(up[7], 7)
+        quantize_h(896, J)
+        down(0, "V", 0, 4, 768, 896)
+        down(1, "S", 0, 2, 896, J)
+        down(6, "V", 2, 4, 896, J)

@@ -61,7 +61,7 @@ def tile_list_tanh_none_kernel(
         h_bf = keep.tile([P, J, PACK], BF16, name="h_bf", align_bytes=64)
         h_codes = keep.tile([P, J], U32, name="h_codes", align_bytes=64)
         h_scales = keep.tile([P, J], U8, name="h_scales", align_bytes=64)
-        wgt_rows = keep.tile([P, J // 2], F32, name="wgt_rows")
+        wgt_rows = keep.tile([P, P], F32, name="wgt_rows")
         wgt_t = keep.tile([P, J], F32, name="wgt_t")
         identity = keep.tile([P, P], F32, name="identity")
         warm = keep.tile([P, 1], F32, name="warm")
@@ -80,18 +80,17 @@ def tile_list_tanh_none_kernel(
             nc.sync.dma_start(out=wgt_sb[:, j0:j1], in_=wgt[:, j0:j1])
 
         def spread_wgt():
+            heads = psum.tile([P, P], F32, name="bank_0", tag="bank_0")
+            nc.tensor.transpose(out=heads[:], in_=wgt_rows[:], identity=identity[:])
             blocks = QUARTER // P
-            for k in range(2):
-                heads = psum.tile([P, blocks, P], F32, name="bank_%d" % k, tag="bank_%d" % k)
-                for b in range(blocks):
-                    j0 = k * QUARTER + b * P
-                    nc.tensor.transpose(out=heads[:, b, :], in_=wgt_rows[:, j0 : j0 + P], identity=identity[:])
-                for half in range(2):
-                    j0 = half * J // 2 + k * QUARTER
-                    nc.scalar.copy(
-                        out=wgt_t[:, j0 : j0 + QUARTER].rearrange("p (b h r) -> p b h r", h=8, r=16),
-                        in_=heads[:, :, 8 * half :: 16].unsqueeze(3).to_broadcast([P, blocks, 8, 16]),
-                    )
+            for g in range(J // QUARTER):
+                nc.scalar.copy(
+                    out=wgt_t[:, g * QUARTER : (g + 1) * QUARTER].rearrange("p (b q r) -> p b q r", q=16, r=8),
+                    in_=heads[:]
+                    .rearrange("p (q b) -> p b q", b=8)[:, g * blocks : (g + 1) * blocks, :]
+                    .unsqueeze(3)
+                    .to_broadcast([P, blocks, 16, 8]),
+                )
             for g in range(J // QUARTER):
                 rows = psum.tile([P, blocks, P], F32, name="bank_%d" % (4 + g), tag="bank_%d" % (4 + g))
                 for b in range(blocks):
@@ -101,7 +100,7 @@ def tile_list_tanh_none_kernel(
 
         def load_wu_scales():
             for q in range(4):
-                nc.scalar.dma_start(
+                nc.sync.dma_start(
                     out=wu_sc_raw[32 * q : 32 * q + 4, :, :].bitcast(I32),
                     in_=wu_scales[:, 4 * q : 4 * q + 4, :].rearrange("a s r -> s a r").bitcast(I32),
                 )
@@ -264,16 +263,14 @@ def tile_list_tanh_none_kernel(
         def load_wd():
             nc.sync.dma_start(out=wd_codes[:], in_=wd_words[0].rearrange("p n i -> p (n i)").bitcast(I32))
 
-        nc.vector.memset(wgt_rows[:], 0.0)
         make_identity(nc, identity[:])
         nc.vector.memset(wu_sc_raw[:].rearrange("p a r -> p (a r)").bitcast(I32), 0)
         nc.vector.memset(wd_sc[:].bitcast(I32), 0)
         nc.sync.dma_start(offsets[:], offs)
+        nc.sync.dma_start(out=wgt_rows[:], in_=wgt[::8, :].rearrange("q (b j) -> q b j", j=P))
         load_wu()
-        for half in range(2):
-            nc.sync.dma_start(out=wgt_rows[8 * half :: 16, :], in_=wgt[::16, half * J // 2 : (half + 1) * J // 2])
-        load_plane(0, 0)
         load_wu_scales()
+        load_plane(0, 0)
         for i in range(1, PACK):
             load_plane(0, i)
         load_plane(1, 0)

@@ -16,6 +16,7 @@ FP8X4 = mybir.dt.float8_e4m3fn_x4
 FP4X4 = mybir.dt.float4_e2m1fn_x4
 MULT = mybir.AluOpType.mult
 TANH = mybir.ActivationFunctionType.Tanh
+COPY = mybir.ActivationFunctionType.Copy
 
 P = 128
 PACK = 4
@@ -64,7 +65,6 @@ def tile_list_tanh_none_kernel(
         wgt_rows = keep.tile([P, P], F32, name="wgt_rows")
         wgt_t = keep.tile([P, J], F32, name="wgt_t")
         identity = keep.tile([P, P], F32, name="identity")
-        warm = keep.tile([P, 1], F32, name="warm")
 
         x_rows = xT.rearrange("(a p i) t -> a p i t", p=P, i=PACK)
         wg_rows = wg.rearrange("(a p i) r -> a p i r", p=P, i=PACK)
@@ -84,7 +84,8 @@ def tile_list_tanh_none_kernel(
             nc.tensor.transpose(out=heads[:], in_=wgt_rows[:], identity=identity[:])
             blocks = QUARTER // P
             for g in range(J // QUARTER):
-                nc.scalar.copy(
+                nc.scalar.activation(
+                    func=COPY,
                     out=wgt_t[:, g * QUARTER : (g + 1) * QUARTER].rearrange("p (b q r) -> p b q r", q=16, r=8),
                     in_=heads[:]
                     .rearrange("p (q b) -> p b q", b=8)[:, g * blocks : (g + 1) * blocks, :]
@@ -281,7 +282,6 @@ def tile_list_tanh_none_kernel(
         load_wg(1)
         load_wd()
         load_wd_scales()
-        nc.scalar.activation(out=warm[:], in_=identity[:, 0:1], func=TANH)
         permute_wu()
         spread_wgt()
 
@@ -376,25 +376,27 @@ def tile_list_tanh_none_kernel(
 
 
         hidden(up[0], 0)
+        quantize_h(0, 128)
+        down(4, "S", 0, 4, 0, 128)
         hidden(up[1], 1)
-        quantize_h(0, 256)
+        quantize_h(128, 256)
         gate_full(2, 0)
+        down(5, "S", 0, 4, 128, 256)
         tanh(gate[2, 0], 2, 0)
         tanh(gate[2, 1], 2, 1)
         gate_full(3, 2)
-        down_pair(0, 0, "SS")
-        up_full(4, 4)
+        up_full(4, 0)
+        hidden_pair(1)
+        down_pair(1, 4, "SS")
         tanh(gate[3, 0], 3, 0)
         tanh(gate[3, 1], 3, 1)
-        hidden_pair(1)
-        down_pair(1, 2, "SS")
         up_full(6, 6)
         hidden_pair(2)
-        down_pair(2, 4, "SS")
+        down_pair(2, 2, "SS")
         hidden(up[6], 6)
         quantize_h(768, 896)
         hidden(up[7], 7)
         quantize_h(896, J)
-        down(0, "V", 0, 4, 768, 896)
-        down(1, "S", 0, 2, 896, J)
-        down(6, "V", 2, 4, 896, J)
+        down(4, "V", 0, 4, 768, 896)
+        down(5, "S", 0, 2, 896, J)
+        down(0, "V", 2, 4, 896, J)

@@ -3,7 +3,7 @@ from contextlib import ExitStack
 import concourse.mybir as mybir
 from concourse.masks import make_identity
 
-K, R, N, T, J = 1024, 512, 512, 2048, 1024
+K, R, N, TOK, J = 1024, 512, 512, 2048, 1024
 FLOPS = 2 * K * R * J * 2 + 2 * R * N * J
 
 F32 = mybir.dt.float32
@@ -35,23 +35,28 @@ def tile_list_tanh_none_kernel(
 
         offsets = keep.tile([P, J // 16], U16, name="offsets")
         wgt_sb = keep.tile([P, J], F32, name="wgt_sb")
-        planes = [[keep.tile([P, T], F32, name="plane_%d_%d" % (a, i), align_bytes=64) for i in range(PACK)] for a in range(PASSES)]
+        planes = [[keep.tile([P, TOK], F32, name="plane_%d_%d" % (a, i), align_bytes=64) for i in range(PACK)] for a in range(PASSES)]
         picked_0 = keep.tile([P, PACK, J], F32, name="picked_0")
-        picked_1 = keep.tile([P, PACK * J + QUARTER], F32, name="picked_1", align_bytes=64)
-        picked = [picked_0, picked_1[:, : PACK * J].rearrange("p (i j) -> p i j", i=PACK)]
+        half_a = keep.tile([P, PACK, 512], F32, name="picked_1a", align_bytes=64)
+        quart = [keep.tile([P, PACK * 256], F32, name="picked_1%s" % n, align_bytes=64) for n in "cd"]
+
+        def picked(a, i0, i1, j0, j1):
+            if a == 0:
+                return picked_0[:, i0:i1, j0:j1]
+            if j1 <= 512:
+                return half_a[:, i0:i1, j0:j1]
+            q = j0 // 256 - 2
+            return quart[q][:].rearrange("p (i j) -> p i j", i=PACK)[:, i0:i1, j0 % 256 : j0 % 256 + j1 - j0]
+
+        def spare(at, words):
+            return quart[at // 512][:, 512 + at % 512 : 512 + at % 512 + words].bitcast(BF16)
+
         x_bf = {}
         x_mx = {}
         wg_raw = [keep.tile([P, PACK, R], F32, name="wg_raw_%d" % a, align_bytes=64) for a in range(PASSES)]
-        wg_bf = {
-            (a, u): keep.tile([P, 2 * P * PACK], BF16, name="wg_bf_%d_%d" % (a, u), align_bytes=64)[:]
-            for a, u in ((0, 0), (0, 1), (1, 1))
-        }
-        wg_bf[1, 0] = picked_1[:, PACK * J - QUARTER :].bitcast(BF16)
+        wg_bf = {}
         wg_codes = [keep.tile([P, R], U32, name="wg_codes_%d" % a, align_bytes=64) for a in range(PASSES)]
-        wg_scales = {
-            (a, u): keep.tile([P, 2 * P], U8, name="wg_scales_%d_%d" % (a, u), align_bytes=64)
-            for a, u in ((0, 0), (1, 0), (1, 1))
-        }
+        wg_scales = {}
         wu_raw = keep.tile([P, PASSES, 2 * R], U8, name="wu_raw", align_bytes=64)
         wu_codes = keep.tile([P, PASSES, 2 * R], U8, name="wu_codes", align_bytes=64)
         wu_sc_raw = keep.tile([P, PASSES, R], U8, name="wu_sc_raw", align_bytes=64)
@@ -121,14 +126,17 @@ def tile_list_tanh_none_kernel(
 
         def gather(a, i, j0, j1):
             nc.vector.tensor_tensor(
-                out=picked[a][:, i, j0:j1],
+                out=picked(a, i, i + 1, j0, j1)[:, 0, :],
                 in0=planes[a][i][:].indirect(offsets[:, j0 // 16 : j1 // 16]),
                 in1=wgt_sb[:, j0:j1],
                 op=MULT,
             )
 
         def x_tile(a, j0, j1, tag):
-            tile = keep.tile([P, j1 - j0, PACK], BF16, name=tag, tag=tag, align_bytes=64)
+            if isinstance(tag, int):
+                tile = spare(tag, 2 * (j1 - j0)).rearrange("p (j i) -> p j i", i=PACK)
+            else:
+                tile = keep.tile([P, j1 - j0, PACK], BF16, name=tag, tag=tag, align_bytes=64)
             for j in range(j0, j1, CH):
                 x_bf[a, j] = (tile, j0)
 
@@ -140,14 +148,14 @@ def tile_list_tanh_none_kernel(
             copy_on(
                 engine,
                 x_cols(a, j0, j1).rearrange("p (c e) i -> p c i e", e=4),
-                picked[a][:, :, j0:j1].rearrange("p i (c e) -> p c i e", e=4),
+                picked(a, 0, PACK, j0, j1).rearrange("p i (c e) -> p c i e", e=4),
             )
 
         def interleave_pair(engine, a, u, j0, j1):
             copy_on(
                 engine,
                 x_cols(a, j0, j1)[:, :, 2 * u : 2 * u + 2].rearrange("p (c e) i -> p c i e", e=4),
-                picked[a][:, 2 * u : 2 * u + 2, j0:j1].rearrange("p i (c e) -> p c i e", e=4),
+                picked(a, 2 * u, 2 * u + 2, j0, j1).rearrange("p i (c e) -> p c i e", e=4),
             )
 
         def mx_tiles(a, j0, j1, scale_tag):
@@ -168,14 +176,21 @@ def tile_list_tanh_none_kernel(
                 in_=x_cols(a, j0, j1).rearrange("p j i -> p (j i)"),
             )
 
-        def interleave_wg(engine, a, u):
+        def interleave_wg(engine, a, u, tag=None):
+            if isinstance(tag, int):
+                wg_bf[a, u] = spare(tag, 512)
+            else:
+                tag = tag or "wg_bf_%d_%d" % (a, u)
+                wg_bf[a, u] = keep.tile([P, 2 * P * PACK], BF16, name=tag, tag=tag, align_bytes=64)[:]
             copy_on(
                 engine,
                 wg_bf[a, u].rearrange("p (t m i) -> p m i t", t=2, i=PACK),
                 wg_raw[a][:].rearrange("p i (m t) -> p m i t", t=PACK)[:, :, :, 2 * u : 2 * u + 2],
             )
 
-        def quantize_wg(a, u):
+        def quantize_wg(a, u, tag=None):
+            tag = tag or "wg_scales_%d_%d" % (a, u)
+            wg_scales[a, u] = keep.tile([P, 2 * P], U8, name=tag, tag=tag, align_bytes=64)
             c0, c1 = 2 * P * u, 2 * P * (u + 1)
             nc.vector.quantize_mx(
                 out=wg_codes[a][:, c0:c1].bitcast(FP8X4),
@@ -264,139 +279,198 @@ def tile_list_tanh_none_kernel(
         def load_wd():
             nc.sync.dma_start(out=wd_codes[:], in_=wd_words[0].rearrange("p n i -> p (n i)").bitcast(I32))
 
-        make_identity(nc, identity[:])
-        nc.vector.memset(wu_sc_raw[:].rearrange("p a r -> p (a r)").bitcast(I32), 0)
-        nc.vector.memset(wd_sc[:].bitcast(I32), 0)
-        nc.sync.dma_start(offsets[:], offs)
-        nc.sync.dma_start(out=wgt_rows[:], in_=wgt[::8, :].rearrange("q (b j) -> q b j", j=P))
-        load_wu()
-        load_wu_scales()
-        load_plane(0, 0)
-        for i in range(1, PACK):
+        def QX(j0, j1, tag=None):
+            mx_tiles(1, j0, j1, tag or "x_scales_1_%d" % j0)
+            quantize_x(1, j0, j1)
+
+        up = {}
+        gate = {}
+
+        def up_early(c, b):
+            up[c] = bank(b, PACK)
+            up_pass(up[c], c, 0)
+
+        def gate_early(g, u, b):
+            gate[g, u] = bank(b, 2)
+            gate_pass(gate[g, u], g, u, 0)
+
+        def gate_late(g, u):
+            gate_pass(gate[g, u], g, u, 1)
+
+        def gate_full(g, u, b):
+            gate_early(g, u, b)
+            gate_late(g, u)
+
+        def up_late(c):
+            up_pass(up[c], c, 1)
+
+        def up_full(c, b):
+            up_early(c, b)
+            up_late(c)
+
+        def T(g, u):
+            tanh(gate[g, u], g, u)
+
+        def H(c):
+            hidden(up[c], c)
+
+        def IX(engine, j0, j1, tag=None):
+            x_tile(1, j0, j1, "x_bf_1_%d" % j0 if tag is None else tag)
+            interleave_x(engine, 1, j0, j1)
+
+        def IP0(engine, j0, j1, tag=None):
+            x_tile(1, j0, j1, "x_bf_1_%d" % j0 if tag is None else tag)
+            interleave_pair(engine, 1, 0, j0, j1)
+
+        def IP1(engine, j0, j1):
+            interleave_pair(engine, 1, 1, j0, j1)
+
+        def head():
+            make_identity(nc, identity[:])
+            nc.vector.memset(wu_sc_raw[:].rearrange("p a r -> p (a r)").bitcast(I32), 0)
+            nc.vector.memset(wd_sc[:].bitcast(I32), 0)
+            nc.sync.dma_start(offsets[:], offs)
+            nc.sync.dma_start(out=wgt_rows[:], in_=wgt[::8, :].rearrange("q (b j) -> q b j", j=P))
+            load_wu()
+            load_wu_scales()
+
+        ys = {}
+
+        def down_mm(b, q0, q1, j0, j1):
+            acc = psum.tile([P, q1 - q0, j1 - j0], F32, name="bank_%d" % b, tag="bank_%d" % b)
+            ys[q0, j0] = (acc, q1, j1)
+            for q in range(q0, q1):
+                nc.tensor.matmul_mx(
+                    out=acc[:, q - q0, :],
+                    lhsT=wd_codes[:, P * q : P * (q + 1)].bitcast(FP8X4),
+                    lhsT_scale=wd_sc[:, P * q : P * (q + 1)],
+                    rhs=h_codes[:, j0:j1].bitcast(FP8X4),
+                    rhs_scale=h_scales[:, j0:j1],
+                    start=True,
+                    stop=True,
+                )
+
+        def store(engine, q0, j0):
+            acc, q1, j1 = ys[q0, j0]
+            y = keep.tile([P, q1 - q0, j1 - j0], F32, name="y_%d_%d" % (q0, j0))
+            copy_on(engine, y[:], acc[:])
+            nc.sync.dma_start(out=out_rows[:, q0:q1, j0:j1], in_=y[:])
+
+        head()
+        for i in range(4):
             load_plane(0, i)
         load_plane(1, 0)
         load_plane(1, 1)
-        load_plane(1, 2)
         load_wg(0)
+        load_plane(1, 2)
         load_plane(1, 3)
         load_wg(1)
         load_wd()
         load_wd_scales()
         permute_wu()
         spread_wgt()
-
-        gather(0, 0, 0, 256)
-        gather(0, 0, 256, 512)
-        gather(0, 0, 512, 768)
-        gather(0, 0, 768, J)
+        for j0 in range(0, J, 256):
+            gather(0, 0, j0, j0 + 256)
         gather(0, 1, 0, J)
         gather(0, 2, 0, J)
         x_tile(0, 0, J, "x_bf_0")
         for j0 in range(0, J, 512):
             gather(0, 3, j0, j0 + 512)
             interleave_x("S", 0, j0, j0 + 512)
-        gather(1, 0, 0, J)
-        for j0 in range(0, J, 512):
-            gather(1, 1, j0, j0 + 512)
+        for i in range(2):
+            for j0, j1 in ((0, 512), (512, 768), (768, J)):
+                gather(1, i, j0, j1)
         mx_tiles(0, 0, J, "x_scales_0")
+        mx_tiles(1, 0, 256, "x_scales_1_0")
         quantize_x(0, 0, J)
-        gather(1, 2, 0, J)
+
         interleave_wg("S", 0, 0)
         interleave_wg("S", 0, 1)
         quantize_wg(0, 0)
-        up = {}
-        gate = {}
-        for c in range(4):
-            up[c] = bank(4 + c, PACK)
-            up_pass(up[c], c, 0)
-        for g in range(2):
-            gate[g, 0] = bank(2 * g, 2)
-            gate_pass(gate[g, 0], g, 0, 0)
-        mx_tiles(1, 0, J, "x_scales_1")
+        quantize_wg(0, 1)
+        gather(1, 2, 0, 512)
+        gather(1, 2, 512, 768)
+        up_early(0, 4)
+        up_early(1, 5)
+        up_early(2, 6)
+        up_early(3, 7)
+        gate_early(0, 0, 0)
+        gate_early(0, 1, 1)
+        gate_early(1, 0, 2)
+        gate_early(1, 1, 3)
         gather(1, 3, 0, 128)
         gather(1, 3, 128, 256)
         gather(1, 3, 256, 512)
         gather(1, 3, 512, 768)
-        x_tile(1, 0, 128, "x_bf_1_0")
-        x_tile(1, 128, 256, "x_bf_1_4")
-        x_tile(1, 256, 512, "x_bf_1_1")
-        interleave_x("S", 1, 0, 128)
-        interleave_x("S", 1, 128, 256)
-        interleave_x("S", 1, 256, 512)
-        interleave_wg("V", 1, 0)
-        interleave_wg("S", 1, 1)
+        IX("S", 0, 128)
+        IX("S", 128, 256)
+        IX("S", 256, 512)
+        IX("S", 512, 768)
         quantize_x(1, 0, 128)
         quantize_x(1, 128, 256)
-        quantize_x(1, 256, 512)
-        wg_scales[0, 1] = keep.tile([P, 2 * P], U8, name="x_bf_1_0", tag="x_bf_1_0", align_bytes=64)
-        quantize_wg(0, 1)
-        for g in range(2):
-            gate[g, 1] = bank(2 * g + 1, 2)
-            gate_pass(gate[g, 1], g, 1, 0)
-        for c in range(4):
-            up_pass(up[c], c, 1)
+        interleave_wg("V", 1, 0)
+        interleave_wg("V", 1, 1, 512)
         quantize_wg(1, 0)
+        QX(256, 512)
         quantize_wg(1, 1)
-        x_tile(1, 512, 768, "wg_raw_1")
-        interleave_x("S", 1, 512, 768)
+        QX(512, 768)
+        gate_late(0, 0)
+        gate_late(0, 1)
+        up_late(0)
+        up_late(1)
+        gate_late(1, 0)
+        gate_late(1, 1)
+        up_late(2)
+        up_late(3)
+        gather(1, 2, 768, J)
         gather(1, 3, 768, J)
-        x_tile(1, 768, J, "x_bf_1_3")
-        for g in range(2):
-            for u in range(2):
-                gate_pass(gate[g, u], g, u, 1)
-                tanh(gate[g, u], g, u)
-        interleave_x("V", 1, 768, J)
-        for g in range(2, 4):
-            quantize_x(1, g * QUARTER, (g + 1) * QUARTER)
-
-
-        def gate_full(g, b0):
-            for u in range(2):
-                gate[g, u] = bank(b0 + u, 2)
-                for a in range(PASSES):
-                    gate_pass(gate[g, u], g, u, a)
-
-
-        def up_full(c0, b0):
-            for c in range(c0, c0 + 2):
-                up[c] = bank(b0 + c - c0, PACK)
-                for a in range(PASSES):
-                    up_pass(up[c], c, a)
-
-
-        def hidden_pair(g):
-            hidden(up[2 * g], 2 * g)
-            hidden(up[2 * g + 1], 2 * g + 1)
-            quantize_h(g * QUARTER, (g + 1) * QUARTER)
-
-
-        def down_pair(g, b0, engines):
-            for u in range(2):
-                down(b0 + u, engines[u], 2 * u, 2 * u + 2, g * QUARTER, (g + 1) * QUARTER)
-
-
-        hidden(up[0], 0)
+        T(0, 0)
+        T(0, 1)
+        T(1, 0)
+        T(1, 1)
+        IX("S", 768, J)
+        gate_full(2, 0, 0)
+        gate_full(2, 1, 1)
+        H(0)
+        H(1)
         quantize_h(0, 128)
-        down(4, "S", 0, 4, 0, 128)
-        hidden(up[1], 1)
+        H(2)
         quantize_h(128, 256)
-        gate_full(2, 0)
-        down(5, "S", 0, 4, 128, 256)
-        tanh(gate[2, 0], 2, 0)
-        tanh(gate[2, 1], 2, 1)
-        gate_full(3, 2)
-        up_full(4, 0)
-        hidden_pair(1)
-        down_pair(1, 4, "SS")
-        tanh(gate[3, 0], 3, 0)
-        tanh(gate[3, 1], 3, 1)
-        up_full(6, 6)
-        hidden_pair(2)
-        down_pair(2, 2, "SS")
-        hidden(up[6], 6)
+        QX(768, J)
+        down_mm(4, 0, 4, 0, 128)
+        down_mm(5, 0, 4, 128, 256)
+        up_full(4, 2)
+        up_full(5, 3)
+        T(2, 0)
+        T(2, 1)
+        H(3)
+        store("V", 0, 0)
+        quantize_h(256, 512)
+        gate_full(3, 0, 0)
+        gate_full(3, 1, 1)
+        store("S", 0, 128)
+        down_mm(6, 0, 2, 256, 512)
+        down_mm(7, 2, 4, 256, 512)
+        up_full(6, 4)
+        up_full(7, 5)
+        T(3, 0)
+        T(3, 1)
+        H(4)
+        H(5)
+        store("S", 0, 256)
+        store("S", 2, 256)
+        H(6)
+        quantize_h(512, 768)
+        down_mm(2, 0, 2, 512, 768)
+        down_mm(3, 2, 4, 512, 768)
+        H(7)
+        store("S", 0, 512)
+        store("S", 2, 512)
         quantize_h(768, 896)
-        hidden(up[7], 7)
         quantize_h(896, J)
-        down(4, "V", 0, 4, 768, 896)
-        down(5, "S", 0, 2, 896, J)
-        down(0, "V", 2, 4, 896, J)
+        down_mm(0, 0, 4, 768, 896)
+        down_mm(1, 0, 2, 896, J)
+        down_mm(6, 2, 4, 896, J)
+        store("V", 0, 768)
+        store("S", 0, 896)
+        store("V", 2, 896)

@@ -38,7 +38,7 @@ def tile_list_tanh_none_kernel(
         planes = [[keep.tile([P, TOK], F32, name="plane_%d_%d" % (a, i), align_bytes=64) for i in range(PACK)] for a in range(PASSES)]
         picked_0 = keep.tile([P, PACK, J], F32, name="picked_0")
         half_a = keep.tile([P, PACK, 512], F32, name="picked_1a", align_bytes=64)
-        quart = [keep.tile([P, PACK * 256], F32, name="picked_1%s" % n, align_bytes=64) for n in "cd"]
+        quart = [keep.tile([P, PACK * 256 + 256], F32, name="picked_1%s" % n, align_bytes=64) for n in "cd"]
 
         def picked(a, i0, i1, j0, j1):
             if a == 0:
@@ -46,10 +46,10 @@ def tile_list_tanh_none_kernel(
             if j1 <= 512:
                 return half_a[:, i0:i1, j0:j1]
             q = j0 // 256 - 2
-            return quart[q][:].rearrange("p (i j) -> p i j", i=PACK)[:, i0:i1, j0 % 256 : j0 % 256 + j1 - j0]
+            return quart[q][:, : PACK * 256].rearrange("p (i j) -> p i j", i=PACK)[:, i0:i1, j0 % 256 : j0 % 256 + j1 - j0]
 
         def spare(at, words):
-            return quart[at // 512][:, 512 + at % 512 : 512 + at % 512 + words].bitcast(BF16)
+            return quart[at // 1280][:, at % 1280 : at % 1280 + words].bitcast(BF16)
 
         x_bf = {}
         x_mx = {}
@@ -322,6 +322,12 @@ def tile_list_tanh_none_kernel(
             x_tile(1, j0, j1, "x_bf_1_%d" % j0 if tag is None else tag)
             interleave_pair(engine, 1, 0, j0, j1)
 
+        def XT(j0, j1, tag):
+            x_tile(1, j0, j1, tag)
+
+        def IPE(engine, j0, j1):
+            interleave_pair(engine, 1, 0, j0, j1)
+
         def IP1(engine, j0, j1):
             interleave_pair(engine, 1, 1, j0, j1)
 
@@ -409,7 +415,7 @@ def tile_list_tanh_none_kernel(
         quantize_x(1, 0, 128)
         quantize_x(1, 128, 256)
         interleave_wg("V", 1, 0)
-        interleave_wg("V", 1, 1, 512)
+        interleave_wg("V", 1, 1, 1792)
         quantize_wg(1, 0)
         QX(256, 512)
         quantize_wg(1, 1)
@@ -468,9 +474,7 @@ def tile_list_tanh_none_kernel(
         store("S", 2, 512)
         quantize_h(768, 896)
         quantize_h(896, J)
-        down_mm(0, 0, 4, 768, 896)
-        down_mm(1, 0, 2, 896, J)
-        down_mm(6, 2, 4, 896, J)
+        down_mm(0, 0, 2, 768, J)
+        down_mm(1, 2, 4, 768, J)
         store("V", 0, 768)
-        store("S", 0, 896)
-        store("V", 2, 896)
+        store("S", 2, 768)

@@ -474,7 +474,7 @@ def tile_list_tanh_none_kernel(
         store("S", 2, 512)
         quantize_h(768, 896)
         quantize_h(896, J)
-        down_mm(0, 0, 2, 768, J)
-        down_mm(1, 2, 4, 768, J)
-        store("V", 0, 768)
-        store("S", 2, 768)
+        for q, b in enumerate((0, 1, 6, 7)):
+            down_mm(b, q, q + 1, 768, J)
+        for q in range(4):
+            store("VS"[q % 2], q, 768)

@@ -415,11 +415,11 @@ def tile_list_tanh_none_kernel(
         quantize_x(1, 0, 128)
         quantize_x(1, 128, 256)
         interleave_wg("V", 1, 0)
-        interleave_wg("V", 1, 1, 1792)
-        quantize_wg(1, 0)
         QX(256, 512)
-        quantize_wg(1, 1)
+        quantize_wg(1, 0)
+        interleave_wg("V", 1, 1, 1792)
         QX(512, 768)
+        quantize_wg(1, 1)
         gate_late(0, 0)
         gate_late(0, 1)
         up_late(0)
@@ -467,14 +467,14 @@ def tile_list_tanh_none_kernel(
         store("S", 2, 256)
         H(6)
         quantize_h(512, 768)
-        down_mm(2, 0, 2, 512, 768)
-        down_mm(3, 2, 4, 512, 768)
+        for q, b in enumerate((2, 3, 0, 1)):
+            down_mm(b, q, q + 1, 512, 768)
         H(7)
-        store("S", 0, 512)
-        store("S", 2, 512)
+        for q in range(4):
+            store("SSSS"[q], q, 512)
         quantize_h(768, 896)
         quantize_h(896, J)
-        for q, b in enumerate((0, 1, 6, 7)):
+        for q, b in enumerate((6, 7, 4, 5)):
             down_mm(b, q, q + 1, 768, J)
         for q in range(4):
-            store("VS"[q % 2], q, 768)
+            store("VSVS"[q], q, 768)

@@ -15,6 +15,7 @@ U8 = mybir.dt.uint8
 FP8X4 = mybir.dt.float8_e4m3fn_x4
 FP4X4 = mybir.dt.float4_e2m1fn_x4
 MULT = mybir.AluOpType.mult
+ADD = mybir.AluOpType.add
 TANH = mybir.ActivationFunctionType.Tanh
 COPY = mybir.ActivationFunctionType.Copy
 
@@ -37,13 +38,13 @@ def tile_list_tanh_none_kernel(
         wgt_sb = keep.tile([P, J], F32, name="wgt_sb")
         planes = [[keep.tile([P, TOK], F32, name="plane_%d_%d" % (a, i), align_bytes=64) for i in range(PACK)] for a in range(PASSES)]
         picked_0 = keep.tile([P, PACK, J], F32, name="picked_0")
-        half_a = keep.tile([P, PACK, 512], F32, name="picked_1a", align_bytes=64)
-        quart = [keep.tile([P, PACK * 256 + 256], F32, name="picked_1%s" % n, align_bytes=64) for n in "cd"]
+        half_a = keep.tile([P, PACK, 768], F32, name="picked_1a", align_bytes=64)
+        quart = [None, keep.tile([P, 512 + PACK * R], F32, name="picked_1d", align_bytes=64)]
 
         def picked(a, i0, i1, j0, j1):
             if a == 0:
                 return picked_0[:, i0:i1, j0:j1]
-            if j1 <= 512:
+            if j1 <= 768:
                 return half_a[:, i0:i1, j0:j1]
             q = j0 // 256 - 2
             return quart[q][:, : PACK * 256].rearrange("p (i j) -> p i j", i=PACK)[:, i0:i1, j0 % 256 : j0 % 256 + j1 - j0]
@@ -53,7 +54,10 @@ def tile_list_tanh_none_kernel(
 
         x_bf = {}
         x_mx = {}
-        wg_raw = [keep.tile([P, PACK, R], F32, name="wg_raw_%d" % a, align_bytes=64) for a in range(PASSES)]
+        wg_raw = [
+            keep.tile([P, PACK, R], F32, name="wg_raw_0", align_bytes=64)[:],
+            quart[1][:, 512:].rearrange("p (i r) -> p i r", i=PACK),
+        ]
         wg_bf = {}
         wg_codes = [keep.tile([P, R], U32, name="wg_codes_%d" % a, align_bytes=64) for a in range(PASSES)]
         wg_scales = {}
@@ -79,7 +83,7 @@ def tile_list_tanh_none_kernel(
             nc.sync.dma_start(out=planes[a][i][:], in_=x_rows[a, :, i, :])
 
         def load_wg(a):
-            nc.sync.dma_start(out=wg_raw[a][:], in_=wg_rows[a])
+            nc.sync.dma_start(out=wg_raw[a], in_=wg_rows[a])
 
         def load_wgt(j0, j1):
             nc.sync.dma_start(out=wgt_sb[:, j0:j1], in_=wgt[:, j0:j1])
@@ -145,6 +149,16 @@ def tile_list_tanh_none_kernel(
             return tile[:, j0 - first : j1 - first, :]
 
         def interleave_x(engine, a, j0, j1):
+            if engine == "G":
+                nc.gpsimd.tensor_scalar(
+                    out=x_cols(a, j0, j1),
+                    in0=picked(a, 0, PACK, j0, j1).rearrange("p i j -> p j i"),
+                    scalar1=1.0,
+                    scalar2=0.0,
+                    op0=MULT,
+                    op1=ADD,
+                )
+                return
             copy_on(
                 engine,
                 x_cols(a, j0, j1).rearrange("p (c e) i -> p c i e", e=4),
@@ -185,7 +199,7 @@ def tile_list_tanh_none_kernel(
             copy_on(
                 engine,
                 wg_bf[a, u].rearrange("p (t m i) -> p m i t", t=2, i=PACK),
-                wg_raw[a][:].rearrange("p i (m t) -> p m i t", t=PACK)[:, :, :, 2 * u : 2 * u + 2],
+                wg_raw[a].rearrange("p i (m t) -> p m i t", t=PACK)[:, :, :, 2 * u : 2 * u + 2],
             )
 
         def quantize_wg(a, u, tag=None):
@@ -375,8 +389,8 @@ def tile_list_tanh_none_kernel(
         load_wd_scales()
         permute_wu()
         spread_wgt()
-        for j0 in range(0, J, 256):
-            gather(0, 0, j0, j0 + 256)
+        for j0, j1 in ((0, 256), (256, 512), (512, J)):
+            gather(0, 0, j0, j1)
         gather(0, 1, 0, J)
         gather(0, 2, 0, J)
         x_tile(0, 0, J, "x_bf_0")
@@ -384,7 +398,7 @@ def tile_list_tanh_none_kernel(
             gather(0, 3, j0, j0 + 512)
             interleave_x("S", 0, j0, j0 + 512)
         for i in range(2):
-            for j0, j1 in ((0, 512), (512, 768), (768, J)):
+            for j0, j1 in ((0, 768), (768, J)):
                 gather(1, i, j0, j1)
         mx_tiles(0, 0, J, "x_scales_0")
         mx_tiles(1, 0, 256, "x_scales_1_0")
@@ -394,8 +408,7 @@ def tile_list_tanh_none_kernel(
         interleave_wg("S", 0, 1)
         quantize_wg(0, 0)
         quantize_wg(0, 1)
-        gather(1, 2, 0, 512)
-        gather(1, 2, 512, 768)
+        gather(1, 2, 0, 768)
         up_early(0, 4)
         up_early(1, 5)
         up_early(2, 6)
@@ -417,7 +430,7 @@ def tile_list_tanh_none_kernel(
         interleave_wg("V", 1, 0)
         QX(256, 512)
         quantize_wg(1, 0)
-        interleave_wg("V", 1, 1, 1792)
+        interleave_wg("V", 1, 1)
         QX(512, 768)
         quantize_wg(1, 1)
         gate_late(0, 0)
@@ -429,12 +442,15 @@ def tile_list_tanh_none_kernel(
         up_late(2)
         up_late(3)
         gather(1, 2, 768, J)
-        gather(1, 3, 768, J)
+        gather(1, 3, 768, 896)
+        gather(1, 3, 896, J)
         T(0, 0)
         T(0, 1)
         T(1, 0)
         T(1, 1)
-        IX("S", 768, J)
+        x_tile(1, 768, J, "x_bf_1_768")
+        interleave_x("V", 1, 768, 896)
+        interleave_x("S", 1, 896, J)
         gate_full(2, 0, 0)
         gate_full(2, 1, 1)
         H(0)
@@ -450,7 +466,7 @@ def tile_list_tanh_none_kernel(
         T(2, 0)
         T(2, 1)
         H(3)
-        store("V", 0, 0)
+        store("S", 0, 0)
         quantize_h(256, 512)
         gate_full(3, 0, 0)
         gate_full(3, 1, 1)
@@ -467,14 +483,14 @@ def tile_list_tanh_none_kernel(
         store("S", 2, 256)
         H(6)
         quantize_h(512, 768)
-        for q, b in enumerate((2, 3, 0, 1)):
-            down_mm(b, q, q + 1, 512, 768)
+        down_mm(2, 0, 2, 512, 768)
+        down_mm(3, 2, 4, 512, 768)
         H(7)
-        for q in range(4):
-            store("SSSS"[q], q, 512)
+        store("S", 0, 512)
+        store("S", 2, 512)
         quantize_h(768, 896)
         quantize_h(896, J)
-        for q, b in enumerate((6, 7, 4, 5)):
+        for q, b in enumerate((0, 1, 6, 7)):
             down_mm(b, q, q + 1, 768, J)
         for q in range(4):
-            store("VSVS"[q], q, 768)
+            store("VS"[q % 2], q, 768)

@@ -35,11 +35,11 @@ def tile_list_tanh_none_kernel(
         psum = ctx.enter_context(tc.psum_pool(name="psum", bufs=1))
 
         offsets = keep.tile([P, J // 16], U16, name="offsets")
-        wgt_sb = keep.tile([P, J], F32, name="wgt_sb")
-        planes = [[keep.tile([P, TOK], F32, name="plane_%d_%d" % (a, i), align_bytes=64) for i in range(PACK)] for a in range(PASSES)]
-        picked_0 = keep.tile([P, PACK, J], F32, name="picked_0")
-        half_a = keep.tile([P, PACK, 768], F32, name="picked_1a", align_bytes=64)
-        quart = [None, keep.tile([P, 512 + PACK * R], F32, name="picked_1d", align_bytes=64)]
+        wgt_sb = keep.tile([P, J], F32, name="wgt_sb", align_bytes=256)
+        planes = [[keep.tile([P, TOK], F32, name="plane_%d_%d" % (a, i), align_bytes=256) for i in range(PACK)] for a in range(PASSES)]
+        picked_0 = keep.tile([P, PACK, J], F32, name="picked_0", align_bytes=256)
+        half_a = keep.tile([P, PACK, 768], F32, name="picked_1a", align_bytes=256)
+        quart = [None, keep.tile([P, 512 + PACK * R], F32, name="picked_1d", align_bytes=256)]
 
         def picked(a, i0, i1, j0, j1):
             if a == 0:
@@ -55,25 +55,25 @@ def tile_list_tanh_none_kernel(
         x_bf = {}
         x_mx = {}
         wg_raw = [
-            keep.tile([P, PACK, R], F32, name="wg_raw_0", align_bytes=64)[:],
+            keep.tile([P, PACK, R], F32, name="wg_raw_0", align_bytes=256)[:],
             quart[1][:, 512:].rearrange("p (i r) -> p i r", i=PACK),
         ]
         wg_bf = {}
-        wg_codes = [keep.tile([P, R], U32, name="wg_codes_%d" % a, align_bytes=64) for a in range(PASSES)]
+        wg_codes = [keep.tile([P, R], U32, name="wg_codes_%d" % a, align_bytes=256) for a in range(PASSES)]
         wg_scales = {}
-        wu_raw = keep.tile([P, PASSES, 2 * R], U8, name="wu_raw", align_bytes=64)
-        wu_codes = keep.tile([P, PASSES, 2 * R], U8, name="wu_codes", align_bytes=64)
-        wu_sc_raw = keep.tile([P, PASSES, R], U8, name="wu_sc_raw", align_bytes=64)
-        wu_sc = keep.tile([P, PASSES, R], U8, name="wu_sc", align_bytes=64)
-        wd_codes = keep.tile([P, N], I32, name="wd_codes", align_bytes=64)
-        wd_sc = keep.tile([P, N], U8, name="wd_sc", align_bytes=64)
-        th = [keep.tile([P, PACK, QUARTER], F32, name="th_%d" % g) for g in range(J // QUARTER)]
-        h_bf = keep.tile([P, J, PACK], BF16, name="h_bf", align_bytes=64)
-        h_codes = keep.tile([P, J], U32, name="h_codes", align_bytes=64)
-        h_scales = keep.tile([P, J], U8, name="h_scales", align_bytes=64)
-        wgt_rows = keep.tile([P, P], F32, name="wgt_rows")
-        wgt_t = keep.tile([P, J], F32, name="wgt_t")
-        identity = keep.tile([P, P], F32, name="identity")
+        wu_raw = keep.tile([P, PASSES, 2 * R], U8, name="wu_raw", align_bytes=256)
+        wu_codes = keep.tile([P, PASSES, 2 * R], U8, name="wu_codes", align_bytes=256)
+        wu_sc_raw = keep.tile([P, PASSES, R], U8, name="wu_sc_raw", align_bytes=256)
+        wu_sc = keep.tile([P, PASSES, R], U8, name="wu_sc", align_bytes=256)
+        wd_codes = keep.tile([P, N], I32, name="wd_codes", align_bytes=256)
+        wd_sc = keep.tile([P, N], U8, name="wd_sc", align_bytes=256)
+        th = [keep.tile([P, PACK, QUARTER], F32, name="th_%d" % g, align_bytes=256) for g in range(J // QUARTER)]
+        h_bf = keep.tile([P, J, PACK], BF16, name="h_bf", align_bytes=256)
+        h_codes = keep.tile([P, J], U32, name="h_codes", align_bytes=256)
+        h_scales = keep.tile([P, J], U8, name="h_scales", align_bytes=256)
+        wgt_rows = keep.tile([P, P], F32, name="wgt_rows", align_bytes=256)
+        wgt_t = keep.tile([P, J], F32, name="wgt_t", align_bytes=256)
+        identity = keep.tile([P, P], F32, name="identity", align_bytes=256)
 
         x_rows = xT.rearrange("(a p i) t -> a p i t", p=P, i=PACK)
         wg_rows = wg.rearrange("(a p i) r -> a p i r", p=P, i=PACK)
@@ -140,7 +140,7 @@ def tile_list_tanh_none_kernel(
             if isinstance(tag, int):
                 tile = spare(tag, 2 * (j1 - j0)).rearrange("p (j i) -> p j i", i=PACK)
             else:
-                tile = keep.tile([P, j1 - j0, PACK], BF16, name=tag, tag=tag, align_bytes=64)
+                tile = keep.tile([P, j1 - j0, PACK], BF16, name=tag, tag=tag, align_bytes=256)
             for j in range(j0, j1, CH):
                 x_bf[a, j] = (tile, j0)
 
@@ -173,8 +173,8 @@ def tile_list_tanh_none_kernel(
             )
 
         def mx_tiles(a, j0, j1, scale_tag):
-            codes = keep.tile([P, j1 - j0], U32, name="x_codes_%d_%d" % (a, j0), align_bytes=64)
-            scales = keep.tile([P, j1 - j0], U8, name=scale_tag, tag=scale_tag, align_bytes=64)
+            codes = keep.tile([P, j1 - j0], U32, name="x_codes_%d_%d" % (a, j0), align_bytes=256)
+            scales = keep.tile([P, j1 - j0], U8, name=scale_tag, tag=scale_tag, align_bytes=256)
             for j in range(j0, j1, CH):
                 x_mx[a, j] = (codes, scales, j0)
 
@@ -195,7 +195,7 @@ def tile_list_tanh_none_kernel(
                 wg_bf[a, u] = spare(tag, 512)
             else:
                 tag = tag or "wg_bf_%d_%d" % (a, u)
-                wg_bf[a, u] = keep.tile([P, 2 * P * PACK], BF16, name=tag, tag=tag, align_bytes=64)[:]
+                wg_bf[a, u] = keep.tile([P, 2 * P * PACK], BF16, name=tag, tag=tag, align_bytes=256)[:]
             copy_on(
                 engine,
                 wg_bf[a, u].rearrange("p (t m i) -> p m i t", t=2, i=PACK),
@@ -204,7 +204,7 @@ def tile_list_tanh_none_kernel(
 
         def quantize_wg(a, u, tag=None):
             tag = tag or "wg_scales_%d_%d" % (a, u)
-            wg_scales[a, u] = keep.tile([P, 2 * P], U8, name=tag, tag=tag, align_bytes=64)
+            wg_scales[a, u] = keep.tile([P, 2 * P], U8, name=tag, tag=tag, align_bytes=256)
             c0, c1 = 2 * P * u, 2 * P * (u + 1)
             nc.vector.quantize_mx(
                 out=wg_codes[a][:, c0:c1].bitcast(FP8X4),
@@ -272,7 +272,7 @@ def tile_list_tanh_none_kernel(
                     start=True,
                     stop=True,
                 )
-            y = keep.tile([P, q1 - q0, j1 - j0], F32, name="y_%d_%d" % (q0, j0))
+            y = keep.tile([P, q1 - q0, j1 - j0], F32, name="y_%d_%d" % (q0, j0), align_bytes=256)
             copy_on(engine, y[:], acc[:])
             nc.sync.dma_start(out=out_rows[:, q0:q1, j0:j1], in_=y[:])
 
@@ -372,7 +372,7 @@ def tile_list_tanh_none_kernel(
 
         def store(engine, q0, j0):
             acc, q1, j1 = ys[q0, j0]
-            y = keep.tile([P, q1 - q0, j1 - j0], F32, name="y_%d_%d" % (q0, j0))
+            y = keep.tile([P, q1 - q0, j1 - j0], F32, name="y_%d_%d" % (q0, j0), align_bytes=256)
             copy_on(engine, y[:], acc[:])
             nc.sync.dma_start(out=out_rows[:, q0:q1, j0:j1], in_=y[:])
 

@@ -3,7 +3,7 @@ from contextlib import ExitStack
 import concourse.mybir as mybir
 from concourse.masks import make_identity
 
-K, R, N, TOK, J = 1024, 512, 512, 2048, 1024
+K, R, N, T, J = 1024, 512, 512, 2048, 1024
 FLOPS = 2 * K * R * J * 2 + 2 * R * N * J
 
 F32 = mybir.dt.float32
@@ -22,8 +22,12 @@ COPY = mybir.ActivationFunctionType.Copy
 P = 128
 PACK = 4
 PASSES = K // (P * PACK)
-CH = 128
+CHUNK = 128
 QUARTER = 256
+HALF = 512
+LATE = J - QUARTER
+ALIGN = 256
+QUADRANTS = 4
 
 
 def tile_list_tanh_none_kernel(
@@ -34,50 +38,55 @@ def tile_list_tanh_none_kernel(
         keep = ctx.enter_context(tc.tile_pool(name="keep", bufs=1))
         psum = ctx.enter_context(tc.psum_pool(name="psum", bufs=1))
 
+        def sbuf(shape, dtype, name):
+            return keep.tile(shape, dtype, name=name, tag=name, align_bytes=ALIGN)
+
+        def bank(b, shape):
+            return psum.tile(shape, F32, name="bank_%d" % b, tag="bank_%d" % b)
+
         offsets = keep.tile([P, J // 16], U16, name="offsets")
-        wgt_sb = keep.tile([P, J], F32, name="wgt_sb", align_bytes=256)
-        planes = [[keep.tile([P, TOK], F32, name="plane_%d_%d" % (a, i), align_bytes=256) for i in range(PACK)] for a in range(PASSES)]
-        picked_0 = keep.tile([P, PACK, J], F32, name="picked_0", align_bytes=256)
-        half_a = keep.tile([P, PACK, 768], F32, name="picked_1a", align_bytes=256)
-        quart = [None, keep.tile([P, 512 + PACK * R], F32, name="picked_1d", align_bytes=256)]
-
-        def picked(a, i0, i1, j0, j1):
-            if a == 0:
-                return picked_0[:, i0:i1, j0:j1]
-            if j1 <= 768:
-                return half_a[:, i0:i1, j0:j1]
-            q = j0 // 256 - 2
-            return quart[q][:, : PACK * 256].rearrange("p (i j) -> p i j", i=PACK)[:, i0:i1, j0 % 256 : j0 % 256 + j1 - j0]
-
-        def spare(at, words):
-            return quart[at // 1280][:, at % 1280 : at % 1280 + words].bitcast(BF16)
+        wgt_sb = sbuf([P, J], F32, "wgt_sb")
+        planes = [[sbuf([P, T], F32, "plane_%d_%d" % (a, i)) for i in range(PACK)] for a in range(PASSES)]
+        picked_0 = sbuf([P, PACK, J], F32, "picked_0")
+        picked_1 = sbuf([P, PACK, LATE], F32, "picked_1")
+        late_and_wg = sbuf([P, 2 * QUARTER + PACK * R], F32, "late_and_wg")
+        picked_late = late_and_wg[:, : PACK * QUARTER].rearrange("p (i j) -> p i j", i=PACK)
+        wg_raw = [
+            sbuf([P, PACK, R], F32, "wg_raw_0")[:],
+            late_and_wg[:, 2 * QUARTER :].rearrange("p (i r) -> p i r", i=PACK),
+        ]
+        wg_codes = [sbuf([P, R], U32, "wg_codes_%d" % a) for a in range(PASSES)]
+        wu_raw = sbuf([P, PASSES, 2 * R], U8, "wu_raw")
+        wu_codes = sbuf([P, PASSES, 2 * R], U8, "wu_codes")
+        wu_sc_raw = sbuf([P, PASSES, R], U8, "wu_sc_raw")
+        wu_sc = sbuf([P, PASSES, R], U8, "wu_sc")
+        wd_codes = sbuf([P, N], I32, "wd_codes")
+        wd_sc = sbuf([P, N], U8, "wd_sc")
+        tanh_ga = [sbuf([P, PACK, QUARTER], F32, "tanh_ga_%d" % g) for g in range(J // QUARTER)]
+        h_bf = sbuf([P, J, PACK], BF16, "h_bf")
+        h_codes = sbuf([P, J], U32, "h_codes")
+        h_scales = sbuf([P, J], U8, "h_scales")
+        wgt_rows = sbuf([P, P], F32, "wgt_rows")
+        wgt_t = sbuf([P, J], F32, "wgt_t")
+        identity = sbuf([P, P], F32, "identity")
 
         x_bf = {}
         x_mx = {}
-        wg_raw = [
-            keep.tile([P, PACK, R], F32, name="wg_raw_0", align_bytes=256)[:],
-            quart[1][:, 512:].rearrange("p (i r) -> p i r", i=PACK),
-        ]
         wg_bf = {}
-        wg_codes = [keep.tile([P, R], U32, name="wg_codes_%d" % a, align_bytes=256) for a in range(PASSES)]
         wg_scales = {}
-        wu_raw = keep.tile([P, PASSES, 2 * R], U8, name="wu_raw", align_bytes=256)
-        wu_codes = keep.tile([P, PASSES, 2 * R], U8, name="wu_codes", align_bytes=256)
-        wu_sc_raw = keep.tile([P, PASSES, R], U8, name="wu_sc_raw", align_bytes=256)
-        wu_sc = keep.tile([P, PASSES, R], U8, name="wu_sc", align_bytes=256)
-        wd_codes = keep.tile([P, N], I32, name="wd_codes", align_bytes=256)
-        wd_sc = keep.tile([P, N], U8, name="wd_sc", align_bytes=256)
-        th = [keep.tile([P, PACK, QUARTER], F32, name="th_%d" % g, align_bytes=256) for g in range(J // QUARTER)]
-        h_bf = keep.tile([P, J, PACK], BF16, name="h_bf", align_bytes=256)
-        h_codes = keep.tile([P, J], U32, name="h_codes", align_bytes=256)
-        h_scales = keep.tile([P, J], U8, name="h_scales", align_bytes=256)
-        wgt_rows = keep.tile([P, P], F32, name="wgt_rows", align_bytes=256)
-        wgt_t = keep.tile([P, J], F32, name="wgt_t", align_bytes=256)
-        identity = keep.tile([P, P], F32, name="identity", align_bytes=256)
+        ub = {}
+        ga = {}
+        y_banks = {}
 
         x_rows = xT.rearrange("(a p i) t -> a p i t", p=P, i=PACK)
         wg_rows = wg.rearrange("(a p i) r -> a p i r", p=P, i=PACK)
         out_rows = out.rearrange("(q p) j -> p q j", p=P)
+
+        def copy_on(engine, dst, src):
+            if engine == "scalar":
+                nc.scalar.copy(out=dst, in_=src)
+            else:
+                nc.vector.tensor_copy(out=dst, in_=src)
 
         def load_plane(a, i):
             nc.sync.dma_start(out=planes[a][i][:], in_=x_rows[a, :, i, :])
@@ -85,198 +94,7 @@ def tile_list_tanh_none_kernel(
         def load_wg(a):
             nc.sync.dma_start(out=wg_raw[a], in_=wg_rows[a])
 
-        def load_wgt(j0, j1):
-            nc.sync.dma_start(out=wgt_sb[:, j0:j1], in_=wgt[:, j0:j1])
-
-        def spread_wgt():
-            heads = psum.tile([P, P], F32, name="bank_0", tag="bank_0")
-            nc.tensor.transpose(out=heads[:], in_=wgt_rows[:], identity=identity[:])
-            blocks = QUARTER // P
-            for g in range(J // QUARTER):
-                nc.scalar.activation(
-                    func=COPY,
-                    out=wgt_t[:, g * QUARTER : (g + 1) * QUARTER].rearrange("p (b q r) -> p b q r", q=16, r=8),
-                    in_=heads[:]
-                    .rearrange("p (q b) -> p b q", b=8)[:, g * blocks : (g + 1) * blocks, :]
-                    .unsqueeze(3)
-                    .to_broadcast([P, blocks, 16, 8]),
-                )
-            for g in range(J // QUARTER):
-                rows = psum.tile([P, blocks, P], F32, name="bank_%d" % (4 + g), tag="bank_%d" % (4 + g))
-                for b in range(blocks):
-                    j0 = g * QUARTER + b * P
-                    nc.tensor.transpose(out=rows[:, b, :], in_=wgt_t[:, j0 : j0 + P], identity=identity[:])
-                nc.scalar.copy(out=wgt_sb[:, g * QUARTER : (g + 1) * QUARTER], in_=rows[:].rearrange("p k j -> p (k j)"))
-
-        def load_wu_scales():
-            for q in range(4):
-                nc.sync.dma_start(
-                    out=wu_sc_raw[32 * q : 32 * q + 4, :, :].bitcast(I32),
-                    in_=wu_scales[:, 4 * q : 4 * q + 4, :].rearrange("a s r -> s a r").bitcast(I32),
-                )
-
-        def load_wd_scales():
-            for q in range(4):
-                nc.sync.dma_start(
-                    out=wd_sc[32 * q : 32 * q + 4, :].bitcast(I32),
-                    in_=wd_scales[0, 4 * q : 4 * q + 4, :].bitcast(I32),
-                )
-
-        def copy_on(engine, dst, src):
-            if engine == "S":
-                nc.scalar.copy(out=dst, in_=src)
-            else:
-                nc.vector.tensor_copy(out=dst, in_=src)
-
-        def gather(a, i, j0, j1):
-            nc.vector.tensor_tensor(
-                out=picked(a, i, i + 1, j0, j1)[:, 0, :],
-                in0=planes[a][i][:].indirect(offsets[:, j0 // 16 : j1 // 16]),
-                in1=wgt_sb[:, j0:j1],
-                op=MULT,
-            )
-
-        def x_tile(a, j0, j1, tag):
-            if isinstance(tag, int):
-                tile = spare(tag, 2 * (j1 - j0)).rearrange("p (j i) -> p j i", i=PACK)
-            else:
-                tile = keep.tile([P, j1 - j0, PACK], BF16, name=tag, tag=tag, align_bytes=256)
-            for j in range(j0, j1, CH):
-                x_bf[a, j] = (tile, j0)
-
-        def x_cols(a, j0, j1):
-            tile, first = x_bf[a, j0]
-            return tile[:, j0 - first : j1 - first, :]
-
-        def interleave_x(engine, a, j0, j1):
-            if engine == "G":
-                nc.gpsimd.tensor_scalar(
-                    out=x_cols(a, j0, j1),
-                    in0=picked(a, 0, PACK, j0, j1).rearrange("p i j -> p j i"),
-                    scalar1=1.0,
-                    scalar2=0.0,
-                    op0=MULT,
-                    op1=ADD,
-                )
-                return
-            copy_on(
-                engine,
-                x_cols(a, j0, j1).rearrange("p (c e) i -> p c i e", e=4),
-                picked(a, 0, PACK, j0, j1).rearrange("p i (c e) -> p c i e", e=4),
-            )
-
-        def interleave_pair(engine, a, u, j0, j1):
-            copy_on(
-                engine,
-                x_cols(a, j0, j1)[:, :, 2 * u : 2 * u + 2].rearrange("p (c e) i -> p c i e", e=4),
-                picked(a, 2 * u, 2 * u + 2, j0, j1).rearrange("p i (c e) -> p c i e", e=4),
-            )
-
-        def mx_tiles(a, j0, j1, scale_tag):
-            codes = keep.tile([P, j1 - j0], U32, name="x_codes_%d_%d" % (a, j0), align_bytes=256)
-            scales = keep.tile([P, j1 - j0], U8, name=scale_tag, tag=scale_tag, align_bytes=256)
-            for j in range(j0, j1, CH):
-                x_mx[a, j] = (codes, scales, j0)
-
-        def x_operand(a, j0, j1):
-            codes, scales, first = x_mx[a, j0]
-            return codes[:, j0 - first : j1 - first].bitcast(FP8X4), scales[:, j0 - first : j1 - first]
-
-        def quantize_x(a, j0, j1):
-            codes, scales = x_operand(a, j0, j1)
-            nc.vector.quantize_mx(
-                out=codes,
-                scales=scales,
-                in_=x_cols(a, j0, j1).rearrange("p j i -> p (j i)"),
-            )
-
-        def interleave_wg(engine, a, u, tag=None):
-            if isinstance(tag, int):
-                wg_bf[a, u] = spare(tag, 512)
-            else:
-                tag = tag or "wg_bf_%d_%d" % (a, u)
-                wg_bf[a, u] = keep.tile([P, 2 * P * PACK], BF16, name=tag, tag=tag, align_bytes=256)[:]
-            copy_on(
-                engine,
-                wg_bf[a, u].rearrange("p (t m i) -> p m i t", t=2, i=PACK),
-                wg_raw[a].rearrange("p i (m t) -> p m i t", t=PACK)[:, :, :, 2 * u : 2 * u + 2],
-            )
-
-        def quantize_wg(a, u, tag=None):
-            tag = tag or "wg_scales_%d_%d" % (a, u)
-            wg_scales[a, u] = keep.tile([P, 2 * P], U8, name=tag, tag=tag, align_bytes=256)
-            c0, c1 = 2 * P * u, 2 * P * (u + 1)
-            nc.vector.quantize_mx(
-                out=wg_codes[a][:, c0:c1].bitcast(FP8X4),
-                scales=wg_scales[a, u][:],
-                in_=wg_bf[a, u],
-            )
-
-        def bank(b, slices):
-            return psum.tile([P, slices, 512 // slices], F32, name="bank_%d" % b, tag="bank_%d" % b)
-
-        def up_pass(acc, c, a):
-            codes, scales = x_operand(a, c * CH, (c + 1) * CH)
-            for t in range(PACK):
-                nc.tensor.matmul_mx(
-                    out=acc[:, t, :],
-                    lhsT=wu_codes[:, a, 2 * P * t : 2 * P * (t + 1)].bitcast(FP4X4),
-                    lhsT_scale=wu_sc[:, a, P * t : P * (t + 1)],
-                    rhs=codes,
-                    rhs_scale=scales,
-                    start=(a == 0 and t == 0),
-                    stop=(a == PASSES - 1 and t == PACK - 1),
-                )
-
-        def gate_pass(acc, g, u, a):
-            codes, scales = x_operand(a, g * QUARTER, (g + 1) * QUARTER)
-            for v in range(2):
-                t = 2 * u + v
-                nc.tensor.matmul_mx(
-                    out=acc[:, v, :],
-                    lhsT=wg_codes[a][:, P * t : P * (t + 1)].bitcast(FP8X4),
-                    lhsT_scale=wg_scales[a, u][:, P * v : P * (v + 1)],
-                    rhs=codes,
-                    rhs_scale=scales,
-                    start=(a == 0 and v == 0),
-                    stop=(a == PASSES - 1 and v == 1),
-                )
-
-        def tanh(acc, g, u):
-            nc.scalar.activation(out=th[g][:, 2 * u : 2 * u + 2, :], in_=acc[:], func=TANH)
-
-        def hidden(acc, c):
-            nc.vector.tensor_tensor(
-                out=h_bf[:, c * CH : (c + 1) * CH, :].rearrange("p (g e) t -> p g t e", e=4),
-                in0=acc[:].rearrange("p t (g e) -> p g t e", e=4),
-                in1=th[c // 2][:, :, c % 2 * CH : (c % 2 + 1) * CH].rearrange("p t (g e) -> p g t e", e=4),
-                op=MULT,
-            )
-
-        def quantize_h(j0, j1):
-            nc.vector.quantize_mx(
-                out=h_codes[:, j0:j1].bitcast(FP8X4),
-                scales=h_scales[:, j0:j1],
-                in_=h_bf[:, j0:j1, :].rearrange("p j t -> p (j t)"),
-            )
-
-        def down(b, engine, q0, q1, j0, j1):
-            acc = psum.tile([P, q1 - q0, j1 - j0], F32, name="bank_%d" % b, tag="bank_%d" % b)
-            for q in range(q0, q1):
-                nc.tensor.matmul_mx(
-                    out=acc[:, q - q0, :],
-                    lhsT=wd_codes[:, P * q : P * (q + 1)].bitcast(FP8X4),
-                    lhsT_scale=wd_sc[:, P * q : P * (q + 1)],
-                    rhs=h_codes[:, j0:j1].bitcast(FP8X4),
-                    rhs_scale=h_scales[:, j0:j1],
-                    start=True,
-                    stop=True,
-                )
-            y = keep.tile([P, q1 - q0, j1 - j0], F32, name="y_%d_%d" % (q0, j0), align_bytes=256)
-            copy_on(engine, y[:], acc[:])
-            nc.sync.dma_start(out=out_rows[:, q0:q1, j0:j1], in_=y[:])
-
-        def permute_wu():
+        def reorder_wu():
             for a in range(PASSES):
                 nc.vector.tensor_copy(
                     out=wu_codes[:, a, :].bitcast(U16).rearrange("p (t m) -> p m t", t=PACK),
@@ -287,78 +105,172 @@ def tile_list_tanh_none_kernel(
                 in_=wu_sc_raw[:].rearrange("p a (m t) -> p a m t", t=PACK),
             )
 
-        def load_wu():
-            nc.sync.dma_start(out=wu_raw[:].bitcast(I32), in_=wu_words.rearrange("a p b -> p a b").bitcast(I32))
+        def spread_wgt():
+            by_pick = bank(0, [P, P])
+            nc.tensor.transpose(out=by_pick[:], in_=wgt_rows[:], identity=identity[:])
+            blocks = QUARTER // P
+            for g in range(J // QUARTER):
+                nc.scalar.activation(
+                    func=COPY,
+                    out=wgt_t[:, g * QUARTER : (g + 1) * QUARTER].rearrange("p (b q r) -> p b q r", q=16, r=8),
+                    in_=by_pick[:]
+                    .rearrange("p (q b) -> p b q", b=8)[:, g * blocks : (g + 1) * blocks, :]
+                    .unsqueeze(3)
+                    .to_broadcast([P, blocks, 16, 8]),
+                )
+            for g in range(J // QUARTER):
+                by_row = bank(4 + g, [P, blocks, P])
+                for b in range(blocks):
+                    j0 = g * QUARTER + b * P
+                    nc.tensor.transpose(out=by_row[:, b, :], in_=wgt_t[:, j0 : j0 + P], identity=identity[:])
+                nc.scalar.copy(
+                    out=wgt_sb[:, g * QUARTER : (g + 1) * QUARTER], in_=by_row[:].rearrange("p b j -> p (b j)")
+                )
 
-        def load_wd():
-            nc.sync.dma_start(out=wd_codes[:], in_=wd_words[0].rearrange("p n i -> p (n i)").bitcast(I32))
+        def picked(a, j0, j1):
+            if a == 0:
+                return picked_0[:, :, j0:j1]
+            if j1 <= LATE:
+                return picked_1[:, :, j0:j1]
+            return picked_late[:, :, j0 - LATE : j1 - LATE]
 
-        def QX(j0, j1, tag=None):
-            mx_tiles(1, j0, j1, tag or "x_scales_1_%d" % j0)
+        def gather(a, i, j0, j1):
+            nc.vector.tensor_tensor(
+                out=picked(a, j0, j1)[:, i, :],
+                in0=planes[a][i][:].indirect(offsets[:, j0 // 16 : j1 // 16]),
+                in1=wgt_sb[:, j0:j1],
+                op=MULT,
+            )
+
+        def new_x_bf(a, j0, j1):
+            tile = sbuf([P, j1 - j0, PACK], BF16, "x_bf_%d_%d" % (a, j0))
+            for j in range(j0, j1, CHUNK):
+                x_bf[a, j] = (tile, j0)
+
+        def x_bf_cols(a, j0, j1):
+            tile, first = x_bf[a, j0]
+            return tile[:, j0 - first : j1 - first, :]
+
+        def interleave_x(engine, a, j0, j1):
+            copy_on(
+                engine,
+                x_bf_cols(a, j0, j1).rearrange("p (c e) i -> p c i e", e=4),
+                picked(a, j0, j1).rearrange("p i (c e) -> p c i e", e=4),
+            )
+
+        def interleave_x_on_gpsimd(a, j0, j1):
+            nc.gpsimd.tensor_scalar(
+                out=x_bf_cols(a, j0, j1),
+                in0=picked(a, j0, j1).rearrange("p i j -> p j i"),
+                scalar1=1.0,
+                scalar2=0.0,
+                op0=MULT,
+                op1=ADD,
+            )
+
+        def new_x_mx(a, j0, j1, scales_name):
+            codes = sbuf([P, j1 - j0], U32, "x_codes_%d_%d" % (a, j0))
+            scales = sbuf([P, j1 - j0], U8, scales_name)
+            for j in range(j0, j1, CHUNK):
+                x_mx[a, j] = (codes, scales, j0)
+
+        def x_operand(a, j0, j1):
+            codes, scales, first = x_mx[a, j0]
+            return codes[:, j0 - first : j1 - first].bitcast(FP8X4), scales[:, j0 - first : j1 - first]
+
+        def quantize_x(a, j0, j1):
+            codes, scales = x_operand(a, j0, j1)
+            nc.vector.quantize_mx(out=codes, scales=scales, in_=x_bf_cols(a, j0, j1).rearrange("p j i -> p (j i)"))
+
+        def quantize_x_quarter(g):
+            j0, j1 = g * QUARTER, (g + 1) * QUARTER
+            new_x_mx(1, j0, j1, "x_scales_1_%d" % j0)
             quantize_x(1, j0, j1)
 
-        up = {}
-        gate = {}
+        def interleave_wg(engine, a, u):
+            wg_bf[a, u] = sbuf([P, 2 * P * PACK], BF16, "wg_bf_%d_%d" % (a, u))
+            copy_on(
+                engine,
+                wg_bf[a, u][:].rearrange("p (t m i) -> p m i t", t=2, i=PACK),
+                wg_raw[a].rearrange("p i (m t) -> p m i t", t=PACK)[:, :, :, 2 * u : 2 * u + 2],
+            )
 
-        def up_early(c, b):
-            up[c] = bank(b, PACK)
-            up_pass(up[c], c, 0)
+        def quantize_wg(a, u):
+            wg_scales[a, u] = sbuf([P, 2 * P], U8, "wg_scales_%d_%d" % (a, u))
+            nc.vector.quantize_mx(
+                out=wg_codes[a][:, 2 * P * u : 2 * P * (u + 1)].bitcast(FP8X4),
+                scales=wg_scales[a, u][:],
+                in_=wg_bf[a, u][:],
+            )
 
-        def gate_early(g, u, b):
-            gate[g, u] = bank(b, 2)
-            gate_pass(gate[g, u], g, u, 0)
+        def up_pass(c, a):
+            codes, scales = x_operand(a, c * CHUNK, (c + 1) * CHUNK)
+            for t in range(PACK):
+                nc.tensor.matmul_mx(
+                    out=ub[c][:, t, :],
+                    lhsT=wu_codes[:, a, 2 * P * t : 2 * P * (t + 1)].bitcast(FP4X4),
+                    lhsT_scale=wu_sc[:, a, P * t : P * (t + 1)],
+                    rhs=codes,
+                    rhs_scale=scales,
+                    start=(a == 0 and t == 0),
+                    stop=(a == PASSES - 1 and t == PACK - 1),
+                )
 
-        def gate_late(g, u):
-            gate_pass(gate[g, u], g, u, 1)
+        def gate_pass(g, u, a):
+            codes, scales = x_operand(a, g * QUARTER, (g + 1) * QUARTER)
+            for v in range(2):
+                t = 2 * u + v
+                nc.tensor.matmul_mx(
+                    out=ga[g, u][:, v, :],
+                    lhsT=wg_codes[a][:, P * t : P * (t + 1)].bitcast(FP8X4),
+                    lhsT_scale=wg_scales[a, u][:, P * v : P * (v + 1)],
+                    rhs=codes,
+                    rhs_scale=scales,
+                    start=(a == 0 and v == 0),
+                    stop=(a == PASSES - 1 and v == 1),
+                )
 
-        def gate_full(g, u, b):
-            gate_early(g, u, b)
-            gate_late(g, u)
+        def open_up(c, b):
+            ub[c] = bank(b, [P, PACK, CHUNK])
+            up_pass(c, 0)
 
-        def up_late(c):
-            up_pass(up[c], c, 1)
+        def open_gate(g, u, b):
+            ga[g, u] = bank(b, [P, 2, QUARTER])
+            gate_pass(g, u, 0)
 
-        def up_full(c, b):
-            up_early(c, b)
-            up_late(c)
+        def up_quarter(g, first_bank):
+            for v in range(2):
+                open_up(2 * g + v, first_bank + v)
+                up_pass(2 * g + v, 1)
 
-        def T(g, u):
-            tanh(gate[g, u], g, u)
+        def gate_quarter(g, first_bank):
+            for u in range(2):
+                open_gate(g, u, first_bank + u)
+                gate_pass(g, u, 1)
 
-        def H(c):
-            hidden(up[c], c)
+        def tanh_quarter(g):
+            for u in range(2):
+                nc.scalar.activation(out=tanh_ga[g][:, 2 * u : 2 * u + 2, :], in_=ga[g, u][:], func=TANH)
 
-        def IX(engine, j0, j1, tag=None):
-            x_tile(1, j0, j1, "x_bf_1_%d" % j0 if tag is None else tag)
-            interleave_x(engine, 1, j0, j1)
+        def hidden(c):
+            j0 = c % 2 * CHUNK
+            nc.vector.tensor_tensor(
+                out=h_bf[:, c * CHUNK : (c + 1) * CHUNK, :].rearrange("p (d e) t -> p d t e", e=4),
+                in0=ub[c][:].rearrange("p t (d e) -> p d t e", e=4),
+                in1=tanh_ga[c // 2][:, :, j0 : j0 + CHUNK].rearrange("p t (d e) -> p d t e", e=4),
+                op=MULT,
+            )
 
-        def IP0(engine, j0, j1, tag=None):
-            x_tile(1, j0, j1, "x_bf_1_%d" % j0 if tag is None else tag)
-            interleave_pair(engine, 1, 0, j0, j1)
+        def quantize_h(j0, j1):
+            nc.vector.quantize_mx(
+                out=h_codes[:, j0:j1].bitcast(FP8X4),
+                scales=h_scales[:, j0:j1],
+                in_=h_bf[:, j0:j1, :].rearrange("p j t -> p (j t)"),
+            )
 
-        def XT(j0, j1, tag):
-            x_tile(1, j0, j1, tag)
-
-        def IPE(engine, j0, j1):
-            interleave_pair(engine, 1, 0, j0, j1)
-
-        def IP1(engine, j0, j1):
-            interleave_pair(engine, 1, 1, j0, j1)
-
-        def head():
-            make_identity(nc, identity[:])
-            nc.vector.memset(wu_sc_raw[:].rearrange("p a r -> p (a r)").bitcast(I32), 0)
-            nc.vector.memset(wd_sc[:].bitcast(I32), 0)
-            nc.sync.dma_start(offsets[:], offs)
-            nc.sync.dma_start(out=wgt_rows[:], in_=wgt[::8, :].rearrange("q (b j) -> q b j", j=P))
-            load_wu()
-            load_wu_scales()
-
-        ys = {}
-
-        def down_mm(b, q0, q1, j0, j1):
-            acc = psum.tile([P, q1 - q0, j1 - j0], F32, name="bank_%d" % b, tag="bank_%d" % b)
-            ys[q0, j0] = (acc, q1, j1)
+        def down(b, q0, q1, j0, j1):
+            acc = bank(b, [P, q1 - q0, j1 - j0])
+            y_banks[q0, j0] = (acc, q1 - q0, j1 - j0)
             for q in range(q0, q1):
                 nc.tensor.matmul_mx(
                     out=acc[:, q - q0, :],
@@ -370,14 +282,32 @@ def tile_list_tanh_none_kernel(
                     stop=True,
                 )
 
-        def store(engine, q0, j0):
-            acc, q1, j1 = ys[q0, j0]
-            y = keep.tile([P, q1 - q0, j1 - j0], F32, name="y_%d_%d" % (q0, j0), align_bytes=256)
-            copy_on(engine, y[:], acc[:])
-            nc.sync.dma_start(out=out_rows[:, q0:q1, j0:j1], in_=y[:])
+        def down_quarter(g, first_bank):
+            for u in range(2):
+                down(first_bank + u, 2 * u, 2 * u + 2, g * QUARTER, (g + 1) * QUARTER)
 
-        head()
-        for i in range(4):
+        def store(engine, q0, j0):
+            acc, blocks, picks = y_banks[q0, j0]
+            y = sbuf([P, blocks, picks], F32, "y_%d_%d" % (q0, j0))
+            copy_on(engine, y[:], acc[:])
+            nc.sync.dma_start(out=out_rows[:, q0 : q0 + blocks, j0 : j0 + picks], in_=y[:])
+
+        def store_quarter(g):
+            for u in range(2):
+                store("scalar", 2 * u, g * QUARTER)
+
+        make_identity(nc, identity[:])
+        nc.vector.memset(wu_sc_raw[:].rearrange("p a r -> p (a r)").bitcast(I32), 0)
+        nc.vector.memset(wd_sc[:].bitcast(I32), 0)
+        nc.sync.dma_start(offsets[:], offs)
+        nc.sync.dma_start(out=wgt_rows[:], in_=wgt[::8, :].rearrange("q (b j) -> q b j", j=P))
+        nc.sync.dma_start(out=wu_raw[:].bitcast(I32), in_=wu_words.rearrange("a p b -> p a b").bitcast(I32))
+        for q in range(QUADRANTS):
+            nc.sync.dma_start(
+                out=wu_sc_raw[32 * q : 32 * q + 4, :, :].bitcast(I32),
+                in_=wu_scales[:, 4 * q : 4 * q + 4, :].rearrange("a s r -> s a r").bitcast(I32),
+            )
+        for i in range(PACK):
             load_plane(0, i)
         load_plane(1, 0)
         load_plane(1, 1)
@@ -385,112 +315,95 @@ def tile_list_tanh_none_kernel(
         load_plane(1, 2)
         load_plane(1, 3)
         load_wg(1)
-        load_wd()
-        load_wd_scales()
-        permute_wu()
+        nc.sync.dma_start(out=wd_codes[:], in_=wd_words[0].rearrange("p n i -> p (n i)").bitcast(I32))
+        for q in range(QUADRANTS):
+            nc.sync.dma_start(
+                out=wd_sc[32 * q : 32 * q + 4, :].bitcast(I32),
+                in_=wd_scales[0, 4 * q : 4 * q + 4, :].bitcast(I32),
+            )
+        reorder_wu()
         spread_wgt()
-        for j0, j1 in ((0, 256), (256, 512), (512, J)):
+
+        for j0, j1 in ((0, QUARTER), (QUARTER, HALF), (HALF, J)):
             gather(0, 0, j0, j1)
         gather(0, 1, 0, J)
         gather(0, 2, 0, J)
-        x_tile(0, 0, J, "x_bf_0")
-        for j0 in range(0, J, 512):
-            gather(0, 3, j0, j0 + 512)
-            interleave_x("S", 0, j0, j0 + 512)
+        new_x_bf(0, 0, J)
+        for j0 in range(0, J, HALF):
+            gather(0, 3, j0, j0 + HALF)
+            interleave_x("scalar", 0, j0, j0 + HALF)
         for i in range(2):
-            for j0, j1 in ((0, 768), (768, J)):
-                gather(1, i, j0, j1)
-        mx_tiles(0, 0, J, "x_scales_0")
-        mx_tiles(1, 0, 256, "x_scales_1_0")
+            gather(1, i, 0, LATE)
+            gather(1, i, LATE, J)
+        new_x_mx(0, 0, J, "x_scales_0")
+        new_x_mx(1, 0, QUARTER, "x_scales_1_0")
         quantize_x(0, 0, J)
-
-        interleave_wg("S", 0, 0)
-        interleave_wg("S", 0, 1)
+        interleave_wg("scalar", 0, 0)
+        interleave_wg("scalar", 0, 1)
         quantize_wg(0, 0)
         quantize_wg(0, 1)
-        gather(1, 2, 0, 768)
-        up_early(0, 4)
-        up_early(1, 5)
-        up_early(2, 6)
-        up_early(3, 7)
-        gate_early(0, 0, 0)
-        gate_early(0, 1, 1)
-        gate_early(1, 0, 2)
-        gate_early(1, 1, 3)
-        gather(1, 3, 0, 128)
-        gather(1, 3, 128, 256)
-        gather(1, 3, 256, 512)
-        gather(1, 3, 512, 768)
-        IX("S", 0, 128)
-        IX("S", 128, 256)
-        IX("S", 256, 512)
-        IX("S", 512, 768)
-        quantize_x(1, 0, 128)
-        quantize_x(1, 128, 256)
-        interleave_wg("V", 1, 0)
-        QX(256, 512)
-        quantize_wg(1, 0)
-        interleave_wg("V", 1, 1)
-        QX(512, 768)
-        quantize_wg(1, 1)
-        gate_late(0, 0)
-        gate_late(0, 1)
-        up_late(0)
-        up_late(1)
-        gate_late(1, 0)
-        gate_late(1, 1)
-        up_late(2)
-        up_late(3)
-        gather(1, 2, 768, J)
-        gather(1, 3, 768, 896)
-        gather(1, 3, 896, J)
-        T(0, 0)
-        T(0, 1)
-        T(1, 0)
-        T(1, 1)
-        x_tile(1, 768, J, "x_bf_1_768")
-        interleave_x("V", 1, 768, 896)
-        interleave_x("S", 1, 896, J)
-        gate_full(2, 0, 0)
-        gate_full(2, 1, 1)
-        H(0)
-        H(1)
-        quantize_h(0, 128)
-        H(2)
-        quantize_h(128, 256)
-        QX(768, J)
-        down_mm(4, 0, 4, 0, 128)
-        down_mm(5, 0, 4, 128, 256)
-        up_full(4, 2)
-        up_full(5, 3)
-        T(2, 0)
-        T(2, 1)
-        H(3)
-        store("S", 0, 0)
-        quantize_h(256, 512)
-        gate_full(3, 0, 0)
-        gate_full(3, 1, 1)
-        store("S", 0, 128)
-        down_mm(6, 0, 2, 256, 512)
-        down_mm(7, 2, 4, 256, 512)
-        up_full(6, 4)
-        up_full(7, 5)
-        T(3, 0)
-        T(3, 1)
-        H(4)
-        H(5)
-        store("S", 0, 256)
-        store("S", 2, 256)
-        H(6)
-        quantize_h(512, 768)
-        down_mm(2, 0, 2, 512, 768)
-        down_mm(3, 2, 4, 512, 768)
-        H(7)
-        store("S", 0, 512)
-        store("S", 2, 512)
-        quantize_h(768, 896)
-        quantize_h(896, J)
+        gather(1, 2, 0, LATE)
+        for c in range(HALF // CHUNK):
+            open_up(c, 4 + c)
+        for g in range(HALF // QUARTER):
+            for u in range(2):
+                open_gate(g, u, 2 * g + u)
+
+        pieces = ((0, CHUNK), (CHUNK, QUARTER), (QUARTER, HALF), (HALF, LATE))
+        for j0, j1 in pieces:
+            gather(1, 3, j0, j1)
+        for j0, j1 in pieces:
+            new_x_bf(1, j0, j1)
+            interleave_x("scalar", 1, j0, j1)
+        quantize_x(1, 0, CHUNK)
+        quantize_x(1, CHUNK, QUARTER)
+        for u in range(2):
+            interleave_wg("vector", 1, u)
+            quantize_x_quarter(1 + u)
+            quantize_wg(1, u)
+        for g in range(HALF // QUARTER):
+            for u in range(2):
+                gate_pass(g, u, 1)
+            for v in range(2):
+                up_pass(2 * g + v, 1)
+        gather(1, 2, LATE, J)
+        gather(1, 3, LATE, J)
+        tanh_quarter(0)
+        tanh_quarter(1)
+        new_x_bf(1, LATE, J)
+        interleave_x_on_gpsimd(1, LATE, LATE + CHUNK)
+        interleave_x("scalar", 1, LATE + CHUNK, J)
+
+        gate_quarter(2, 0)
+        hidden(0)
+        hidden(1)
+        quantize_h(0, CHUNK)
+        hidden(2)
+        quantize_h(CHUNK, QUARTER)
+        quantize_x_quarter(3)
+        down(4, 0, PACK, 0, CHUNK)
+        down(5, 0, PACK, CHUNK, QUARTER)
+        up_quarter(2, 2)
+        tanh_quarter(2)
+        hidden(3)
+        store("scalar", 0, 0)
+        quantize_h(QUARTER, HALF)
+        gate_quarter(3, 0)
+        store("scalar", 0, CHUNK)
+        down_quarter(1, 6)
+        up_quarter(3, 4)
+        tanh_quarter(3)
+        hidden(4)
+        hidden(5)
+        store_quarter(1)
+        hidden(6)
+        quantize_h(HALF, LATE)
+        down_quarter(2, 2)
+        hidden(7)
+        store_quarter(2)
+        quantize_h(LATE, LATE + CHUNK)
+        quantize_h(LATE + CHUNK, J)
         for q, b in enumerate((0, 1, 6, 7)):
-            down_mm(b, q, q + 1, 768, J)
-        for q in range(4):
-            store("VS"[q % 2], q, 768)
+            down(b, q, q + 1, LATE, J)
+        for q in range(PACK):
+            store(("vector", "scalar")[q % 2], q, LATE)

@@ -142,8 +142,8 @@ def tile_list_tanh_none_kernel(
                 op=MULT,
             )
 
-        def new_x_bf(a, j0, j1):
-            tile = sbuf([P, j1 - j0, PACK], BF16, "x_bf_%d_%d" % (a, j0))
+        def new_x_bf(a, j0, j1, name=None):
+            tile = sbuf([P, j1 - j0, PACK], BF16, name or "x_bf_%d_%d" % (a, j0))
             for j in range(j0, j1, CHUNK):
                 x_bf[a, j] = (tile, j0)
 
@@ -156,6 +156,23 @@ def tile_list_tanh_none_kernel(
                 engine,
                 x_bf_cols(a, j0, j1).rearrange("p (c e) i -> p c i e", e=4),
                 picked(a, j0, j1).rearrange("p i (c e) -> p c i e", e=4),
+            )
+
+        def interleave_pair(engine, a, i, j0, j1):
+            copy_on(
+                engine,
+                x_bf_cols(a, j0, j1).rearrange("p (c e) i -> p c i e", e=4)[:, :, i : i + 2, :],
+                picked(a, j0, j1).rearrange("p i (c e) -> p c i e", e=4)[:, :, i : i + 2, :],
+            )
+
+        def interleave_pair_on_gpsimd(a, i, j0, j1):
+            nc.gpsimd.tensor_scalar(
+                out=x_bf_cols(a, j0, j1)[:, :, i : i + 2],
+                in0=picked(a, j0, j1).rearrange("p i j -> p j i")[:, :, i : i + 2],
+                scalar1=1.0,
+                scalar2=0.0,
+                op0=MULT,
+                op1=ADD,
             )
 
         def interleave_x_on_gpsimd(a, j0, j1):
@@ -252,9 +269,25 @@ def tile_list_tanh_none_kernel(
             for u in range(2):
                 nc.scalar.activation(out=tanh_ga[g][:, 2 * u : 2 * u + 2, :], in_=ga[g, u][:], func=TANH)
 
-        def hidden(c):
+        def tanh_pair(g, u):
+            nc.scalar.activation(out=tanh_ga[g][:, 2 * u : 2 * u + 2, :], in_=ga[g, u][:], func=TANH)
+
+        def gate_both(g, u, b):
+            open_gate(g, u, b)
+            gate_pass(g, u, 1)
+
+        def up_both(c, b):
+            open_up(c, b)
+            up_pass(c, 1)
+
+        def park_up(c):
+            parked = sbuf([P, PACK, CHUNK], F32, "ub_parked_%d" % c)
+            nc.scalar.copy(out=parked[:], in_=ub[c][:])
+            ub[c] = parked
+
+        def hidden(c, engine=None):
             j0 = c % 2 * CHUNK
-            nc.vector.tensor_tensor(
+            (engine or nc.vector).tensor_tensor(
                 out=h_bf[:, c * CHUNK : (c + 1) * CHUNK, :].rearrange("p (d e) t -> p d t e", e=4),
                 in0=ub[c][:].rearrange("p t (d e) -> p d t e", e=4),
                 in1=tanh_ga[c // 2][:, :, j0 : j0 + CHUNK].rearrange("p t (d e) -> p d t e", e=4),
@@ -349,61 +382,87 @@ def tile_list_tanh_none_kernel(
             for u in range(2):
                 open_gate(g, u, 2 * g + u)
 
-        pieces = ((0, CHUNK), (CHUNK, QUARTER), (QUARTER, HALF), (HALF, LATE))
-        for j0, j1 in pieces:
-            gather(1, 3, j0, j1)
-        for j0, j1 in pieces:
-            new_x_bf(1, j0, j1)
-            interleave_x("scalar", 1, j0, j1)
-        quantize_x(1, 0, CHUNK)
-        quantize_x(1, CHUNK, QUARTER)
-        for u in range(2):
-            interleave_wg("vector", 1, u)
-            quantize_x_quarter(1 + u)
-            quantize_wg(1, u)
-        for g in range(HALF // QUARTER):
-            for u in range(2):
-                gate_pass(g, u, 1)
-            for v in range(2):
-                up_pass(2 * g + v, 1)
+        gather(1, 3, 0, 128)
+        gather(1, 3, 128, 256)
+        gather(1, 3, 256, 512)
+        gather(1, 3, 512, 768)
+        new_x_bf(1, 0, 128)
+        interleave_x("scalar", 1, 0, 128)
+        new_x_bf(1, 128, 256)
+        interleave_x("scalar", 1, 128, 256)
+        new_x_bf(1, 256, 512)
+        interleave_x("scalar", 1, 256, 512)
+        new_x_bf(1, 512, 768)
+        interleave_x("scalar", 1, 512, 768)
+        quantize_x(1, 0, 128)
+        quantize_x(1, 128, 256)
+        interleave_wg("vector", 1, 0)
+        quantize_x_quarter(1)
+        quantize_wg(1, 0)
+        interleave_wg("vector", 1, 1)
+        quantize_x_quarter(2)
+        quantize_wg(1, 1)
+        gate_pass(0, 0, 1)
+        gate_pass(0, 1, 1)
+        up_pass(0, 1)
+        up_pass(1, 1)
+        gate_pass(1, 0, 1)
+        gate_pass(1, 1, 1)
+        up_pass(2, 1)
+        up_pass(3, 1)
         gather(1, 2, LATE, J)
         gather(1, 3, LATE, J)
-        tanh_quarter(0)
-        tanh_quarter(1)
+        tanh_pair(0, 0)
+        tanh_pair(0, 1)
+        tanh_pair(1, 0)
+        tanh_pair(1, 1)
         new_x_bf(1, LATE, J)
         interleave_x_on_gpsimd(1, LATE, LATE + CHUNK)
         interleave_x("scalar", 1, LATE + CHUNK, J)
-
-        gate_quarter(2, 0)
+        gate_both(2, 0, 0)
+        up_both(4, 2)
+        gate_both(2, 1, 1)
+        up_both(5, 3)
         hidden(0)
         hidden(1)
-        quantize_h(0, CHUNK)
+        quantize_h(0, 128)
         hidden(2)
-        quantize_h(CHUNK, QUARTER)
-        quantize_x_quarter(3)
-        down(4, 0, PACK, 0, CHUNK)
-        down(5, 0, PACK, CHUNK, QUARTER)
-        up_quarter(2, 2)
-        tanh_quarter(2)
+        quantize_h(128, 256)
         hidden(3)
+        quantize_x_quarter(3)
+        quantize_h(256, 512)
+        tanh_pair(2, 0)
+        tanh_pair(2, 1)
+        down(5, 0, 4, 0, 128)
+        down(6, 0, 4, 128, 256)
+        gate_both(3, 0, 0)
+        down(7, 0, 2, 256, 512)
+        gate_both(3, 1, 1)
         store("scalar", 0, 0)
-        quantize_h(QUARTER, HALF)
-        gate_quarter(3, 0)
-        store("scalar", 0, CHUNK)
-        down_quarter(1, 6)
-        up_quarter(3, 4)
-        tanh_quarter(3)
+        store("scalar", 0, 128)
+        down(5, 2, 4, 256, 512)
+        up_both(6, 4)
+        up_both(7, 6)
         hidden(4)
         hidden(5)
-        store_quarter(1)
+        tanh_pair(3, 0)
+        tanh_pair(3, 1)
+        store("vector", 0, 256)
+        store("scalar", 2, 256)
+        quantize_h(512, 768)
+        down(2, 0, 2, 512, 768)
+        down(3, 2, 4, 512, 768)
         hidden(6)
-        quantize_h(HALF, LATE)
-        down_quarter(2, 2)
         hidden(7)
-        store_quarter(2)
-        quantize_h(LATE, LATE + CHUNK)
-        quantize_h(LATE + CHUNK, J)
-        for q, b in enumerate((0, 1, 6, 7)):
-            down(b, q, q + 1, LATE, J)
-        for q in range(PACK):
-            store(("vector", "scalar")[q % 2], q, LATE)
+        store("scalar", 0, 512)
+        store("scalar", 2, 512)
+        quantize_h(768, 896)
+        quantize_h(896, 1024)
+        down(7, 0, 1, 768, 1024)
+        down(0, 1, 2, 768, 1024)
+        down(1, 2, 3, 768, 1024)
+        down(5, 3, 4, 768, 1024)
+        store("vector", 0, 768)
+        store("scalar", 1, 768)
+        store("vector", 2, 768)
+        store("scalar", 3, 768)

@@ -62,7 +62,7 @@ def tile_list_tanh_none_kernel(
         wu_sc = sbuf([P, PASSES, R], U8, "wu_sc")
         wd_codes = sbuf([P, N], I32, "wd_codes")
         wd_sc = sbuf([P, N], U8, "wd_sc")
-        tanh_ga = [sbuf([P, PACK, QUARTER], F32, "tanh_ga_%d" % g) for g in range(J // QUARTER)]
+        tanh_ga = {}
         h_bf = sbuf([P, J, PACK], BF16, "h_bf")
         h_codes = sbuf([P, J], U32, "h_codes")
         h_scales = sbuf([P, J], U8, "h_scales")
@@ -204,8 +204,8 @@ def tile_list_tanh_none_kernel(
             new_x_mx(1, j0, j1, "x_scales_1_%d" % j0)
             quantize_x(1, j0, j1)
 
-        def interleave_wg(engine, a, u):
-            wg_bf[a, u] = sbuf([P, 2 * P * PACK], BF16, "wg_bf_%d_%d" % (a, u))
+        def interleave_wg(engine, a, u, name=None):
+            wg_bf[a, u] = sbuf([P, 2 * P * PACK], BF16, name or "wg_bf_%d_%d" % (a, u))
             copy_on(
                 engine,
                 wg_bf[a, u][:].rearrange("p (t m i) -> p m i t", t=2, i=PACK),
@@ -269,7 +269,9 @@ def tile_list_tanh_none_kernel(
             for u in range(2):
                 nc.scalar.activation(out=tanh_ga[g][:, 2 * u : 2 * u + 2, :], in_=ga[g, u][:], func=TANH)
 
-        def tanh_pair(g, u):
+        def tanh_pair(g, u, name=None):
+            if g not in tanh_ga:
+                tanh_ga[g] = sbuf([P, PACK, QUARTER], F32, name or "tanh_ga_%d" % g)
             nc.scalar.activation(out=tanh_ga[g][:, 2 * u : 2 * u + 2, :], in_=ga[g, u][:], func=TANH)
 
         def gate_both(g, u, b):
@@ -372,10 +374,10 @@ def tile_list_tanh_none_kernel(
         new_x_mx(1, 0, QUARTER, "x_scales_1_0")
         quantize_x(0, 0, J)
         interleave_wg("scalar", 0, 0)
-        interleave_wg("scalar", 0, 1)
         quantize_wg(0, 0)
-        quantize_wg(0, 1)
+        interleave_wg("scalar", 0, 1, "wg_bf_0_0")
         gather(1, 2, 0, LATE)
+        quantize_wg(0, 1)
         for c in range(HALF // CHUNK):
             open_up(c, 4 + c)
         for g in range(HALF // QUARTER):

@@ -399,11 +399,11 @@ def tile_list_tanh_none_kernel(
         quantize_x(1, 0, 128)
         quantize_x(1, 128, 256)
         interleave_wg("vector", 1, 0)
-        quantize_x_quarter(1)
-        quantize_wg(1, 0)
         interleave_wg("vector", 1, 1)
-        quantize_x_quarter(2)
+        quantize_wg(1, 0)
         quantize_wg(1, 1)
+        quantize_x_quarter(1)
+        quantize_x_quarter(2)
         gate_pass(0, 0, 1)
         gate_pass(0, 1, 1)
         up_pass(0, 1)

@@ -62,7 +62,6 @@ def tile_list_tanh_none_kernel(
         wu_sc = sbuf([P, PASSES, R], U8, "wu_sc")
         wd_codes = sbuf([P, N], I32, "wd_codes")
         wd_sc = sbuf([P, N], U8, "wd_sc")
-        tanh_ga = {}
         h_bf = sbuf([P, J, PACK], BF16, "h_bf")
         h_codes = sbuf([P, J], U32, "h_codes")
         h_scales = sbuf([P, J], U8, "h_scales")
@@ -74,6 +73,7 @@ def tile_list_tanh_none_kernel(
         x_mx = {}
         wg_bf = {}
         wg_scales = {}
+        tanh_ga = {}
         ub = {}
         ga = {}
         y_banks = {}
@@ -142,8 +142,8 @@ def tile_list_tanh_none_kernel(
                 op=MULT,
             )
 
-        def new_x_bf(a, j0, j1, name=None):
-            tile = sbuf([P, j1 - j0, PACK], BF16, name or "x_bf_%d_%d" % (a, j0))
+        def new_x_bf(a, j0, j1):
+            tile = sbuf([P, j1 - j0, PACK], BF16, "x_bf_%d_%d" % (a, j0))
             for j in range(j0, j1, CHUNK):
                 x_bf[a, j] = (tile, j0)
 
@@ -156,23 +156,6 @@ def tile_list_tanh_none_kernel(
                 engine,
                 x_bf_cols(a, j0, j1).rearrange("p (c e) i -> p c i e", e=4),
                 picked(a, j0, j1).rearrange("p i (c e) -> p c i e", e=4),
-            )
-
-        def interleave_pair(engine, a, i, j0, j1):
-            copy_on(
-                engine,
-                x_bf_cols(a, j0, j1).rearrange("p (c e) i -> p c i e", e=4)[:, :, i : i + 2, :],
-                picked(a, j0, j1).rearrange("p i (c e) -> p c i e", e=4)[:, :, i : i + 2, :],
-            )
-
-        def interleave_pair_on_gpsimd(a, i, j0, j1):
-            nc.gpsimd.tensor_scalar(
-                out=x_bf_cols(a, j0, j1)[:, :, i : i + 2],
-                in0=picked(a, j0, j1).rearrange("p i j -> p j i")[:, :, i : i + 2],
-                scalar1=1.0,
-                scalar2=0.0,
-                op0=MULT,
-                op1=ADD,
             )
 
         def interleave_x_on_gpsimd(a, j0, j1):
@@ -204,8 +187,8 @@ def tile_list_tanh_none_kernel(
             new_x_mx(1, j0, j1, "x_scales_1_%d" % j0)
             quantize_x(1, j0, j1)
 
-        def interleave_wg(engine, a, u, name=None):
-            wg_bf[a, u] = sbuf([P, 2 * P * PACK], BF16, name or "wg_bf_%d_%d" % (a, u))
+        def interleave_wg(engine, a, u, name):
+            wg_bf[a, u] = sbuf([P, 2 * P * PACK], BF16, name)
             copy_on(
                 engine,
                 wg_bf[a, u][:].rearrange("p (t m i) -> p m i t", t=2, i=PACK),
@@ -255,41 +238,22 @@ def tile_list_tanh_none_kernel(
             ga[g, u] = bank(b, [P, 2, QUARTER])
             gate_pass(g, u, 0)
 
-        def up_quarter(g, first_bank):
-            for v in range(2):
-                open_up(2 * g + v, first_bank + v)
-                up_pass(2 * g + v, 1)
-
-        def gate_quarter(g, first_bank):
-            for u in range(2):
-                open_gate(g, u, first_bank + u)
-                gate_pass(g, u, 1)
-
-        def tanh_quarter(g):
-            for u in range(2):
-                nc.scalar.activation(out=tanh_ga[g][:, 2 * u : 2 * u + 2, :], in_=ga[g, u][:], func=TANH)
-
-        def tanh_pair(g, u, name=None):
-            if g not in tanh_ga:
-                tanh_ga[g] = sbuf([P, PACK, QUARTER], F32, name or "tanh_ga_%d" % g)
-            nc.scalar.activation(out=tanh_ga[g][:, 2 * u : 2 * u + 2, :], in_=ga[g, u][:], func=TANH)
-
-        def gate_both(g, u, b):
-            open_gate(g, u, b)
-            gate_pass(g, u, 1)
-
-        def up_both(c, b):
+        def up(c, b):
             open_up(c, b)
             up_pass(c, 1)
 
-        def park_up(c):
-            parked = sbuf([P, PACK, CHUNK], F32, "ub_parked_%d" % c)
-            nc.scalar.copy(out=parked[:], in_=ub[c][:])
-            ub[c] = parked
+        def gate(g, u, b):
+            open_gate(g, u, b)
+            gate_pass(g, u, 1)
 
-        def hidden(c, engine=None):
+        def tanh_quarter(g):
+            tanh_ga[g] = sbuf([P, PACK, QUARTER], F32, "tanh_ga_%d" % g)
+            for u in range(2):
+                nc.scalar.activation(out=tanh_ga[g][:, 2 * u : 2 * u + 2, :], in_=ga[g, u][:], func=TANH)
+
+        def hidden(c):
             j0 = c % 2 * CHUNK
-            (engine or nc.vector).tensor_tensor(
+            nc.vector.tensor_tensor(
                 out=h_bf[:, c * CHUNK : (c + 1) * CHUNK, :].rearrange("p (d e) t -> p d t e", e=4),
                 in0=ub[c][:].rearrange("p t (d e) -> p d t e", e=4),
                 in1=tanh_ga[c // 2][:, :, j0 : j0 + CHUNK].rearrange("p t (d e) -> p d t e", e=4),
@@ -317,19 +281,14 @@ def tile_list_tanh_none_kernel(
                     stop=True,
                 )
 
-        def down_quarter(g, first_bank):
-            for u in range(2):
-                down(first_bank + u, 2 * u, 2 * u + 2, g * QUARTER, (g + 1) * QUARTER)
+        def down_pair(g, u, b):
+            down(b, 2 * u, 2 * u + 2, g * QUARTER, (g + 1) * QUARTER)
 
         def store(engine, q0, j0):
             acc, blocks, picks = y_banks[q0, j0]
             y = sbuf([P, blocks, picks], F32, "y_%d_%d" % (q0, j0))
             copy_on(engine, y[:], acc[:])
             nc.sync.dma_start(out=out_rows[:, q0 : q0 + blocks, j0 : j0 + picks], in_=y[:])
-
-        def store_quarter(g):
-            for u in range(2):
-                store("scalar", 2 * u, g * QUARTER)
 
         make_identity(nc, identity[:])
         nc.vector.memset(wu_sc_raw[:].rearrange("p a r -> p (a r)").bitcast(I32), 0)
@@ -359,7 +318,7 @@ def tile_list_tanh_none_kernel(
         reorder_wu()
         spread_wgt()
 
-        for j0, j1 in ((0, QUARTER), (QUARTER, HALF), (HALF, J)):
+        for j0, j1 in ((0, HALF), (HALF, J)):
             gather(0, 0, j0, j1)
         gather(0, 1, 0, J)
         gather(0, 2, 0, J)
@@ -370,10 +329,11 @@ def tile_list_tanh_none_kernel(
         for i in range(2):
             gather(1, i, 0, LATE)
             gather(1, i, LATE, J)
-        new_x_mx(0, 0, J, "x_scales_0")
+        new_x_mx(0, 0, LATE, "x_scales_0")
         new_x_mx(1, 0, QUARTER, "x_scales_1_0")
-        quantize_x(0, 0, J)
-        interleave_wg("scalar", 0, 0)
+        quantize_x(0, 0, HALF)
+        quantize_x(0, HALF, LATE)
+        interleave_wg("scalar", 0, 0, "wg_bf_0_0")
         quantize_wg(0, 0)
         interleave_wg("scalar", 0, 1, "wg_bf_0_0")
         gather(1, 2, 0, LATE)
@@ -384,87 +344,73 @@ def tile_list_tanh_none_kernel(
             for u in range(2):
                 open_gate(g, u, 2 * g + u)
 
-        gather(1, 3, 0, 128)
-        gather(1, 3, 128, 256)
-        gather(1, 3, 256, 512)
-        gather(1, 3, 512, 768)
-        new_x_bf(1, 0, 128)
-        interleave_x("scalar", 1, 0, 128)
-        new_x_bf(1, 128, 256)
-        interleave_x("scalar", 1, 128, 256)
-        new_x_bf(1, 256, 512)
-        interleave_x("scalar", 1, 256, 512)
-        new_x_bf(1, 512, 768)
-        interleave_x("scalar", 1, 512, 768)
-        quantize_x(1, 0, 128)
-        quantize_x(1, 128, 256)
-        interleave_wg("vector", 1, 0)
-        interleave_wg("vector", 1, 1)
-        quantize_wg(1, 0)
-        quantize_wg(1, 1)
+        pieces = ((0, CHUNK), (CHUNK, QUARTER), (QUARTER, HALF), (HALF, LATE))
+        for j0, j1 in pieces:
+            gather(1, 3, j0, j1)
+        for j0, j1 in pieces:
+            new_x_bf(1, j0, j1)
+            interleave_x("scalar", 1, j0, j1)
+        quantize_x(1, 0, CHUNK)
+        quantize_x(1, CHUNK, QUARTER)
+        for u in range(2):
+            interleave_wg("vector", 1, u, "wg_bf_1_%d" % u)
+        for u in range(2):
+            quantize_wg(1, u)
         quantize_x_quarter(1)
         quantize_x_quarter(2)
-        gate_pass(0, 0, 1)
-        gate_pass(0, 1, 1)
-        up_pass(0, 1)
-        up_pass(1, 1)
-        gate_pass(1, 0, 1)
-        gate_pass(1, 1, 1)
-        up_pass(2, 1)
-        up_pass(3, 1)
+        for g in range(HALF // QUARTER):
+            for u in range(2):
+                gate_pass(g, u, 1)
+            for v in range(2):
+                up_pass(2 * g + v, 1)
         gather(1, 2, LATE, J)
         gather(1, 3, LATE, J)
-        tanh_pair(0, 0)
-        tanh_pair(0, 1)
-        tanh_pair(1, 0)
-        tanh_pair(1, 1)
+        new_x_mx(0, LATE, J, "wg_bf_1_1")
+        quantize_x(0, LATE, J)
+        tanh_quarter(0)
+        tanh_quarter(1)
         new_x_bf(1, LATE, J)
         interleave_x_on_gpsimd(1, LATE, LATE + CHUNK)
         interleave_x("scalar", 1, LATE + CHUNK, J)
-        gate_both(2, 0, 0)
-        up_both(4, 2)
-        gate_both(2, 1, 1)
-        up_both(5, 3)
+
+        for u in range(2):
+            gate(2, u, u)
+        for v in range(2):
+            up(4 + v, 2 + v)
         hidden(0)
         hidden(1)
-        quantize_h(0, 128)
+        quantize_h(0, CHUNK)
         hidden(2)
-        quantize_h(128, 256)
+        quantize_h(CHUNK, QUARTER)
         hidden(3)
         quantize_x_quarter(3)
-        quantize_h(256, 512)
-        tanh_pair(2, 0)
-        tanh_pair(2, 1)
-        down(5, 0, 4, 0, 128)
-        down(6, 0, 4, 128, 256)
-        gate_both(3, 0, 0)
-        down(7, 0, 2, 256, 512)
-        gate_both(3, 1, 1)
+        quantize_h(QUARTER, HALF)
+        tanh_quarter(2)
+        down(5, 0, PACK, 0, CHUNK)
+        down(6, 0, PACK, CHUNK, QUARTER)
+        gate(3, 0, 0)
+        down_pair(1, 0, 7)
+        gate(3, 1, 1)
         store("scalar", 0, 0)
-        store("scalar", 0, 128)
-        down(5, 2, 4, 256, 512)
-        up_both(6, 4)
-        up_both(7, 6)
+        store("scalar", 0, CHUNK)
+        down_pair(1, 1, 5)
+        up(6, 4)
+        up(7, 6)
         hidden(4)
         hidden(5)
-        tanh_pair(3, 0)
-        tanh_pair(3, 1)
-        store("vector", 0, 256)
-        store("scalar", 2, 256)
-        quantize_h(512, 768)
-        down(2, 0, 2, 512, 768)
-        down(3, 2, 4, 512, 768)
+        tanh_quarter(3)
+        store("vector", 0, QUARTER)
+        store("scalar", 2, QUARTER)
+        quantize_h(HALF, LATE)
+        for u in range(2):
+            down_pair(2, u, 2 + u)
         hidden(6)
         hidden(7)
-        store("scalar", 0, 512)
-        store("scalar", 2, 512)
-        quantize_h(768, 896)
-        quantize_h(896, 1024)
-        down(7, 0, 1, 768, 1024)
-        down(0, 1, 2, 768, 1024)
-        down(1, 2, 3, 768, 1024)
-        down(5, 3, 4, 768, 1024)
-        store("vector", 0, 768)
-        store("scalar", 1, 768)
-        store("vector", 2, 768)
-        store("scalar", 3, 768)
+        for u in range(2):
+            store("scalar", 2 * u, HALF)
+        quantize_h(LATE, LATE + CHUNK)
+        quantize_h(LATE + CHUNK, J)
+        for q, b in enumerate((7, 0, 1, 5)):
+            down(b, q, q + 1, LATE, J)
+        for q in range(PACK):
+            store(("vector", "scalar")[q % 2], q, LATE)

@@ -26,6 +26,7 @@ CHUNK = 128
 QUARTER = 256
 HALF = 512
 LATE = J - QUARTER
+SPLIT = 64
 ALIGN = 256
 QUADRANTS = 4
 
@@ -49,11 +50,11 @@ def tile_list_tanh_none_kernel(
         planes = [[sbuf([P, T], F32, "plane_%d_%d" % (a, i)) for i in range(PACK)] for a in range(PASSES)]
         picked_0 = sbuf([P, PACK, J], F32, "picked_0")
         picked_1 = sbuf([P, PACK, LATE], F32, "picked_1")
-        late_and_wg = sbuf([P, 2 * QUARTER + PACK * R], F32, "late_and_wg")
-        picked_late = late_and_wg[:, : PACK * QUARTER].rearrange("p (i j) -> p i j", i=PACK)
-        wg_raw = [
-            sbuf([P, PACK, R], F32, "wg_raw_0")[:],
-            late_and_wg[:, 2 * QUARTER :].rearrange("p (i r) -> p i r", i=PACK),
+        wg_flat = [sbuf([P, PACK * R], F32, "wg_raw_%d" % a) for a in range(PASSES)]
+        wg_raw = [flat[:].rearrange("p (i r) -> p i r", i=PACK) for flat in wg_flat]
+        picked_late = [
+            sbuf([P, 2, QUARTER], F32, "picked_late")[:],
+            wg_flat[1][:, (PACK - 1) * R :].rearrange("p (i j) -> p i j", i=2),
         ]
         wg_codes = [sbuf([P, R], U32, "wg_codes_%d" % a) for a in range(PASSES)]
         wu_raw = sbuf([P, PASSES, 2 * R], U8, "wu_raw")
@@ -130,20 +131,18 @@ def tile_list_tanh_none_kernel(
         def picked(a, j0, j1):
             if a == 0:
                 return picked_0[:, :, j0:j1]
-            if j1 <= LATE:
-                return picked_1[:, :, j0:j1]
-            return picked_late[:, :, j0 - LATE : j1 - LATE]
+            return picked_1[:, :, j0:j1]
 
         def gather(a, i, j0, j1):
             nc.vector.tensor_tensor(
-                out=picked(a, j0, j1)[:, i, :],
+                out=picked_late[i // 2][:, i % 2, :] if (a, j0) == (1, LATE) else picked(a, j0, j1)[:, i, :],
                 in0=planes[a][i][:].indirect(offsets[:, j0 // 16 : j1 // 16]),
                 in1=wgt_sb[:, j0:j1],
                 op=MULT,
             )
 
-        def new_x_bf(a, j0, j1):
-            tile = sbuf([P, j1 - j0, PACK], BF16, "x_bf_%d_%d" % (a, j0))
+        def new_x_bf(a, j0, j1, name):
+            tile = sbuf([P, j1 - j0, PACK], BF16, name)
             for j in range(j0, j1, CHUNK):
                 x_bf[a, j] = (tile, j0)
 
@@ -158,15 +157,13 @@ def tile_list_tanh_none_kernel(
                 picked(a, j0, j1).rearrange("p i (c e) -> p c i e", e=4),
             )
 
-        def interleave_x_on_gpsimd(a, j0, j1):
-            nc.gpsimd.tensor_scalar(
-                out=x_bf_cols(a, j0, j1),
-                in0=picked(a, j0, j1).rearrange("p i j -> p j i"),
-                scalar1=1.0,
-                scalar2=0.0,
-                op0=MULT,
-                op1=ADD,
-            )
+        def lay_pair(engine, u, j0, j1):
+            dst = x_bf_cols(1, j0, j1)[:, :, 2 * u : 2 * u + 2]
+            src = picked_late[u].rearrange("p i j -> p j i")
+            if engine == "gpsimd":
+                nc.gpsimd.tensor_scalar(out=dst, in0=src, scalar1=1.0, scalar2=0.0, op0=MULT, op1=ADD)
+            else:
+                copy_on(engine, dst, src)
 
         def new_x_mx(a, j0, j1, scales_name):
             codes = sbuf([P, j1 - j0], U32, "x_codes_%d_%d" % (a, j0))
@@ -182,17 +179,19 @@ def tile_list_tanh_none_kernel(
             codes, scales = x_operand(a, j0, j1)
             nc.vector.quantize_mx(out=codes, scales=scales, in_=x_bf_cols(a, j0, j1).rearrange("p j i -> p (j i)"))
 
-        def quantize_x_quarter(g):
+        def quantize_x_quarter(g, scales_name):
             j0, j1 = g * QUARTER, (g + 1) * QUARTER
-            new_x_mx(1, j0, j1, "x_scales_1_%d" % j0)
+            new_x_mx(1, j0, j1, scales_name)
             quantize_x(1, j0, j1)
 
-        def interleave_wg(engine, a, u, name):
+        def new_wg_bf(a, u, name):
             wg_bf[a, u] = sbuf([P, 2 * P * PACK], BF16, name)
+
+        def interleave_wg(engine, a, u, m0, m1):
             copy_on(
                 engine,
-                wg_bf[a, u][:].rearrange("p (t m i) -> p m i t", t=2, i=PACK),
-                wg_raw[a].rearrange("p i (m t) -> p m i t", t=PACK)[:, :, :, 2 * u : 2 * u + 2],
+                wg_bf[a, u][:].rearrange("p (t m i) -> p m i t", t=2, i=PACK)[:, m0:m1, :, :],
+                wg_raw[a].rearrange("p i (m t) -> p m i t", t=PACK)[:, m0:m1, :, 2 * u : 2 * u + 2],
             )
 
         def quantize_wg(a, u):
@@ -322,7 +321,7 @@ def tile_list_tanh_none_kernel(
             gather(0, 0, j0, j1)
         gather(0, 1, 0, J)
         gather(0, 2, 0, J)
-        new_x_bf(0, 0, J)
+        new_x_bf(0, 0, J, "x_bf_0")
         for j0 in range(0, J, HALF):
             gather(0, 3, j0, j0 + HALF)
             interleave_x("scalar", 0, j0, j0 + HALF)
@@ -333,9 +332,13 @@ def tile_list_tanh_none_kernel(
         new_x_mx(1, 0, QUARTER, "x_scales_1_0")
         quantize_x(0, 0, HALF)
         quantize_x(0, HALF, LATE)
-        interleave_wg("scalar", 0, 0, "wg_bf_0_0")
+        new_wg_bf(0, 0, "wg_bf_0")
+        interleave_wg("scalar", 0, 0, 0, P)
         quantize_wg(0, 0)
-        interleave_wg("scalar", 0, 1, "wg_bf_0_0")
+        new_wg_bf(0, 1, "wg_bf_0")
+        interleave_wg("scalar", 0, 1, 0, P)
+        new_x_bf(1, LATE, J, "wg_raw_0")
+        lay_pair("scalar", 0, LATE, J)
         gather(1, 2, 0, LATE)
         quantize_wg(0, 1)
         for c in range(HALF // CHUNK):
@@ -347,17 +350,22 @@ def tile_list_tanh_none_kernel(
         pieces = ((0, CHUNK), (CHUNK, QUARTER), (QUARTER, HALF), (HALF, LATE))
         for j0, j1 in pieces:
             gather(1, 3, j0, j1)
-        for j0, j1 in pieces:
-            new_x_bf(1, j0, j1)
+        for j0, j1 in pieces[:3]:
+            new_x_bf(1, j0, j1, "x_bf_1_%d" % j0)
             interleave_x("scalar", 1, j0, j1)
         quantize_x(1, 0, CHUNK)
         quantize_x(1, CHUNK, QUARTER)
         for u in range(2):
-            interleave_wg("vector", 1, u, "wg_bf_1_%d" % u)
-        for u in range(2):
-            quantize_wg(1, u)
-        quantize_x_quarter(1)
-        quantize_x_quarter(2)
+            new_wg_bf(1, u, "wg_bf_1_%d" % u)
+        interleave_wg("vector", 1, 0, 0, P)
+        interleave_wg("vector", 1, 1, 0, SPLIT)
+        interleave_wg("scalar", 1, 1, SPLIT, P)
+        quantize_wg(1, 0)
+        quantize_x_quarter(1, "x_scales_1_1")
+        quantize_wg(1, 1)
+        for j0 in range(HALF, LATE, CHUNK):
+            x_bf[1, j0] = (wg_flat[1][:, :R].bitcast(BF16).rearrange("p (j i) -> p j i", i=PACK), HALF)
+            interleave_x("scalar", 1, j0, j0 + CHUNK)
         for g in range(HALF // QUARTER):
             for u in range(2):
                 gate_pass(g, u, 1)
@@ -365,13 +373,12 @@ def tile_list_tanh_none_kernel(
                 up_pass(2 * g + v, 1)
         gather(1, 2, LATE, J)
         gather(1, 3, LATE, J)
+        quantize_x_quarter(2, "x_scales_1_2")
         new_x_mx(0, LATE, J, "wg_bf_1_1")
         quantize_x(0, LATE, J)
         tanh_quarter(0)
         tanh_quarter(1)
-        new_x_bf(1, LATE, J)
-        interleave_x_on_gpsimd(1, LATE, LATE + CHUNK)
-        interleave_x("scalar", 1, LATE + CHUNK, J)
+        lay_pair("gpsimd", 1, LATE, J)
 
         for u in range(2):
             gate(2, u, u)
@@ -383,7 +390,7 @@ def tile_list_tanh_none_kernel(
         hidden(2)
         quantize_h(CHUNK, QUARTER)
         hidden(3)
-        quantize_x_quarter(3)
+        quantize_x_quarter(3, "tanh_ga_0")
         quantize_h(QUARTER, HALF)
         tanh_quarter(2)
         down(5, 0, PACK, 0, CHUNK)

@@ -37,6 +37,7 @@ def tile_list_tanh_none_kernel(
     nc = tc.nc
     with ExitStack() as ctx:
         keep = ctx.enter_context(tc.tile_pool(name="keep", bufs=1))
+        shared = ctx.enter_context(tc.tile_pool(name="shared", bufs=1))
         psum = ctx.enter_context(tc.psum_pool(name="psum", bufs=1))
 
         def sbuf(shape, dtype, name):
@@ -50,7 +51,10 @@ def tile_list_tanh_none_kernel(
         planes = [[sbuf([P, T], F32, "plane_%d_%d" % (a, i)) for i in range(PACK)] for a in range(PASSES)]
         picked_0 = sbuf([P, PACK, J], F32, "picked_0")
         picked_1 = sbuf([P, PACK, LATE], F32, "picked_1")
-        wg_flat = [sbuf([P, PACK * R], F32, "wg_raw_%d" % a) for a in range(PASSES)]
+        wg_flat = [
+            shared.tile([P, PACK * R], F32, name="wg_raw_0", offset=0, align_bytes=ALIGN),
+            sbuf([P, PACK * R], F32, "wg_raw_1"),
+        ]
         wg_raw = [flat[:].rearrange("p (i r) -> p i r", i=PACK) for flat in wg_flat]
         picked_late = [
             sbuf([P, 2, QUARTER], F32, "picked_late")[:],
@@ -75,6 +79,7 @@ def tile_list_tanh_none_kernel(
         wg_bf = {}
         wg_scales = {}
         tanh_ga = {}
+        first_sc = []
         ub = {}
         ga = {}
         y_banks = {}
@@ -102,8 +107,12 @@ def tile_list_tanh_none_kernel(
                     in_=wu_raw[:, a, :].bitcast(U16).rearrange("p (m t) -> p m t", t=PACK),
                 )
             nc.vector.tensor_copy(
-                out=wu_sc[:].rearrange("p a (t m) -> p a m t", t=PACK),
-                in_=wu_sc_raw[:].rearrange("p a (m t) -> p a m t", t=PACK),
+                out=wu_sc[:, 0, P:].rearrange("p (t m) -> p m t", t=PACK - 1),
+                in_=wu_sc_raw[:, 0, :].rearrange("p (m t) -> p m t", t=PACK)[:, :, 1:],
+            )
+            nc.vector.tensor_copy(
+                out=wu_sc[:, 1, :].rearrange("p (t m) -> p m t", t=PACK),
+                in_=wu_sc_raw[:, 1, :].rearrange("p (m t) -> p m t", t=PACK),
             )
 
         def spread_wgt():
@@ -208,7 +217,7 @@ def tile_list_tanh_none_kernel(
                 nc.tensor.matmul_mx(
                     out=ub[c][:, t, :],
                     lhsT=wu_codes[:, a, 2 * P * t : 2 * P * (t + 1)].bitcast(FP4X4),
-                    lhsT_scale=wu_sc[:, a, P * t : P * (t + 1)],
+                    lhsT_scale=first_sc[0][:] if (a, t) == (0, 0) else wu_sc[:, a, P * t : P * (t + 1)],
                     rhs=codes,
                     rhs_scale=scales,
                     start=(a == 0 and t == 0),
@@ -337,15 +346,19 @@ def tile_list_tanh_none_kernel(
         quantize_wg(0, 0)
         new_wg_bf(0, 1, "wg_bf_0")
         interleave_wg("scalar", 0, 1, 0, P)
-        new_x_bf(1, LATE, J, "wg_raw_0")
+        late_bf = shared.tile([P, QUARTER, PACK], BF16, name="late_bf", offset=0, align_bytes=ALIGN)
+        for j0 in range(LATE, J, CHUNK):
+            x_bf[1, j0] = (late_bf, LATE)
         lay_pair("scalar", 0, LATE, J)
         gather(1, 2, 0, LATE)
+        first_sc.append(shared.tile([P, P], U8, name="first_sc", offset=4096, align_bytes=ALIGN))
+        nc.vector.tensor_copy(out=first_sc[0][:], in_=wu_sc_raw[:, 0, :].rearrange("p (m t) -> p m t", t=PACK)[:, :, 0])
         quantize_wg(0, 1)
-        for c in range(HALF // CHUNK):
-            open_up(c, 4 + c)
         for g in range(HALF // QUARTER):
             for u in range(2):
                 open_gate(g, u, 2 * g + u)
+        for c in range(HALF // CHUNK):
+            open_up(c, 4 + c)
 
         pieces = ((0, CHUNK), (CHUNK, QUARTER), (QUARTER, HALF), (HALF, LATE))
         for j0, j1 in pieces:

@@ -27,6 +27,9 @@ QUARTER = 256
 HALF = 512
 LATE = J - QUARTER
 SPLIT = 64
+PAGE = 4096
+SKEW = 1088
+PITCH = 1200
 ALIGN = 256
 QUADRANTS = 4
 
@@ -38,26 +41,30 @@ def tile_list_tanh_none_kernel(
     with ExitStack() as ctx:
         keep = ctx.enter_context(tc.tile_pool(name="keep", bufs=1))
         shared = ctx.enter_context(tc.tile_pool(name="shared", bufs=1))
+        placed = ctx.enter_context(tc.tile_pool(name="placed", bufs=1))
         psum = ctx.enter_context(tc.psum_pool(name="psum", bufs=1))
 
         def sbuf(shape, dtype, name):
             return keep.tile(shape, dtype, name=name, tag=name, align_bytes=ALIGN)
 
+        def place(shape, name, offset):
+            return placed.tile(shape, F32, name=name, offset=offset, align_bytes=ALIGN if offset % ALIGN == 0 else 64)
+
         def bank(b, shape):
             return psum.tile(shape, F32, name="bank_%d" % b, tag="bank_%d" % b)
 
         offsets = keep.tile([P, J // 16], U16, name="offsets")
-        wgt_sb = sbuf([P, J], F32, "wgt_sb")
+        wgt_sb = place([P, J], "wgt_sb", 0)
         planes = [[sbuf([P, T], F32, "plane_%d_%d" % (a, i)) for i in range(PACK)] for a in range(PASSES)]
-        picked_0 = sbuf([P, PACK, J], F32, "picked_0")
-        picked_1 = sbuf([P, PACK, LATE], F32, "picked_1")
+        picked_0 = place([P, PACK, PITCH], "picked_0", PAGE + SKEW)
+        picked_1 = place([P, PACK, PITCH], "picked_1", 6 * PAGE + SKEW)
         wg_flat = [
             shared.tile([P, PACK * R], F32, name="wg_raw_0", offset=0, align_bytes=ALIGN),
-            sbuf([P, PACK * R], F32, "wg_raw_1"),
+            place([P, PACK * R], "wg_raw_1", 11 * PAGE + 2304),
         ]
         wg_raw = [flat[:].rearrange("p (i r) -> p i r", i=PACK) for flat in wg_flat]
         picked_late = [
-            sbuf([P, 2, QUARTER], F32, "picked_late")[:],
+            place([P, 2, QUARTER], "picked_late", 14 * PAGE + 64)[:],
             wg_flat[1][:, (PACK - 1) * R :].rearrange("p (i j) -> p i j", i=2),
         ]
         wg_codes = [sbuf([P, R], U32, "wg_codes_%d" % a) for a in range(PASSES)]

@@ -27,10 +27,9 @@ QUARTER = 256
 HALF = 512
 LATE = J - QUARTER
 SPLIT = 64
-PAGE = 4096
-SKEW = 1088
 PITCH = 1200
 ALIGN = 256
+LATE_BF_BYTES = 4096
 QUADRANTS = 4
 
 
@@ -41,30 +40,26 @@ def tile_list_tanh_none_kernel(
     with ExitStack() as ctx:
         keep = ctx.enter_context(tc.tile_pool(name="keep", bufs=1))
         shared = ctx.enter_context(tc.tile_pool(name="shared", bufs=1))
-        placed = ctx.enter_context(tc.tile_pool(name="placed", bufs=1))
         psum = ctx.enter_context(tc.psum_pool(name="psum", bufs=1))
 
         def sbuf(shape, dtype, name):
             return keep.tile(shape, dtype, name=name, tag=name, align_bytes=ALIGN)
 
-        def place(shape, name, offset):
-            return placed.tile(shape, F32, name=name, offset=offset, align_bytes=ALIGN if offset % ALIGN == 0 else 64)
+        def on_wg_0(shape, dtype, name, offset):
+            return shared.tile(shape, dtype, name=name, offset=offset, align_bytes=ALIGN)
 
         def bank(b, shape):
             return psum.tile(shape, F32, name="bank_%d" % b, tag="bank_%d" % b)
 
         offsets = keep.tile([P, J // 16], U16, name="offsets")
-        wgt_sb = place([P, J], "wgt_sb", 0)
+        wgt_sb = sbuf([P, J], F32, "wgt_sb")
         planes = [[sbuf([P, T], F32, "plane_%d_%d" % (a, i)) for i in range(PACK)] for a in range(PASSES)]
-        picked_0 = place([P, PACK, PITCH], "picked_0", PAGE + SKEW)
-        picked_1 = place([P, PACK, PITCH], "picked_1", 6 * PAGE + SKEW)
-        wg_flat = [
-            shared.tile([P, PACK * R], F32, name="wg_raw_0", offset=0, align_bytes=ALIGN),
-            place([P, PACK * R], "wg_raw_1", 11 * PAGE + 2304),
-        ]
+        picked_0 = sbuf([P, PACK, J], F32, "picked_0")
+        picked_1 = sbuf([P, PACK, PITCH], F32, "picked_1")
+        wg_flat = [on_wg_0([P, PACK * R], F32, "wg_raw_0", 0), sbuf([P, PACK * R], F32, "wg_raw_1")]
         wg_raw = [flat[:].rearrange("p (i r) -> p i r", i=PACK) for flat in wg_flat]
         picked_late = [
-            place([P, 2, QUARTER], "picked_late", 14 * PAGE + 64)[:],
+            picked_1[:, :2, LATE:J],
             wg_flat[1][:, (PACK - 1) * R :].rearrange("p (i j) -> p i j", i=2),
         ]
         wg_codes = [sbuf([P, R], U32, "wg_codes_%d" % a) for a in range(PASSES)]
@@ -86,7 +81,7 @@ def tile_list_tanh_none_kernel(
         wg_bf = {}
         wg_scales = {}
         tanh_ga = {}
-        first_sc = []
+        wu_scale_of = {(a, t): wu_sc[:, a, P * t : P * (t + 1)] for a in range(PASSES) for t in range(PACK) if a or t}
         ub = {}
         ga = {}
         y_banks = {}
@@ -122,6 +117,12 @@ def tile_list_tanh_none_kernel(
                 in_=wu_sc_raw[:, 1, :].rearrange("p (m t) -> p m t", t=PACK),
             )
 
+        def reorder_first_scales():
+            wu_scale_of[0, 0] = on_wg_0([P, P], U8, "wu_sc_first", LATE_BF_BYTES)[:]
+            nc.vector.tensor_copy(
+                out=wu_scale_of[0, 0], in_=wu_sc_raw[:, 0, :].rearrange("p (m t) -> p m t", t=PACK)[:, :, 0]
+            )
+
         def spread_wgt():
             by_pick = bank(0, [P, P])
             nc.tensor.transpose(out=by_pick[:], in_=wgt_rows[:], identity=identity[:])
@@ -145,26 +146,27 @@ def tile_list_tanh_none_kernel(
                 )
 
         def picked(a, j0, j1):
-            if a == 0:
-                return picked_0[:, :, j0:j1]
-            return picked_1[:, :, j0:j1]
+            return (picked_0, picked_1)[a][:, :, j0:j1]
 
         def gather(a, i, j0, j1):
+            is_late = (a, j0) == (1, LATE)
             nc.vector.tensor_tensor(
-                out=picked_late[i // 2][:, i % 2, :] if (a, j0) == (1, LATE) else picked(a, j0, j1)[:, i, :],
+                out=picked_late[i // 2][:, i % 2, :] if is_late else picked(a, j0, j1)[:, i, :],
                 in0=planes[a][i][:].indirect(offsets[:, j0 // 16 : j1 // 16]),
                 in1=wgt_sb[:, j0:j1],
                 op=MULT,
             )
 
-        def new_x_bf(a, j0, j1, name):
-            tile = sbuf([P, j1 - j0, PACK], BF16, name)
+        def use_x_bf(a, j0, j1, place):
             for j in range(j0, j1, CHUNK):
-                x_bf[a, j] = (tile, j0)
+                x_bf[a, j] = (place, j0)
+
+        def new_x_bf(a, j0, j1):
+            use_x_bf(a, j0, j1, sbuf([P, j1 - j0, PACK], BF16, "x_bf_%d_%d" % (a, j0))[:])
 
         def x_bf_cols(a, j0, j1):
-            tile, first = x_bf[a, j0]
-            return tile[:, j0 - first : j1 - first, :]
+            place, first = x_bf[a, j0]
+            return place[:, j0 - first : j1 - first, :]
 
         def interleave_x(engine, a, j0, j1):
             copy_on(
@@ -173,8 +175,8 @@ def tile_list_tanh_none_kernel(
                 picked(a, j0, j1).rearrange("p i (c e) -> p c i e", e=4),
             )
 
-        def lay_pair(engine, u, j0, j1):
-            dst = x_bf_cols(1, j0, j1)[:, :, 2 * u : 2 * u + 2]
+        def lay_late_pair(engine, u):
+            dst = x_bf_cols(1, LATE, J)[:, :, 2 * u : 2 * u + 2]
             src = picked_late[u].rearrange("p i j -> p j i")
             if engine == "gpsimd":
                 nc.gpsimd.tensor_scalar(out=dst, in0=src, scalar1=1.0, scalar2=0.0, op0=MULT, op1=ADD)
@@ -224,7 +226,7 @@ def tile_list_tanh_none_kernel(
                 nc.tensor.matmul_mx(
                     out=ub[c][:, t, :],
                     lhsT=wu_codes[:, a, 2 * P * t : 2 * P * (t + 1)].bitcast(FP4X4),
-                    lhsT_scale=first_sc[0][:] if (a, t) == (0, 0) else wu_sc[:, a, P * t : P * (t + 1)],
+                    lhsT_scale=wu_scale_of[a, t],
                     rhs=codes,
                     rhs_scale=scales,
                     start=(a == 0 and t == 0),
@@ -337,13 +339,12 @@ def tile_list_tanh_none_kernel(
             gather(0, 0, j0, j1)
         gather(0, 1, 0, J)
         gather(0, 2, 0, J)
-        new_x_bf(0, 0, J, "x_bf_0")
+        new_x_bf(0, 0, J)
         for j0 in range(0, J, HALF):
             gather(0, 3, j0, j0 + HALF)
             interleave_x("scalar", 0, j0, j0 + HALF)
         for i in range(2):
-            gather(1, i, 0, LATE)
-            gather(1, i, LATE, J)
+            gather(1, i, 0, J)
         new_x_mx(0, 0, LATE, "x_scales_0")
         new_x_mx(1, 0, QUARTER, "x_scales_1_0")
         quantize_x(0, 0, HALF)
@@ -353,13 +354,10 @@ def tile_list_tanh_none_kernel(
         quantize_wg(0, 0)
         new_wg_bf(0, 1, "wg_bf_0")
         interleave_wg("scalar", 0, 1, 0, P)
-        late_bf = shared.tile([P, QUARTER, PACK], BF16, name="late_bf", offset=0, align_bytes=ALIGN)
-        for j0 in range(LATE, J, CHUNK):
-            x_bf[1, j0] = (late_bf, LATE)
-        lay_pair("scalar", 0, LATE, J)
+        use_x_bf(1, LATE, J, on_wg_0([P, QUARTER, PACK], BF16, "x_bf_late", 0)[:])
+        lay_late_pair("scalar", 0)
         gather(1, 2, 0, LATE)
-        first_sc.append(shared.tile([P, P], U8, name="first_sc", offset=4096, align_bytes=ALIGN))
-        nc.vector.tensor_copy(out=first_sc[0][:], in_=wu_sc_raw[:, 0, :].rearrange("p (m t) -> p m t", t=PACK)[:, :, 0])
+        reorder_first_scales()
         quantize_wg(0, 1)
         for g in range(HALF // QUARTER):
             for u in range(2):
@@ -371,7 +369,7 @@ def tile_list_tanh_none_kernel(
         for j0, j1 in pieces:
             gather(1, 3, j0, j1)
         for j0, j1 in pieces[:3]:
-            new_x_bf(1, j0, j1, "x_bf_1_%d" % j0)
+            new_x_bf(1, j0, j1)
             interleave_x("scalar", 1, j0, j1)
         quantize_x(1, 0, CHUNK)
         quantize_x(1, CHUNK, QUARTER)
@@ -383,8 +381,8 @@ def tile_list_tanh_none_kernel(
         quantize_wg(1, 0)
         quantize_x_quarter(1, "x_scales_1_1")
         quantize_wg(1, 1)
+        use_x_bf(1, HALF, LATE, wg_flat[1][:, :R].bitcast(BF16).rearrange("p (j i) -> p j i", i=PACK))
         for j0 in range(HALF, LATE, CHUNK):
-            x_bf[1, j0] = (wg_flat[1][:, :R].bitcast(BF16).rearrange("p (j i) -> p j i", i=PACK), HALF)
             interleave_x("scalar", 1, j0, j0 + CHUNK)
         for g in range(HALF // QUARTER):
             for u in range(2):
@@ -398,7 +396,7 @@ def tile_list_tanh_none_kernel(
         quantize_x(0, LATE, J)
         tanh_quarter(0)
         tanh_quarter(1)
-        lay_pair("gpsimd", 1, LATE, J)
+        lay_late_pair("gpsimd", 1)
 
         for u in range(2):
             gate(2, u, u)
@@ -406,20 +404,19 @@ def tile_list_tanh_none_kernel(
             up(4 + v, 2 + v)
         hidden(0)
         hidden(1)
-        quantize_h(0, CHUNK)
         hidden(2)
-        quantize_h(CHUNK, QUARTER)
+        quantize_h(0, QUARTER)
         hidden(3)
         quantize_x_quarter(3, "tanh_ga_0")
         quantize_h(QUARTER, HALF)
         tanh_quarter(2)
-        down(5, 0, PACK, 0, CHUNK)
-        down(6, 0, PACK, CHUNK, QUARTER)
+        down_pair(0, 0, 5)
+        down_pair(0, 1, 6)
         gate(3, 0, 0)
         down_pair(1, 0, 7)
         gate(3, 1, 1)
         store("scalar", 0, 0)
-        store("scalar", 0, CHUNK)
+        store("scalar", 2, 0)
         down_pair(1, 1, 5)
         up(6, 4)
         up(7, 6)

@@ -72,6 +72,7 @@ def tile_list_tanh_none_kernel(
         h_bf = sbuf([P, J, PACK], BF16, "h_bf")
         h_codes = sbuf([P, J], U32, "h_codes")
         h_scales = sbuf([P, J], U8, "h_scales")
+        y_sb = [sbuf([P, PACK, QUARTER], F32, "y_%d" % g) for g in range(J // QUARTER)]
         wgt_rows = sbuf([P, P], F32, "wgt_rows")
         wgt_t = sbuf([P, J], F32, "wgt_t")
         identity = sbuf([P, P], F32, "identity")
@@ -81,7 +82,9 @@ def tile_list_tanh_none_kernel(
         wg_bf = {}
         wg_scales = {}
         tanh_ga = {}
-        wu_scale_of = {(a, t): wu_sc[:, a, P * t : P * (t + 1)] for a in range(PASSES) for t in range(PACK) if a or t}
+        wu_slice = {
+            (a, t): wu_codes[:, a, 2 * P * t : 2 * P * (t + 1)] for a in range(PASSES) for t in range(PACK) if a or t
+        }
         ub = {}
         ga = {}
         y_banks = {}
@@ -104,23 +107,22 @@ def tile_list_tanh_none_kernel(
 
         def reorder_wu():
             for a in range(PASSES):
+                t0 = 1 - a
                 nc.vector.tensor_copy(
-                    out=wu_codes[:, a, :].bitcast(U16).rearrange("p (t m) -> p m t", t=PACK),
-                    in_=wu_raw[:, a, :].bitcast(U16).rearrange("p (m t) -> p m t", t=PACK),
+                    out=wu_codes[:, a, 2 * P * t0 :].bitcast(U16).rearrange("p (t m) -> p m t", m=P),
+                    in_=wu_raw[:, a, :].bitcast(U16).rearrange("p (m t) -> p m t", t=PACK)[:, :, t0:],
                 )
-            nc.vector.tensor_copy(
-                out=wu_sc[:, 0, P:].rearrange("p (t m) -> p m t", t=PACK - 1),
-                in_=wu_sc_raw[:, 0, :].rearrange("p (m t) -> p m t", t=PACK)[:, :, 1:],
-            )
-            nc.vector.tensor_copy(
-                out=wu_sc[:, 1, :].rearrange("p (t m) -> p m t", t=PACK),
-                in_=wu_sc_raw[:, 1, :].rearrange("p (m t) -> p m t", t=PACK),
-            )
+            for a in range(PASSES):
+                nc.vector.tensor_copy(
+                    out=wu_sc[:, a, :].rearrange("p (t m) -> p m t", t=PACK),
+                    in_=wu_sc_raw[:, a, :].rearrange("p (m t) -> p m t", t=PACK),
+                )
 
-        def reorder_first_scales():
-            wu_scale_of[0, 0] = on_wg_0([P, P], U8, "wu_sc_first", LATE_BF_BYTES)[:]
-            nc.vector.tensor_copy(
-                out=wu_scale_of[0, 0], in_=wu_sc_raw[:, 0, :].rearrange("p (m t) -> p m t", t=PACK)[:, :, 0]
+        def reorder_first_words():
+            wu_slice[0, 0] = on_wg_0([P, 2 * P], U8, "wu_first", LATE_BF_BYTES)[:]
+            nc.scalar.copy(
+                out=wu_slice[0, 0].bitcast(U16),
+                in_=wu_raw[:, 0, :].bitcast(U16).rearrange("p (m t) -> p m t", t=PACK)[:, :, 0],
             )
 
         def spread_wgt():
@@ -225,8 +227,8 @@ def tile_list_tanh_none_kernel(
             for t in range(PACK):
                 nc.tensor.matmul_mx(
                     out=ub[c][:, t, :],
-                    lhsT=wu_codes[:, a, 2 * P * t : 2 * P * (t + 1)].bitcast(FP4X4),
-                    lhsT_scale=wu_scale_of[a, t],
+                    lhsT=wu_slice[a, t].bitcast(FP4X4),
+                    lhsT_scale=wu_sc[:, a, P * t : P * (t + 1)],
                     rhs=codes,
                     rhs_scale=scales,
                     start=(a == 0 and t == 0),
@@ -286,8 +288,8 @@ def tile_list_tanh_none_kernel(
 
         def down(b, q0, q1, j0, j1):
             acc = bank(b, [P, q1 - q0, j1 - j0])
-            y_banks[q0, j0] = (acc, q1 - q0, j1 - j0)
             for q in range(q0, q1):
+                y_banks[q, j0] = (acc, q0)
                 nc.tensor.matmul_mx(
                     out=acc[:, q - q0, :],
                     lhsT=wd_codes[:, P * q : P * (q + 1)].bitcast(FP8X4),
@@ -301,11 +303,12 @@ def tile_list_tanh_none_kernel(
         def down_pair(g, u, b):
             down(b, 2 * u, 2 * u + 2, g * QUARTER, (g + 1) * QUARTER)
 
-        def store(engine, q0, j0):
-            acc, blocks, picks = y_banks[q0, j0]
-            y = sbuf([P, blocks, picks], F32, "y_%d_%d" % (q0, j0))
-            copy_on(engine, y[:], acc[:])
-            nc.sync.dma_start(out=out_rows[:, q0 : q0 + blocks, j0 : j0 + picks], in_=y[:])
+        def empty(engine, q0, q1, j0):
+            acc, first = y_banks[q0, j0]
+            copy_on(engine, y_sb[j0 // QUARTER][:, q0:q1, :], acc[:, q0 - first : q1 - first, :])
+
+        def store(q0, q1, j0):
+            nc.sync.dma_start(out=out_rows[:, q0:q1, j0 : j0 + QUARTER], in_=y_sb[j0 // QUARTER][:, q0:q1, :])
 
         make_identity(nc, identity[:])
         nc.vector.memset(wu_sc_raw[:].rearrange("p a r -> p (a r)").bitcast(I32), 0)
@@ -357,7 +360,7 @@ def tile_list_tanh_none_kernel(
         use_x_bf(1, LATE, J, on_wg_0([P, QUARTER, PACK], BF16, "x_bf_late", 0)[:])
         lay_late_pair("scalar", 0)
         gather(1, 2, 0, LATE)
-        reorder_first_scales()
+        reorder_first_words()
         quantize_wg(0, 1)
         for g in range(HALF // QUARTER):
             for u in range(2):
@@ -415,26 +418,33 @@ def tile_list_tanh_none_kernel(
         gate(3, 0, 0)
         down_pair(1, 0, 7)
         gate(3, 1, 1)
-        store("scalar", 0, 0)
-        store("scalar", 2, 0)
+        empty("scalar", 0, 2, 0)
+        empty("scalar", 2, 4, 0)
+        store(0, 4, 0)
         down_pair(1, 1, 5)
         up(6, 4)
         up(7, 6)
         hidden(4)
+        empty("vector", 0, 2, QUARTER)
+        store(0, 2, QUARTER)
         hidden(5)
         tanh_quarter(3)
-        store("vector", 0, QUARTER)
-        store("scalar", 2, QUARTER)
-        quantize_h(HALF, LATE)
+        empty("scalar", 2, 4, QUARTER)
+        store(2, 4, QUARTER)
+        quantize_h(HALF, HALF + CHUNK)
+        quantize_h(HALF + CHUNK, LATE)
         for u in range(2):
             down_pair(2, u, 2 + u)
         hidden(6)
         hidden(7)
-        for u in range(2):
-            store("scalar", 2 * u, HALF)
+        for q in range(PACK):
+            empty("scalar", q, q + 1, HALF)
+            store(q, q + 1, HALF)
         quantize_h(LATE, LATE + CHUNK)
         quantize_h(LATE + CHUNK, J)
         for q, b in enumerate((7, 0, 1, 5)):
             down(b, q, q + 1, LATE, J)
         for q in range(PACK):
-            store(("vector", "scalar")[q % 2], q, LATE)
+            empty(("vector", "scalar")[q % 2], q, q + 1, LATE)
+        for q0, q1 in ((0, 1), (1, 2), (2, 4)):
+            store(q0, q1, LATE)

@@ -64,7 +64,6 @@ def tile_list_tanh_none_kernel(
         ]
         wg_codes = [sbuf([P, R], U32, "wg_codes_%d" % a) for a in range(PASSES)]
         wu_raw = sbuf([P, PASSES, 2 * R], U8, "wu_raw")
-        wu_codes = sbuf([P, PASSES, 2 * R], U8, "wu_codes")
         wu_sc_raw = sbuf([P, PASSES, R], U8, "wu_sc_raw")
         wu_sc = sbuf([P, PASSES, R], U8, "wu_sc")
         wd_codes = sbuf([P, N], I32, "wd_codes")
@@ -82,9 +81,7 @@ def tile_list_tanh_none_kernel(
         wg_bf = {}
         wg_scales = {}
         tanh_ga = {}
-        wu_slice = {
-            (a, t): wu_codes[:, a, 2 * P * t : 2 * P * (t + 1)] for a in range(PASSES) for t in range(PACK) if a or t
-        }
+        wu_slice = {}
         ub = {}
         ga = {}
         y_banks = {}
@@ -105,18 +102,23 @@ def tile_list_tanh_none_kernel(
         def load_wg(a):
             nc.sync.dma_start(out=wg_raw[a], in_=wg_rows[a])
 
-        def reorder_wu():
-            for a in range(PASSES):
-                t0 = 1 - a
-                nc.vector.tensor_copy(
-                    out=wu_codes[:, a, 2 * P * t0 :].bitcast(U16).rearrange("p (t m) -> p m t", m=P),
-                    in_=wu_raw[:, a, :].bitcast(U16).rearrange("p (m t) -> p m t", t=PACK)[:, :, t0:],
-                )
+        def reorder_wu_scales():
             for a in range(PASSES):
                 nc.vector.tensor_copy(
                     out=wu_sc[:, a, :].rearrange("p (t m) -> p m t", t=PACK),
                     in_=wu_sc_raw[:, a, :].rearrange("p (m t) -> p m t", t=PACK),
                 )
+
+        def reorder_wu_words():
+            wu_codes = sbuf([P, PASSES, 2 * R], U8, "plane_0_0")
+            for a in range(PASSES):
+                t0 = 1 - a
+                nc.scalar.copy(
+                    out=wu_codes[:, a, 2 * P * t0 :].bitcast(U16).rearrange("p (t m) -> p m t", m=P),
+                    in_=wu_raw[:, a, :].bitcast(U16).rearrange("p (m t) -> p m t", t=PACK)[:, :, t0:],
+                )
+                for t in range(t0, PACK):
+                    wu_slice[a, t] = wu_codes[:, a, 2 * P * t : 2 * P * (t + 1)]
 
         def reorder_first_words():
             wu_slice[0, 0] = on_wg_0([P, 2 * P], U8, "wu_first", LATE_BF_BYTES)[:]
@@ -303,26 +305,28 @@ def tile_list_tanh_none_kernel(
         def down_pair(g, u, b):
             down(b, 2 * u, 2 * u + 2, g * QUARTER, (g + 1) * QUARTER)
 
-        def empty(engine, q0, q1, j0):
+        def store(engine, q0, q1, j0):
             acc, first = y_banks[q0, j0]
             copy_on(engine, y_sb[j0 // QUARTER][:, q0:q1, :], acc[:, q0 - first : q1 - first, :])
-
-        def store(q0, q1, j0):
-            nc.sync.dma_start(out=out_rows[:, q0:q1, j0 : j0 + QUARTER], in_=y_sb[j0 // QUARTER][:, q0:q1, :])
+            for q in range(q0, q1):
+                nc.sync.dma_start(out=out_rows[:, q, j0 : j0 + QUARTER], in_=y_sb[j0 // QUARTER][:, q, :])
 
         make_identity(nc, identity[:])
         nc.vector.memset(wu_sc_raw[:].rearrange("p a r -> p (a r)").bitcast(I32), 0)
         nc.vector.memset(wd_sc[:].bitcast(I32), 0)
-        nc.sync.dma_start(offsets[:], offs)
         nc.sync.dma_start(out=wgt_rows[:], in_=wgt[::8, :].rearrange("q (b j) -> q b j", j=P))
-        nc.sync.dma_start(out=wu_raw[:].bitcast(I32), in_=wu_words.rearrange("a p b -> p a b").bitcast(I32))
+        nc.sync.dma_start(offsets[:], offs)
+        nc.sync.dma_start(out=planes[0][0][:, : T // 2], in_=x_rows[0, :, 0, : T // 2])
         for q in range(QUADRANTS):
             nc.sync.dma_start(
                 out=wu_sc_raw[32 * q : 32 * q + 4, :, :].bitcast(I32),
                 in_=wu_scales[:, 4 * q : 4 * q + 4, :].rearrange("a s r -> s a r").bitcast(I32),
             )
-        for i in range(PACK):
-            load_plane(0, i)
+        nc.sync.dma_start(out=planes[0][0][:, T // 2 :], in_=x_rows[0, :, 0, T // 2 :])
+        load_plane(0, 1)
+        nc.sync.dma_start(out=wu_raw[:].bitcast(I32), in_=wu_words.rearrange("a p b -> p a b").bitcast(I32))
+        load_plane(0, 2)
+        load_plane(0, 3)
         load_plane(1, 0)
         load_plane(1, 1)
         load_wg(0)
@@ -335,11 +339,12 @@ def tile_list_tanh_none_kernel(
                 out=wd_sc[32 * q : 32 * q + 4, :].bitcast(I32),
                 in_=wd_scales[0, 4 * q : 4 * q + 4, :].bitcast(I32),
             )
-        reorder_wu()
         spread_wgt()
+        reorder_wu_scales()
 
-        for j0, j1 in ((0, HALF), (HALF, J)):
+        for j0, j1 in ((0, QUARTER), (QUARTER, HALF), (HALF, J)):
             gather(0, 0, j0, j1)
+        reorder_wu_words()
         gather(0, 1, 0, J)
         gather(0, 2, 0, J)
         new_x_bf(0, 0, J)
@@ -348,10 +353,10 @@ def tile_list_tanh_none_kernel(
             interleave_x("scalar", 0, j0, j0 + HALF)
         for i in range(2):
             gather(1, i, 0, J)
-        new_x_mx(0, 0, LATE, "x_scales_0")
+        new_x_mx(0, 0, J, "x_scales_0")
         new_x_mx(1, 0, QUARTER, "x_scales_1_0")
-        quantize_x(0, 0, HALF)
-        quantize_x(0, HALF, LATE)
+        for j0 in range(0, J, HALF):
+            quantize_x(0, j0, j0 + HALF)
         new_wg_bf(0, 0, "wg_bf_0")
         interleave_wg("scalar", 0, 0, 0, P)
         quantize_wg(0, 0)
@@ -395,8 +400,6 @@ def tile_list_tanh_none_kernel(
         gather(1, 2, LATE, J)
         gather(1, 3, LATE, J)
         quantize_x_quarter(2, "x_scales_1_2")
-        new_x_mx(0, LATE, J, "wg_bf_1_1")
-        quantize_x(0, LATE, J)
         tanh_quarter(0)
         tanh_quarter(1)
         lay_late_pair("gpsimd", 1)
@@ -418,19 +421,16 @@ def tile_list_tanh_none_kernel(
         gate(3, 0, 0)
         down_pair(1, 0, 7)
         gate(3, 1, 1)
-        empty("scalar", 0, 2, 0)
-        empty("scalar", 2, 4, 0)
-        store(0, 4, 0)
+        store("scalar", 0, 2, 0)
+        store("scalar", 2, 4, 0)
         down_pair(1, 1, 5)
         up(6, 4)
         up(7, 6)
         hidden(4)
-        empty("vector", 0, 2, QUARTER)
-        store(0, 2, QUARTER)
+        store("vector", 0, 2, QUARTER)
         hidden(5)
         tanh_quarter(3)
-        empty("scalar", 2, 4, QUARTER)
-        store(2, 4, QUARTER)
+        store("scalar", 2, 4, QUARTER)
         quantize_h(HALF, HALF + CHUNK)
         quantize_h(HALF + CHUNK, LATE)
         for u in range(2):
@@ -438,13 +438,10 @@ def tile_list_tanh_none_kernel(
         hidden(6)
         hidden(7)
         for q in range(PACK):
-            empty("scalar", q, q + 1, HALF)
-            store(q, q + 1, HALF)
+            store("scalar", q, q + 1, HALF)
         quantize_h(LATE, LATE + CHUNK)
         quantize_h(LATE + CHUNK, J)
         for q, b in enumerate((7, 0, 1, 5)):
             down(b, q, q + 1, LATE, J)
         for q in range(PACK):
-            empty(("vector", "scalar")[q % 2], q, q + 1, LATE)
-        for q0, q1 in ((0, 1), (1, 2), (2, 4)):
-            store(q0, q1, LATE)
+            store(("vector", "scalar")[q % 2], q, q + 1, LATE)

from contextlib import ExitStack

import concourse.mybir as mybir
from concourse.masks import make_identity

K, R, N, T, J = 1024, 512, 512, 2048, 1024
FLOPS = 2 * K * R * J * 2 + 2 * R * N * J

F32 = mybir.dt.float32
BF16 = mybir.dt.bfloat16
I32 = mybir.dt.int32
U32 = mybir.dt.uint32
U16 = mybir.dt.uint16
U8 = mybir.dt.uint8
FP8X4 = mybir.dt.float8_e4m3fn_x4
FP4X4 = mybir.dt.float4_e2m1fn_x4
MULT = mybir.AluOpType.mult
ADD = mybir.AluOpType.add
TANH = mybir.ActivationFunctionType.Tanh
COPY = mybir.ActivationFunctionType.Copy

P = 128
PACK = 4
PASSES = K // (P * PACK)
CHUNK = 128
QUARTER = 256
HALF = 512
LATE = J - QUARTER
SPLIT = 64
PITCH = 1200
ALIGN = 256
LATE_BF_BYTES = 4096
QUADRANTS = 4


def tile_list_tanh_none_kernel(
    tc, xT, wgt, wg, wu_words, wu_scales, wd_words, wd_scales, offs, out
):
    nc = tc.nc
    with ExitStack() as ctx:
        keep = ctx.enter_context(tc.tile_pool(name="keep", bufs=1))
        shared = ctx.enter_context(tc.tile_pool(name="shared", bufs=1))
        psum = ctx.enter_context(tc.psum_pool(name="psum", bufs=1))

        def sbuf(shape, dtype, name):
            return keep.tile(shape, dtype, name=name, tag=name, align_bytes=ALIGN)

        def on_wg_0(shape, dtype, name, offset):
            return shared.tile(shape, dtype, name=name, offset=offset, align_bytes=ALIGN)

        def bank(b, shape):
            return psum.tile(shape, F32, name="bank_%d" % b, tag="bank_%d" % b)

        offsets = keep.tile([P, J // 16], U16, name="offsets")
        wgt_sb = sbuf([P, J], F32, "wgt_sb")
        planes = [[sbuf([P, T], F32, "plane_%d_%d" % (a, i)) for i in range(PACK)] for a in range(PASSES)]
        picked_0 = sbuf([P, PACK, J], F32, "picked_0")
        picked_1 = sbuf([P, PACK, PITCH], F32, "picked_1")
        wg_flat = [on_wg_0([P, PACK * R], F32, "wg_raw_0", 0), sbuf([P, PACK * R], F32, "wg_raw_1")]
        wg_raw = [flat[:].rearrange("p (i r) -> p i r", i=PACK) for flat in wg_flat]
        picked_late = [
            picked_1[:, :2, LATE:J],
            wg_flat[1][:, (PACK - 1) * R :].rearrange("p (i j) -> p i j", i=2),
        ]
        wg_codes = [sbuf([P, R], U32, "wg_codes_%d" % a) for a in range(PASSES)]
        wu_raw = sbuf([P, PASSES, 2 * R], U8, "wu_raw")
        wu_sc_raw = sbuf([P, PASSES, R], U8, "wu_sc_raw")
        wu_sc = sbuf([P, PASSES, R], U8, "wu_sc")
        wd_codes = sbuf([P, N], I32, "wd_codes")
        wd_sc = sbuf([P, N], U8, "wd_sc")
        h_bf = sbuf([P, J, PACK], BF16, "h_bf")
        h_codes = sbuf([P, J], U32, "h_codes")
        h_scales = sbuf([P, J], U8, "h_scales")
        y_sb = [sbuf([P, PACK, QUARTER], F32, "y_%d" % g) for g in range(J // QUARTER)]
        wgt_rows = sbuf([P, P], F32, "wgt_rows")
        wgt_t = sbuf([P, J], F32, "wgt_t")
        identity = sbuf([P, P], F32, "identity")

        x_bf = {}
        x_mx = {}
        wg_bf = {}
        wg_scales = {}
        tanh_ga = {}
        wu_slice = {}
        ub = {}
        ga = {}
        y_banks = {}

        x_rows = xT.rearrange("(a p i) t -> a p i t", p=P, i=PACK)
        wg_rows = wg.rearrange("(a p i) r -> a p i r", p=P, i=PACK)
        out_rows = out.rearrange("(q p) j -> p q j", p=P)

        def copy_on(engine, dst, src):
            if engine == "scalar":
                nc.scalar.copy(out=dst, in_=src)
            else:
                nc.vector.tensor_copy(out=dst, in_=src)

        def load_plane(a, i):
            nc.sync.dma_start(out=planes[a][i][:], in_=x_rows[a, :, i, :])

        def load_wg(a):
            nc.sync.dma_start(out=wg_raw[a], in_=wg_rows[a])

        def reorder_wu_scales():
            for a in range(PASSES):
                nc.vector.tensor_copy(
                    out=wu_sc[:, a, :].rearrange("p (t m) -> p m t", t=PACK),
                    in_=wu_sc_raw[:, a, :].rearrange("p (m t) -> p m t", t=PACK),
                )

        def reorder_wu_words():
            wu_codes = sbuf([P, PASSES, 2 * R], U8, "plane_0_0")
            for a in range(PASSES):
                t0 = 1 - a
                nc.scalar.copy(
                    out=wu_codes[:, a, 2 * P * t0 :].bitcast(U16).rearrange("p (t m) -> p m t", m=P),
                    in_=wu_raw[:, a, :].bitcast(U16).rearrange("p (m t) -> p m t", t=PACK)[:, :, t0:],
                )
                for t in range(t0, PACK):
                    wu_slice[a, t] = wu_codes[:, a, 2 * P * t : 2 * P * (t + 1)]

        def reorder_first_words():
            wu_slice[0, 0] = on_wg_0([P, 2 * P], U8, "wu_first", LATE_BF_BYTES)[:]
            nc.scalar.copy(
                out=wu_slice[0, 0].bitcast(U16),
                in_=wu_raw[:, 0, :].bitcast(U16).rearrange("p (m t) -> p m t", t=PACK)[:, :, 0],
            )

        def spread_wgt():
            by_pick = bank(0, [P, P])
            nc.tensor.transpose(out=by_pick[:], in_=wgt_rows[:], identity=identity[:])
            blocks = QUARTER // P
            for g in range(J // QUARTER):
                nc.scalar.activation(
                    func=COPY,
                    out=wgt_t[:, g * QUARTER : (g + 1) * QUARTER].rearrange("p (b q r) -> p b q r", q=16, r=8),
                    in_=by_pick[:]
                    .rearrange("p (q b) -> p b q", b=8)[:, g * blocks : (g + 1) * blocks, :]
                    .unsqueeze(3)
                    .to_broadcast([P, blocks, 16, 8]),
                )
            for g in range(J // QUARTER):
                by_row = bank(4 + g, [P, blocks, P])
                for b in range(blocks):
                    j0 = g * QUARTER + b * P
                    nc.tensor.transpose(out=by_row[:, b, :], in_=wgt_t[:, j0 : j0 + P], identity=identity[:])
                nc.scalar.copy(
                    out=wgt_sb[:, g * QUARTER : (g + 1) * QUARTER], in_=by_row[:].rearrange("p b j -> p (b j)")
                )

        def picked(a, j0, j1):
            return (picked_0, picked_1)[a][:, :, j0:j1]

        def gather(a, i, j0, j1):
            is_late = (a, j0) == (1, LATE)
            nc.vector.tensor_tensor(
                out=picked_late[i // 2][:, i % 2, :] if is_late else picked(a, j0, j1)[:, i, :],
                in0=planes[a][i][:].indirect(offsets[:, j0 // 16 : j1 // 16]),
                in1=wgt_sb[:, j0:j1],
                op=MULT,
            )

        def use_x_bf(a, j0, j1, place):
            for j in range(j0, j1, CHUNK):
                x_bf[a, j] = (place, j0)

        def new_x_bf(a, j0, j1):
            use_x_bf(a, j0, j1, sbuf([P, j1 - j0, PACK], BF16, "x_bf_%d_%d" % (a, j0))[:])

        def x_bf_cols(a, j0, j1):
            place, first = x_bf[a, j0]
            return place[:, j0 - first : j1 - first, :]

        def interleave_x(engine, a, j0, j1):
            copy_on(
                engine,
                x_bf_cols(a, j0, j1).rearrange("p (c e) i -> p c i e", e=4),
                picked(a, j0, j1).rearrange("p i (c e) -> p c i e", e=4),
            )

        def lay_late_pair(engine, u):
            dst = x_bf_cols(1, LATE, J)[:, :, 2 * u : 2 * u + 2]
            src = picked_late[u].rearrange("p i j -> p j i")
            if engine == "gpsimd":
                nc.gpsimd.tensor_scalar(out=dst, in0=src, scalar1=1.0, scalar2=0.0, op0=MULT, op1=ADD)
            else:
                copy_on(engine, dst, src)

        def new_x_mx(a, j0, j1, scales_name):
            codes = sbuf([P, j1 - j0], U32, "x_codes_%d_%d" % (a, j0))
            scales = sbuf([P, j1 - j0], U8, scales_name)
            for j in range(j0, j1, CHUNK):
                x_mx[a, j] = (codes, scales, j0)

        def x_operand(a, j0, j1):
            codes, scales, first = x_mx[a, j0]
            return codes[:, j0 - first : j1 - first].bitcast(FP8X4), scales[:, j0 - first : j1 - first]

        def quantize_x(a, j0, j1):
            codes, scales = x_operand(a, j0, j1)
            nc.vector.quantize_mx(out=codes, scales=scales, in_=x_bf_cols(a, j0, j1).rearrange("p j i -> p (j i)"))

        def quantize_x_quarter(g, scales_name):
            j0, j1 = g * QUARTER, (g + 1) * QUARTER
            new_x_mx(1, j0, j1, scales_name)
            quantize_x(1, j0, j1)

        def new_wg_bf(a, u, name):
            wg_bf[a, u] = sbuf([P, 2 * P * PACK], BF16, name)

        def interleave_wg(engine, a, u, m0, m1):
            copy_on(
                engine,
                wg_bf[a, u][:].rearrange("p (t m i) -> p m i t", t=2, i=PACK)[:, m0:m1, :, :],
                wg_raw[a].rearrange("p i (m t) -> p m i t", t=PACK)[:, m0:m1, :, 2 * u : 2 * u + 2],
            )

        def quantize_wg(a, u):
            wg_scales[a, u] = sbuf([P, 2 * P], U8, "wg_scales_%d_%d" % (a, u))
            nc.vector.quantize_mx(
                out=wg_codes[a][:, 2 * P * u : 2 * P * (u + 1)].bitcast(FP8X4),
                scales=wg_scales[a, u][:],
                in_=wg_bf[a, u][:],
            )

        def up_pass(c, a):
            codes, scales = x_operand(a, c * CHUNK, (c + 1) * CHUNK)
            for t in range(PACK):
                nc.tensor.matmul_mx(
                    out=ub[c][:, t, :],
                    lhsT=wu_slice[a, t].bitcast(FP4X4),
                    lhsT_scale=wu_sc[:, a, P * t : P * (t + 1)],
                    rhs=codes,
                    rhs_scale=scales,
                    start=(a == 0 and t == 0),
                    stop=(a == PASSES - 1 and t == PACK - 1),
                )

        def gate_pass(g, u, a):
            codes, scales = x_operand(a, g * QUARTER, (g + 1) * QUARTER)
            for v in range(2):
                t = 2 * u + v
                nc.tensor.matmul_mx(
                    out=ga[g, u][:, v, :],
                    lhsT=wg_codes[a][:, P * t : P * (t + 1)].bitcast(FP8X4),
                    lhsT_scale=wg_scales[a, u][:, P * v : P * (v + 1)],
                    rhs=codes,
                    rhs_scale=scales,
                    start=(a == 0 and v == 0),
                    stop=(a == PASSES - 1 and v == 1),
                )

        def open_up(c, b):
            ub[c] = bank(b, [P, PACK, CHUNK])
            up_pass(c, 0)

        def open_gate(g, u, b):
            ga[g, u] = bank(b, [P, 2, QUARTER])
            gate_pass(g, u, 0)

        def up(c, b):
            open_up(c, b)
            up_pass(c, 1)

        def gate(g, u, b):
            open_gate(g, u, b)
            gate_pass(g, u, 1)

        def tanh_quarter(g):
            tanh_ga[g] = sbuf([P, PACK, QUARTER], F32, "tanh_ga_%d" % g)
            for u in range(2):
                nc.scalar.activation(out=tanh_ga[g][:, 2 * u : 2 * u + 2, :], in_=ga[g, u][:], func=TANH)

        def hidden(c):
            j0 = c % 2 * CHUNK
            nc.vector.tensor_tensor(
                out=h_bf[:, c * CHUNK : (c + 1) * CHUNK, :].rearrange("p (d e) t -> p d t e", e=4),
                in0=ub[c][:].rearrange("p t (d e) -> p d t e", e=4),
                in1=tanh_ga[c // 2][:, :, j0 : j0 + CHUNK].rearrange("p t (d e) -> p d t e", e=4),
                op=MULT,
            )

        def quantize_h(j0, j1):
            nc.vector.quantize_mx(
                out=h_codes[:, j0:j1].bitcast(FP8X4),
                scales=h_scales[:, j0:j1],
                in_=h_bf[:, j0:j1, :].rearrange("p j t -> p (j t)"),
            )

        def down(b, q0, q1, j0, j1):
            acc = bank(b, [P, q1 - q0, j1 - j0])
            for q in range(q0, q1):
                y_banks[q, j0] = (acc, q0)
                nc.tensor.matmul_mx(
                    out=acc[:, q - q0, :],
                    lhsT=wd_codes[:, P * q : P * (q + 1)].bitcast(FP8X4),
                    lhsT_scale=wd_sc[:, P * q : P * (q + 1)],
                    rhs=h_codes[:, j0:j1].bitcast(FP8X4),
                    rhs_scale=h_scales[:, j0:j1],
                    start=True,
                    stop=True,
                )

        def down_pair(g, u, b):
            down(b, 2 * u, 2 * u + 2, g * QUARTER, (g + 1) * QUARTER)

        def store(engine, q0, q1, j0):
            acc, first = y_banks[q0, j0]
            copy_on(engine, y_sb[j0 // QUARTER][:, q0:q1, :], acc[:, q0 - first : q1 - first, :])
            for q in range(q0, q1):
                nc.sync.dma_start(out=out_rows[:, q, j0 : j0 + QUARTER], in_=y_sb[j0 // QUARTER][:, q, :])

        make_identity(nc, identity[:])
        nc.vector.memset(wu_sc_raw[:].rearrange("p a r -> p (a r)").bitcast(I32), 0)
        nc.vector.memset(wd_sc[:].bitcast(I32), 0)
        nc.sync.dma_start(out=wgt_rows[:], in_=wgt[::8, :].rearrange("q (b j) -> q b j", j=P))
        nc.sync.dma_start(offsets[:], offs)
        nc.sync.dma_start(out=planes[0][0][:, : T // 2], in_=x_rows[0, :, 0, : T // 2])
        for q in range(QUADRANTS):
            nc.sync.dma_start(
                out=wu_sc_raw[32 * q : 32 * q + 4, :, :].bitcast(I32),
                in_=wu_scales[:, 4 * q : 4 * q + 4, :].rearrange("a s r -> s a r").bitcast(I32),
            )
        nc.sync.dma_start(out=planes[0][0][:, T // 2 :], in_=x_rows[0, :, 0, T // 2 :])
        load_plane(0, 1)
        nc.sync.dma_start(out=wu_raw[:].bitcast(I32), in_=wu_words.rearrange("a p b -> p a b").bitcast(I32))
        load_plane(0, 2)
        load_plane(0, 3)
        load_plane(1, 0)
        load_plane(1, 1)
        load_wg(0)
        load_plane(1, 2)
        load_plane(1, 3)
        load_wg(1)
        nc.sync.dma_start(out=wd_codes[:], in_=wd_words[0].rearrange("p n i -> p (n i)").bitcast(I32))
        for q in range(QUADRANTS):
            nc.sync.dma_start(
                out=wd_sc[32 * q : 32 * q + 4, :].bitcast(I32),
                in_=wd_scales[0, 4 * q : 4 * q + 4, :].bitcast(I32),
            )
        spread_wgt()
        reorder_wu_scales()

        for j0, j1 in ((0, QUARTER), (QUARTER, HALF), (HALF, J)):
            gather(0, 0, j0, j1)
        reorder_wu_words()
        gather(0, 1, 0, J)
        gather(0, 2, 0, J)
        new_x_bf(0, 0, J)
        for j0 in range(0, J, HALF):
            gather(0, 3, j0, j0 + HALF)
            interleave_x("scalar", 0, j0, j0 + HALF)
        for i in range(2):
            gather(1, i, 0, J)
        new_x_mx(0, 0, J, "x_scales_0")
        new_x_mx(1, 0, QUARTER, "x_scales_1_0")
        for j0 in range(0, J, HALF):
            quantize_x(0, j0, j0 + HALF)
        new_wg_bf(0, 0, "wg_bf_0")
        interleave_wg("scalar", 0, 0, 0, P)
        quantize_wg(0, 0)
        new_wg_bf(0, 1, "wg_bf_0")
        interleave_wg("scalar", 0, 1, 0, P)
        use_x_bf(1, LATE, J, on_wg_0([P, QUARTER, PACK], BF16, "x_bf_late", 0)[:])
        lay_late_pair("scalar", 0)
        gather(1, 2, 0, LATE)
        reorder_first_words()
        quantize_wg(0, 1)
        for g in range(HALF // QUARTER):
            for u in range(2):
                open_gate(g, u, 2 * g + u)
        for c in range(HALF // CHUNK):
            open_up(c, 4 + c)

        pieces = ((0, CHUNK), (CHUNK, QUARTER), (QUARTER, HALF), (HALF, LATE))
        for j0, j1 in pieces:
            gather(1, 3, j0, j1)
        for j0, j1 in pieces[:3]:
            new_x_bf(1, j0, j1)
            interleave_x("scalar", 1, j0, j1)
        quantize_x(1, 0, CHUNK)
        quantize_x(1, CHUNK, QUARTER)
        for u in range(2):
            new_wg_bf(1, u, "wg_bf_1_%d" % u)
        interleave_wg("vector", 1, 0, 0, P)
        interleave_wg("vector", 1, 1, 0, SPLIT)
        interleave_wg("scalar", 1, 1, SPLIT, P)
        quantize_wg(1, 0)
        quantize_x_quarter(1, "x_scales_1_1")
        quantize_wg(1, 1)
        use_x_bf(1, HALF, LATE, wg_flat[1][:, :R].bitcast(BF16).rearrange("p (j i) -> p j i", i=PACK))
        for j0 in range(HALF, LATE, CHUNK):
            interleave_x("scalar", 1, j0, j0 + CHUNK)
        for g in range(HALF // QUARTER):
            for u in range(2):
                gate_pass(g, u, 1)
            for v in range(2):
                up_pass(2 * g + v, 1)
        gather(1, 2, LATE, J)
        gather(1, 3, LATE, J)
        quantize_x_quarter(2, "x_scales_1_2")
        tanh_quarter(0)
        tanh_quarter(1)
        lay_late_pair("gpsimd", 1)

        for u in range(2):
            gate(2, u, u)
        for v in range(2):
            up(4 + v, 2 + v)
        hidden(0)
        hidden(1)
        hidden(2)
        quantize_h(0, QUARTER)
        hidden(3)
        quantize_x_quarter(3, "tanh_ga_0")
        quantize_h(QUARTER, HALF)
        tanh_quarter(2)
        down_pair(0, 0, 5)
        down_pair(0, 1, 6)
        gate(3, 0, 0)
        down_pair(1, 0, 7)
        gate(3, 1, 1)
        store("scalar", 0, 2, 0)
        store("scalar", 2, 4, 0)
        down_pair(1, 1, 5)
        up(6, 4)
        up(7, 6)
        hidden(4)
        store("vector", 0, 2, QUARTER)
        hidden(5)
        tanh_quarter(3)
        store("scalar", 2, 4, QUARTER)
        quantize_h(HALF, HALF + CHUNK)
        quantize_h(HALF + CHUNK, LATE)
        for u in range(2):
            down_pair(2, u, 2 + u)
        hidden(6)
        hidden(7)
        for q in range(PACK):
            store("scalar", q, q + 1, HALF)
        quantize_h(LATE, LATE + CHUNK)
        quantize_h(LATE + CHUNK, J)
        for q, b in enumerate((7, 0, 1, 5)):
            down(b, q, q + 1, LATE, J)
        for q in range(PACK):
            store(("vector", "scalar")[q % 2], q, q + 1, LATE)
